import numpy as np
import ml_dtypes


def mxq(x, axis, fmt="e4m3"):
    dtype, down = {"e4m3": (ml_dtypes.float8_e4m3fn, 7), "e5m2": (ml_dtypes.float8_e5m2, 14)}[fmt]
    v = np.moveaxis(np.asarray(x, np.float32).astype(ml_dtypes.bfloat16).astype(np.float64), axis, -1)
    blocks = v.reshape(v.shape[:-1] + (-1, 32))
    amax = np.abs(blocks).max(-1, keepdims=True)
    byte = np.maximum(np.where(amax > 0, np.frexp(amax)[1] - 1 + 127, 0) - down, 1)
    scale = np.exp2(byte - 127.0)
    codes = (blocks / scale).astype(np.float32).astype(dtype).astype(np.float64)
    return np.moveaxis((codes * scale).reshape(v.shape), -1, axis)


WIDE = False


def mx_kscale(k):
    if not WIDE:
        return np.ones(k)
    levels = np.array([10, -10, 5, -5, 0])
    if k % 512:
        return np.exp2(np.random.permutation(np.resize(levels, k // 32))).repeat(32)
    a = np.empty((k // 512, 16))
    for p in range(k // 512):
        a[p, :8] = np.random.permutation(np.resize(levels, 8))
        for g in range(8):
            far = levels[np.abs(levels - a[p, g]) >= 10]
            a[p, g + 8] = far[np.random.randint(len(far))]
    return np.exp2(a.ravel()).repeat(32)


def f64(x):
    return np.asarray(x).astype(np.float64)


def striped(idx):
    return np.tile(idx.reshape(-1, 16).T, (8, 1)).astype(np.uint16)


def unstriped(offs):
    return offs[:16].T.reshape(-1).astype(np.int64)


E2M1 = np.array([0.0, 0.5, 1.0, 1.5, 2.0, 3.0, 4.0, 6.0, -0.0, -0.5, -1.0, -1.5, -2.0, -3.0, -4.0, -6.0])


def pack_weight(w, fmt):
    k, n = w.shape
    w = f64(np.asarray(w, np.float32).astype(ml_dtypes.bfloat16)).reshape(k // 32, 32, n)
    amax = np.abs(w).max(1)
    if fmt == "e4m3":
        byte = np.frexp(amax)[1] - 1 + 127 - 7
    else:
        mant, ex = np.frexp(amax / 6.0)
        byte = np.where(mant > 0.5, ex, ex - 1) + 127
    byte = np.clip(np.where(amax > 0, byte, 1), 1, 254)
    scaled = (w * np.exp2(127.0 - byte)[:, None, :]).reshape(k, n).astype(np.float32)
    by_word = np.ascontiguousarray(scaled.reshape(k // 512, 128, 4, n).transpose(0, 1, 3, 2))
    if fmt == "e4m3":
        words = by_word.astype(ml_dtypes.float8_e4m3fn).view(np.uint8)
    else:
        c = by_word.astype(ml_dtypes.float4_e2m1fn).view(np.uint8) & 0xF
        words = (c[..., 0::2] | (c[..., 1::2] << 4)).reshape(k // 512, 128, 2 * n)
    return np.ascontiguousarray(words), np.ascontiguousarray(byte.astype(np.uint8).reshape(k // 512, 16, n))


def unpack_weight(words, scales, fmt):
    g, _, n = scales.shape
    words = np.ascontiguousarray(words).reshape(g, 128, n, -1)
    if fmt == "e4m3":
        vals = words.view(ml_dtypes.float8_e4m3fn).astype(np.float64)
    else:
        nib = np.empty((g, 128, n, 4), np.uint8)
        nib[..., 0::2] = words & 0xF
        nib[..., 1::2] = words >> 4
        vals = E2M1[nib]
    vals = vals * np.repeat(np.exp2(scales.astype(np.float64) - 127.0), 8, axis=1)[..., None]
    return vals.transpose(0, 1, 3, 2).reshape(g * 512, n)


def gelu(v):
    return 0.5 * v * (1.0 + np.tanh(np.sqrt(2.0 / np.pi) * (v + 0.044715 * v**3)))


T, S, T2, P, KH, K, R, H, N = 4096, 1024, 2048, 512, 512, 1024, 1024, 1024, 512

def setup_inputs():
    n = np.random.standard_normal
    s = mx_kscale(K)[:, None]
    u = mx_kscale(R)[:, None]
    uh = mx_kscale(H)[:, None]
    tab_words, tab_scales = pack_weight(n((K, T)) * s, "e4m3")
    wf_words, wf_scales = pack_weight(1.4 * n((KH, R)) / np.sqrt(K) / s[:KH], "e2m1")
    w3_words, w3_scales = pack_weight(n((H, N)) / np.sqrt(H) / uh, "e4m3")
    return {
        "tab_words": tab_words, "tab_scales": tab_scales,
        "offs": striped(np.random.permutation(T)[:S]),
        "wf_words": wf_words, "wf_scales": wf_scales,
        "wb": (1.4 * n((KH, R)) / np.sqrt(K) / s[KH:]).astype(np.float32),
        "gain": (np.exp(0.3 * n(R)) * u[:, 0]).astype(np.float32),
        "w2": (1.2 * n((R, H)) / np.sqrt(R) / u * uh.T).astype(np.float32),
        "page0": (n((H, T2)) * uh).astype(np.float32),
        "wgs": np.exp(0.3 * n((128, S))).astype(np.float32),
        "offs2": striped(np.random.permutation(T2)[:S]),
        "offs3": striped(np.random.permutation(T2)[:P]),
        "bias": (0.6 * n(H) * uh[:, 0]).astype(np.float32),
        "w3_words": w3_words, "w3_scales": w3_scales,
        "shift": (0.8 * n((N, P))).astype(np.float32),
    }

def reference(tab_words, tab_scales, offs, wf_words, wf_scales, wb, gain, w2, page0, wgs, offs2, offs3, bias, w3_words, w3_scales, shift):
    v = unpack_weight(tab_words, tab_scales, "e4m3")[:, unstriped(offs)]
    wf = unpack_weight(wf_words, wf_scales, "e2m1")
    wbq = mxq(f64(wb), 0, "e4m3")
    y1 = wf.T @ v[:KH] + wbq.T @ v[KH:]
    e = y1 / (1.0 + np.exp(-y1)) * f64(gain)[:, None]
    h = mxq(f64(w2), 0, "e4m3").T @ mxq(e, 0, "e4m3")
    page = f64(page0).copy()
    page[:, unstriped(offs2)] = np.tile(f64(wgs), (H // 128, 1)) * h
    x = page[:, unstriped(offs3)]
    z = x + f64(bias)[:, None]
    w3 = unpack_weight(w3_words, w3_scales, "e4m3")
    return (w3.T @ mxq(z, 0, "e4m3")) + f64(shift)

@@ -1,0 +1,324 @@
+from contextlib import ExitStack
+
+import concourse.mybir as mybir
+
+F32 = mybir.dt.float32
+BF16 = mybir.dt.bfloat16
+I32 = mybir.dt.int32
+U32 = mybir.dt.uint32
+U16 = mybir.dt.uint16
+U8 = mybir.dt.uint8
+FP8X4 = mybir.dt.float8_e4m3fn_x4
+FP4X4 = mybir.dt.float4_e2m1fn_x4
+MULT = mybir.AluOpType.mult
+ADD = mybir.AluOpType.add
+ACT = mybir.ActivationFunctionType
+
+P = 128
+T, S, T2, M = 4096, 1024, 2048, 512
+HALF = 512
+FLOPS = 4831838208
+
+
+def tile_list_query_slot_cache_kernel(
+    tc, tab_words, tab_scales, offs, wf_words, wf_scales, wb, gain, w2, page0, wgs,
+    offs2, offs3, bias, w3_words, w3_scales, shift, out,
+):
+    nc = tc.nc
+    with ExitStack() as ctx:
+        lists = ctx.enter_context(tc.tile_pool(name="lists", bufs=1))
+        first = ctx.enter_context(tc.tile_pool(name="first", bufs=1))
+        psum = ctx.enter_context(tc.psum_pool(name="psum", bufs=1))
+
+        def bank(name, shape, number):
+            return psum.tile(shape, F32, name=name, tag="bank%d" % number)
+
+        idx = lists.tile([P, S // 16], U16, name="idx")
+        idx2 = lists.tile([P, S // 16], U16, name="idx2")
+        idx3 = lists.tile([P, M // 16], U16, name="idx3")
+
+        nc.sync.dma_start(idx[:], offs)
+        nc.sync.dma_start(idx2[:], offs2)
+        nc.sync.dma_start(idx3[:], offs3)
+        tab = [first.tile([P, T], I32, name="tab0", tag="tab0", bufs=1, align_bytes=64)]
+        nc.sync.dma_start(tab[0][:], tab_words[0].rearrange("p t i -> p (t i)").bitcast(I32))
+        tab_sc = first.tile([P, T], U8, name="tab_sc", align_bytes=64)
+        wf_sc_raw = first.tile([P, 1024], U8, name="wf_sc_raw", align_bytes=64)
+        w3_sc = first.tile([P, 512], U8, name="w3_sc", align_bytes=64)
+        for plane in (tab_sc, wf_sc_raw, w3_sc):
+            nc.vector.memset(plane[:].bitcast(I32), 0)
+        for q in range(4):
+            nc.sync.dma_start(tab_sc[32 * q : 32 * q + 8, :].bitcast(I32), tab_scales[:, 4 * q : 4 * q + 4, :].bitcast(I32))
+        for q in range(4):
+            queue = nc.gpsimd if q == 3 else nc.sync
+            queue.dma_start(wf_sc_raw[32 * q : 32 * q + 4, :].bitcast(I32), wf_scales[0, 4 * q : 4 * q + 4, :].bitcast(I32))
+        for q in range(4):
+            nc.gpsimd.dma_start(w3_sc[32 * q : 32 * q + 8, :].bitcast(I32), w3_scales[:, 4 * q : 4 * q + 4, :].bitcast(I32))
+        with tc.tile_pool(name="warmup", bufs=1) as warmup:
+            warm = warmup.tile([P, 48 * 1024], F32, name="warm")
+            nc.vector.memset(warm[:, 0:1], 0.0)
+            nc.scalar.activation(warm[:, 8:9], warm[:, 0:1], ACT.Silu)
+        sb = ctx.enter_context(tc.tile_pool(name="sb", bufs=1))
+
+        def sbuf(name, shape, dtype, tag=None, bufs=1):
+            pool = first if tag == "tab0" else sb
+            return pool.tile(shape, dtype, name=name, tag=tag or name, bufs=bufs, align_bytes=64)
+
+        def load_tab(a):
+            tile = sbuf("tab%d" % a, [P, T], I32)
+            nc.sync.dma_start(tile[:], tab_words[a].rearrange("p t i -> p (t i)").bitcast(I32))
+            return tile
+
+        def load_weight(name, rows, tag):
+            tile = sbuf(name, [P, 4, HALF], F32, tag)
+            nc.sync.dma_start(tile[:], rows.rearrange("(p i) c -> p i c", i=4))
+            return tile
+
+        page_rows = page0.rearrange("(a p t) c -> a t p c", a=2, t=4)
+        wgs_rows = wgs.rearrange("(q t) j -> q t j", t=4)
+        pages = {}
+
+        def load_page(k, tag=None):
+            pages[k] = sbuf("page%d" % k, [P, T2], F32, tag)
+            nc.sync.dma_start(pages[k][:], page_rows[k // 4, k % 4])
+
+        wgs0 = {}
+
+        def load_wgs0(t):
+            wgs0[t] = sbuf("wgs0_%d" % t, [P, HALF], F32)
+            for q in (0, 2, 1, 3):
+                nc.sync.dma_start(wgs0[t][32 * q : 32 * q + 32, :], wgs_rows[:, t, 0:HALF])
+
+        wf_raw = sbuf("wf_raw", [P, 2048], U8)
+        nc.sync.dma_start(wf_raw[:].bitcast(I32), wf_words[0].bitcast(I32))
+        tab.append(load_tab(1))
+        gain_sb = sbuf("gain_sb", [P, 2, 4], F32)
+        nc.sync.dma_start(gain_sb[:], gain.rearrange("(b p t) -> p b t", b=2, t=4))
+        wb_raw = [load_weight("wb_raw%d" % b, wb[:, HALF * b : HALF * (b + 1)], "raw%d" % b) for b in range(2)]
+        w2_raw = {}
+        for b in range(2):
+            w2_raw[0, b] = load_weight("w2_raw0%d" % b, w2[HALF * b : HALF * (b + 1), 0:HALF], "raw%d" % (2 + b))
+        for k in range(3):
+            load_wgs0(k)
+            load_page(k)
+        load_wgs0(3)
+        bias_sb = sbuf("bias_sb", [P, 2, 4], F32)
+        nc.sync.dma_start(bias_sb[:], bias.rearrange("(a p t) -> p a t", a=2, t=4))
+
+        wf_w = sbuf("wf_w", [P, 2048], U8)
+        nc.vector.tensor_copy(
+            wf_w[:].rearrange("p (b t m e) -> p b t m e", b=2, t=4, e=2),
+            wf_raw[:].rearrange("p (b m t e) -> p b t m e", b=2, t=4, e=2),
+        )
+
+        v_w, v_sc = {}, {}
+
+        def gather_words(a, jh):
+            v_w[a, jh] = sbuf("v_w%d%d" % (a, jh), [P, HALF], U32)
+            nc.vector.tensor_copy(v_w[a, jh][:], tab[a][:].bitcast(U32).indirect(idx[:, 32 * jh : 32 * jh + 32]))
+
+        def gather_scales(jh):
+            v_sc[jh] = sbuf("v_sc%d" % jh, [P, HALF], U8)
+            nc.vector.tensor_copy(v_sc[jh][:], tab_sc[:].indirect(idx[:, 32 * jh : 32 * jh + 32]))
+
+        gather_words(0, 0)
+        gather_scales(0)
+        wf_sc = sbuf("wf_sc", [P, 1024], U8)
+        nc.vector.tensor_copy(
+            wf_sc[:].rearrange("p (b t m) -> p b t m", b=2, t=4),
+            wf_sc_raw[:].rearrange("p (b m t) -> p b t m", b=2, t=4),
+        )
+        gather_words(1, 0)
+        gather_words(0, 1)
+        gather_scales(1)
+        gather_words(1, 1)
+
+        def quantise_weight(name, raw, tp, copy):
+            grouped = sbuf("grouped", [P, 2, P, 4], BF16, bufs=4)
+            copy(
+                grouped[:].rearrange("p t m i -> p m i t"),
+                raw[:].rearrange("p i (m t) -> p m i t", t=4)[:, :, :, 2 * tp : 2 * tp + 2],
+            )
+            codes = sbuf(name + "_w", [P, 256], U32)
+            scales = sbuf(name + "_sc", [P, 256], U8)
+            nc.vector.quantize_mx(codes[:].bitcast(FP8X4), scales[:], grouped[:].rearrange("p t m i -> p (t m i)"))
+            return codes, scales
+
+        def stationary(pairs, t):
+            codes, scales = pairs[t // 2]
+            cols = slice(P * (t % 2), P * (t % 2 + 1))
+            return codes[:, cols].bitcast(FP8X4), scales[:, cols]
+
+        def wf_pass(acc, b, t, jh, cols, start):
+            c = 4 * b + t
+            nc.tensor.matmul_mx(
+                acc, lhsT=wf_w[:, 256 * c : 256 * (c + 1)].bitcast(FP4X4), lhsT_scale=wf_sc[:, P * c : P * (c + 1)],
+                rhs=v_w[0, jh][:, cols].bitcast(FP8X4), rhs_scale=v_sc[jh][:, cols], start=start, stop=False,
+            )
+
+        wb_q = {}
+
+        def wb_pass(acc, b, t, jh, cols, stop):
+            codes, scales = stationary(wb_q[b], t)
+            nc.tensor.matmul_mx(
+                acc, lhsT=codes, lhsT_scale=scales,
+                rhs=v_w[1, jh][:, cols].bitcast(FP8X4), rhs_scale=v_sc[jh][4:P, cols], start=False, stop=stop,
+            )
+
+        e_w = {(b, jh): sbuf("e_w%d%d" % (b, jh), [P, HALF], U32) for b in range(2) for jh in range(2)}
+        e_sc = {(b, jh): sbuf("e_sc%d%d" % (b, jh), [P, HALF], U8) for b in range(2) for jh in range(2)}
+
+        y_first = {}
+        for b in range(2):
+            for jq in range(4):
+                y_first[b, jq] = bank("y%d%d" % (b, jq), [P, 4, P], 4 * b + jq)
+                for t in range(4):
+                    wf_pass(y_first[b, jq][:, t, :], b, t, 0, slice(P * jq, P * (jq + 1)), t == 0)
+
+        wb_q[0] = [quantise_weight("wb00", wb_raw[0], 0, nc.vector.tensor_copy), quantise_weight("wb01", wb_raw[0], 1, nc.scalar.copy)]
+        wb_q[1] = [quantise_weight("wb1%d" % tp, wb_raw[1], tp, nc.vector.tensor_copy) for tp in range(2)]
+
+        def e_first(b, jp):
+            e_bf = sbuf("e_bf", [P, 256, 4], BF16, bufs=3)
+            for u in range(2):
+                jq = 2 * jp + u
+                for t in range(4):
+                    wb_pass(y_first[b, jq][:, t, :], b, t, 0, slice(P * jq, P * (jq + 1)), t == 3)
+                act = sbuf("act", [P, P, 4], F32, tag="act", bufs=3)
+                nc.scalar.activation(act[:], y_first[b, jq][:].rearrange("p t j -> p j t"), ACT.Silu)
+                nc.vector.tensor_tensor(
+                    e_bf[:, P * u : P * (u + 1), :], act[:], gain_sb[:, b : b + 1, :].to_broadcast([P, P, 4]), MULT
+                )
+            cols = slice(256 * jp, 256 * (jp + 1))
+            nc.vector.quantize_mx(e_w[b, 0][:, cols].bitcast(FP8X4), e_sc[b, 0][:, cols], e_bf[:].rearrange("p j t -> p (j t)"))
+
+        w2_q = {(a, b): {} for a in range(2) for b in range(2)}
+
+        def quantise_w2(a, b, tp):
+            w2_q[a, b][tp] = quantise_weight("w2%d%d%d" % (a, b, tp), w2_raw[a, b], tp, nc.scalar.copy)
+
+        e_first(0, 0)
+        e_first(0, 1)
+        e_first(1, 0)
+        quantise_w2(0, 0, 0)
+        e_first(1, 1)
+        quantise_w2(0, 1, 0)
+
+        def encode(k, jh):
+            a, t = divmod(k, 4)
+            acc = bank("h_acc%d%d" % (k, jh), [P, HALF], 4 + k % 4)
+            for b in range(2):
+                codes, scales = stationary(w2_q[a, b], t)
+                nc.tensor.matmul_mx(
+                    acc[:], lhsT=codes, lhsT_scale=scales, rhs=e_w[b, jh][:].bitcast(FP8X4), rhs_scale=e_sc[b, jh][:],
+                    start=(b == 0), stop=(b == 1),
+                )
+            h = sbuf("h%d%d" % (k, jh), [P, HALF], F32, "h%d" % k)
+            nc.scalar.copy(h[:], acc[:])
+            return h
+
+        def write_slots(k, jh, weight, h=None):
+            h = h if h is not None else encode(k, jh)
+            nc.vector.tensor_tensor(pages[k][:].indirect(idx2[:, 32 * jh : 32 * jh + 32]), h[:], weight, MULT)
+
+        w2_raw[1, 0] = load_weight("w2_raw10", w2[0:HALF, HALF:], "tab0")
+        load_page(3, "tab1")
+        w2_raw[1, 1] = load_weight("w2_raw11", w2[HALF:, HALF:], "raw0")
+        load_page(4, "raw1")
+
+        write_slots(0, 0, wgs0[0][:])
+        write_slots(1, 0, wgs0[1][:])
+        quantise_w2(0, 0, 1)
+        quantise_w2(0, 1, 1)
+        load_page(5, "raw2")
+        load_page(6, "raw3")
+        write_slots(2, 0, wgs0[2][:])
+        quantise_w2(1, 0, 0)
+        write_slots(3, 0, wgs0[3][:])
+        quantise_w2(1, 1, 0)
+        write_slots(4, 0, wgs0[0][:])
+        write_slots(5, 0, wgs0[1][:])
+        quantise_w2(1, 0, 1)
+        quantise_w2(1, 1, 1)
+        load_page(7, "tab0")
+        wgs1 = sbuf("wgs1", [P, 4, HALF], F32, "raw0")
+        for q in (0, 2, 1, 3):
+            nc.sync.dma_start(wgs1[32 * q : 32 * q + 32, :, :], wgs_rows[:, :, HALF:])
+        write_slots(6, 0, wgs0[2][:])
+        write_slots(7, 0, wgs0[3][:])
+
+        for b in range(2):
+            planes = sbuf("planes%d" % b, [P, 4, HALF], BF16)
+            for t in range(4):
+                acc = bank("y_second%d%d" % (b, t), [P, HALF], t)
+                wf_pass(acc[:], b, t, 1, slice(0, HALF), True)
+                wb_pass(acc[:], b, t, 1, slice(0, HALF), True)
+                act = sbuf("act", [P, HALF], F32, tag="act", bufs=3)
+                nc.scalar.activation(act[:], acc[:], ACT.Silu)
+                nc.scalar.activation(planes[:, t, :], act[:], ACT.Copy, scale=gain_sb[:, b, t : t + 1])
+            woven = sbuf("woven%d" % b, [P, HALF, 4], BF16)
+            nc.scalar.copy(
+                woven[:].rearrange("p (c i) t -> p c t i", i=4), planes[:].rearrange("p t (c i) -> p c t i", i=4)
+            )
+            nc.vector.quantize_mx(e_w[b, 1][:].bitcast(FP8X4), e_sc[b, 1][:], woven[:].rearrange("p j t -> p (j t)"))
+
+        w3_w = []
+        for a in range(2):
+            w3_w.append(sbuf("w3_w%d" % a, [P, 512], I32, "v_w%d1" % a))
+            nc.sync.dma_start(w3_w[a][:], w3_words[a].rearrange("p c i -> p (c i)").bitcast(I32))
+        shift_sb = sbuf("shift_sb", [P, 4, M], F32, "planes0")
+        nc.sync.dma_start(shift_sb[:], shift.rearrange("(n p) m -> p n m", p=P))
+
+        h_second = [encode(k, 1) for k in range(8)]
+
+        z_bf = {}
+        for mh in range(2):
+            z_bf[0, mh] = sbuf("z_bf0%d" % mh, [P, 256, 4], BF16, "e_w%d1" % mh)
+            z_bf[1, mh] = sbuf("z_bf1%d" % mh, [P, 256, 4], BF16)
+
+        def add_bias(k, mh, x):
+            a, t = divmod(k, 4)
+            nc.scalar.activation(z_bf[a, mh][:, :, t], x, ACT.Identity, bias=bias_sb[:, a, t : t + 1])
+
+        def read_slots(k):
+            x = sbuf("x%d" % k, [P, M], F32, "h%d" % ((k + 1) % 7))
+            nc.vector.tensor_copy(x[:], pages[k][:].indirect(idx3[:]))
+            for mh in range(2):
+                add_bias(k, mh, x[:, 256 * mh : 256 * (mh + 1)])
+
+        accs = {}
+
+        def project(a, mh):
+            codes = sbuf("z_w%d%d" % (a, mh), [P, 256], U32)
+            scales = sbuf("z_sc%d%d" % (a, mh), [P, 256], U8)
+            nc.vector.quantize_mx(codes[:].bitcast(FP8X4), scales[:], z_bf[a, mh][:].rearrange("p m t -> p (m t)"))
+            for n in range(4):
+                if a == 0:
+                    accs[n, mh] = bank("o_acc%d%d" % (n, mh), [P, 256], 4 * mh + n)
+                cols = slice(P * n, P * (n + 1))
+                nc.tensor.matmul_mx(
+                    accs[n, mh][:], lhsT=w3_w[a][:, cols].bitcast(FP8X4), lhsT_scale=w3_sc[4 * a : P, cols],
+                    rhs=codes[:].bitcast(FP8X4), rhs_scale=scales[:], start=(a == 0), stop=(a == 1),
+                )
+
+        write_slots(0, 1, wgs1[:, 0, :], h_second[0])
+        for k in range(1, 7):
+            write_slots(k, 1, wgs1[:, k % 4, :], h_second[k])
+            read_slots(k - 1)
+            if k == 5:
+                project(0, 0)
+                project(0, 1)
+        read_slots(6)
+        write_slots(7, 1, wgs1[:, 3, :], h_second[7])
+        for mh in range(2):
+            x = sbuf("x7%d" % mh, [P, 256], F32, "h%d" % (1 + mh))
+            nc.vector.tensor_copy(x[:], pages[7][:].indirect(idx3[:, 16 * mh : 16 * mh + 16]))
+            add_bias(7, mh, x[:])
+        for mh in range(2):
+            project(1, mh)
+        for mh in range(2):
+            cols = slice(256 * mh, 256 * (mh + 1))
+            for n in range(4):
+                res = sbuf("res%d%d" % (n, mh), [P, 256], F32)
+                nc.vector.tensor_tensor(res[:], accs[n, mh][:], shift_sb[:, n, cols], ADD)
+                nc.sync.dma_start(out[P * n : P * (n + 1), cols], res[:])

@@ -17,6 +17,8 @@ ACT = mybir.ActivationFunctionType
 P = 128
 T, S, T2, M = 4096, 1024, 2048, 512
 HALF = 512
+QUARTER = 256
+KIB = 1024
 FLOPS = 4831838208
 
 
@@ -27,50 +29,44 @@ def tile_list_query_slot_cache_kernel(
     nc = tc.nc
     with ExitStack() as ctx:
         lists = ctx.enter_context(tc.tile_pool(name="lists", bufs=1))
-        first = ctx.enter_context(tc.tile_pool(name="first", bufs=1))
+        sb = ctx.enter_context(tc.tile_pool(name="sb", bufs=1))
         psum = ctx.enter_context(tc.psum_pool(name="psum", bufs=1))
+        banks = [psum.tile([P, HALF], F32, name="bank%d" % n) for n in range(8)]
 
-        def bank(name, shape, number):
-            return psum.tile(shape, F32, name=name, tag="bank%d" % number)
+        free = [0]
+
+        def room(nbytes):
+            start = free[0]
+            free[0] = start + (nbytes + 63) // 64 * 64
+            return start
+
+        def sbuf(name, shape, dtype, at=None):
+            nbytes = 1 if dtype == U8 else 2 if dtype in (BF16, U16) else 4
+            for n in shape[1:]:
+                nbytes = nbytes * n
+            return sb.tile(shape, dtype, name=name, align_bytes=64, offset=room(nbytes) if at is None else at)
 
         idx = lists.tile([P, S // 16], U16, name="idx")
         idx2 = lists.tile([P, S // 16], U16, name="idx2")
         idx3 = lists.tile([P, M // 16], U16, name="idx3")
 
-        nc.sync.dma_start(idx[:], offs)
-        nc.sync.dma_start(idx2[:], offs2)
-        nc.sync.dma_start(idx3[:], offs3)
-        tab = [first.tile([P, T], I32, name="tab0", tag="tab0", bufs=1, align_bytes=64)]
-        nc.sync.dma_start(tab[0][:], tab_words[0].rearrange("p t i -> p (t i)").bitcast(I32))
-        tab_sc = first.tile([P, T], U8, name="tab_sc", align_bytes=64)
-        wf_sc_raw = first.tile([P, 1024], U8, name="wf_sc_raw", align_bytes=64)
-        w3_sc = first.tile([P, 512], U8, name="w3_sc", align_bytes=64)
-        for plane in (tab_sc, wf_sc_raw, w3_sc):
-            nc.vector.memset(plane[:].bitcast(I32), 0)
-        for q in range(4):
-            nc.sync.dma_start(tab_sc[32 * q : 32 * q + 8, :].bitcast(I32), tab_scales[:, 4 * q : 4 * q + 4, :].bitcast(I32))
-        for q in range(4):
-            queue = nc.gpsimd if q == 3 else nc.sync
-            queue.dma_start(wf_sc_raw[32 * q : 32 * q + 4, :].bitcast(I32), wf_scales[0, 4 * q : 4 * q + 4, :].bitcast(I32))
-        for q in range(4):
-            nc.gpsimd.dma_start(w3_sc[32 * q : 32 * q + 8, :].bitcast(I32), w3_scales[:, 4 * q : 4 * q + 4, :].bitcast(I32))
-        with tc.tile_pool(name="warmup", bufs=1) as warmup:
-            warm = warmup.tile([P, 48 * 1024], F32, name="warm")
-            nc.vector.memset(warm[:, 0:1], 0.0)
-            nc.scalar.activation(warm[:, 8:9], warm[:, 0:1], ACT.Silu)
-        sb = ctx.enter_context(tc.tile_pool(name="sb", bufs=1))
+        at_tab0 = room(16 * KIB)
+        tab_sc = sbuf("tab_sc", [P, T], U8)
+        wf_sc_raw = sbuf("wf_sc_raw", [P, 1024], U8)
+        wf_w = sbuf("wf_w", [P, 1024], U16)
+        wf_sc = sbuf("wf_sc", [P, 1024], U8)
+        wf_raw = sbuf("wf_raw", [P, 56 * KIB], U16, at=free[0])
+        at_tab1 = room(16 * KIB)
+        at_wb = [room(8 * KIB) for b in range(2)]
+        at_w2 = [room(8 * KIB) for b in range(4)]
 
-        def sbuf(name, shape, dtype, tag=None, bufs=1):
-            pool = first if tag == "tab0" else sb
-            return pool.tile(shape, dtype, name=name, tag=tag or name, bufs=bufs, align_bytes=64)
-
-        def load_tab(a):
-            tile = sbuf("tab%d" % a, [P, T], I32)
+        def load_tab(a, at):
+            tile = sbuf("tab%d" % a, [P, T], I32, at)
             nc.sync.dma_start(tile[:], tab_words[a].rearrange("p t i -> p (t i)").bitcast(I32))
             return tile
 
-        def load_weight(name, rows, tag):
-            tile = sbuf(name, [P, 4, HALF], F32, tag)
+        def load_weight(name, rows, at):
+            tile = sbuf(name, [P, 4, HALF], F32, at)
             nc.sync.dma_start(tile[:], rows.rearrange("(p i) c -> p i c", i=4))
             return tile
 
@@ -78,70 +74,80 @@ def tile_list_query_slot_cache_kernel(
         wgs_rows = wgs.rearrange("(q t) j -> q t j", t=4)
         pages = {}
 
-        def load_page(k, tag=None):
-            pages[k] = sbuf("page%d" % k, [P, T2], F32, tag)
+        def load_page(k, at=None):
+            pages[k] = sbuf("page%d" % k, [P, T2], F32, at)
             nc.sync.dma_start(pages[k][:], page_rows[k // 4, k % 4])
 
-        wgs0 = {}
-
-        def load_wgs0(t):
-            wgs0[t] = sbuf("wgs0_%d" % t, [P, HALF], F32)
+        def load_wgs(name, ts, cols, at=None):
+            tile = sbuf(name, [P, ts.stop - ts.start, HALF], F32, at)
             for q in (0, 2, 1, 3):
-                nc.sync.dma_start(wgs0[t][32 * q : 32 * q + 32, :], wgs_rows[:, t, 0:HALF])
+                nc.sync.dma_start(tile[32 * q : 32 * q + 32, :, :], wgs_rows[:, ts, cols])
+            return tile
 
-        wf_raw = sbuf("wf_raw", [P, 2048], U8)
-        nc.sync.dma_start(wf_raw[:].bitcast(I32), wf_words[0].bitcast(I32))
-        tab.append(load_tab(1))
+        nc.sync.dma_start(idx[:], offs)
+        nc.sync.dma_start(wf_raw[:, 0:1024].bitcast(I32), wf_words[0].bitcast(I32))
+        nc.gpsimd.memset(wf_sc_raw[:].bitcast(I32), 0)
+        for q in range(4):
+            nc.sync.dma_start(wf_sc_raw[32 * q : 32 * q + 4, :].bitcast(I32), wf_scales[0, 4 * q : 4 * q + 4, :].bitcast(I32))
+        tab = [load_tab(0, at_tab0)]
+        nc.sync.dma_start(idx2[:], offs2)
+        nc.sync.dma_start(idx3[:], offs3)
+        nc.vector.memset(tab_sc[:].bitcast(I32), 0)
+        for q in range(4):
+            nc.sync.dma_start(tab_sc[32 * q : 32 * q + 8, :].bitcast(I32), tab_scales[:, 4 * q : 4 * q + 4, :].bitcast(I32))
+        nc.vector.tensor_copy(
+            wf_w[:].rearrange("p (b t m) -> p b t m", b=2, t=4),
+            wf_raw[:, 0:1024].rearrange("p (b m t) -> p b t m", b=2, t=4),
+        )
+        tab.append(load_tab(1, at_tab1))
+        wb_raw = [load_weight("wb_raw0", wb[:, 0:HALF], at_wb[0])]
         gain_sb = sbuf("gain_sb", [P, 2, 4], F32)
         nc.sync.dma_start(gain_sb[:], gain.rearrange("(b p t) -> p b t", b=2, t=4))
-        wb_raw = [load_weight("wb_raw%d" % b, wb[:, HALF * b : HALF * (b + 1)], "raw%d" % b) for b in range(2)]
+        wb_raw.append(load_weight("wb_raw1", wb[:, HALF:], at_wb[1]))
         w2_raw = {}
         for b in range(2):
-            w2_raw[0, b] = load_weight("w2_raw0%d" % b, w2[HALF * b : HALF * (b + 1), 0:HALF], "raw%d" % (2 + b))
-        for k in range(3):
-            load_wgs0(k)
+            w2_raw[0, b] = load_weight("w2_raw0%d" % b, w2[HALF * b : HALF * (b + 1), 0:HALF], at_w2[b])
+        wgs_00 = load_wgs("wgs_00", slice(0, 1), slice(0, HALF))
+        load_page(0)
+        wgs_0r = load_wgs("wgs_0r", slice(1, 4), slice(0, HALF))
+        wgs0 = [wgs_00[:, 0, :]] + [wgs_0r[:, t, :] for t in range(3)]
+        for k in range(1, 3):
             load_page(k)
-        load_wgs0(3)
+        for b in range(2):
+            w2_raw[1, b] = load_weight("w2_raw1%d" % b, w2[HALF * b : HALF * (b + 1), HALF:], at_w2[2 + b])
+        load_page(3)
         bias_sb = sbuf("bias_sb", [P, 2, 4], F32)
         nc.sync.dma_start(bias_sb[:], bias.rearrange("(a p t) -> p a t", a=2, t=4))
 
-        wf_w = sbuf("wf_w", [P, 2048], U8)
-        nc.vector.tensor_copy(
-            wf_w[:].rearrange("p (b t m e) -> p b t m e", b=2, t=4, e=2),
-            wf_raw[:].rearrange("p (b m t e) -> p b t m e", b=2, t=4, e=2),
-        )
-
-        v_w, v_sc = {}, {}
-
-        def gather_words(a, jh):
-            v_w[a, jh] = sbuf("v_w%d%d" % (a, jh), [P, HALF], U32)
-            nc.vector.tensor_copy(v_w[a, jh][:], tab[a][:].bitcast(U32).indirect(idx[:, 32 * jh : 32 * jh + 32]))
-
-        def gather_scales(jh):
-            v_sc[jh] = sbuf("v_sc%d" % jh, [P, HALF], U8)
-            nc.vector.tensor_copy(v_sc[jh][:], tab_sc[:].indirect(idx[:, 32 * jh : 32 * jh + 32]))
-
-        gather_words(0, 0)
-        gather_scales(0)
-        wf_sc = sbuf("wf_sc", [P, 1024], U8)
+        v0 = sbuf("v0", [P, S], U32)
+        nc.vector.tensor_copy(v0[:], tab[0][:].bitcast(U32).indirect(idx[:]))
+        v_sc = sbuf("v_sc", [P, S], U8)
+        nc.vector.tensor_copy(v_sc[:], tab_sc[:].indirect(idx[:]))
         nc.vector.tensor_copy(
             wf_sc[:].rearrange("p (b t m) -> p b t m", b=2, t=4),
             wf_sc_raw[:].rearrange("p (b m t) -> p b t m", b=2, t=4),
         )
-        gather_words(1, 0)
-        gather_words(0, 1)
-        gather_scales(1)
-        gather_words(1, 1)
+        v1 = {}
 
-        def quantise_weight(name, raw, tp, copy):
-            grouped = sbuf("grouped", [P, 2, P, 4], BF16, bufs=4)
-            copy(
-                grouped[:].rearrange("p t m i -> p m i t"),
+        def gather_second_pass(jh, at):
+            v1[jh] = sbuf("v1%d" % jh, [P, HALF], U32, at)
+            nc.vector.tensor_copy(v1[jh][:], tab[1][:].bitcast(U32).indirect(idx[:, 32 * jh : 32 * jh + 32]))
+
+        at_last_act = room(2 * KIB)
+        acts = {(b, jq): sbuf("act%d%d" % (b, jq), [P, HALF], F32, at_last_act if (b, jq) == (1, 3) else None) for b in range(2) for jq in range(4)}
+        wb_grouped = sbuf("wb_grouped", [P, 4, P, 4], BF16)
+
+        def cast_weight(raw, tp, staging):
+            tile = staging[:].bitcast(BF16).rearrange("p (t m i) -> p t m i", t=2, i=4)
+            nc.scalar.copy(
+                tile.rearrange("p t m i -> p m i t"),
                 raw[:].rearrange("p i (m t) -> p m i t", t=4)[:, :, :, 2 * tp : 2 * tp + 2],
             )
-            codes = sbuf(name + "_w", [P, 256], U32)
+            return tile
+
+        def quantise_weight(name, tile, codes):
             scales = sbuf(name + "_sc", [P, 256], U8)
-            nc.vector.quantize_mx(codes[:].bitcast(FP8X4), scales[:], grouped[:].rearrange("p t m i -> p (t m i)"))
+            nc.vector.quantize_mx(codes.bitcast(FP8X4), scales[:], tile.rearrange("p t m i -> p (t m i)"))
             return codes, scales
 
         def stationary(pairs, t):
@@ -149,176 +155,203 @@ def tile_list_query_slot_cache_kernel(
             cols = slice(P * (t % 2), P * (t % 2 + 1))
             return codes[:, cols].bitcast(FP8X4), scales[:, cols]
 
-        def wf_pass(acc, b, t, jh, cols, start):
+        def wf_pass(acc, b, t, j0, n, start):
             c = 4 * b + t
             nc.tensor.matmul_mx(
-                acc, lhsT=wf_w[:, 256 * c : 256 * (c + 1)].bitcast(FP4X4), lhsT_scale=wf_sc[:, P * c : P * (c + 1)],
-                rhs=v_w[0, jh][:, cols].bitcast(FP8X4), rhs_scale=v_sc[jh][:, cols], start=start, stop=False,
+                acc, lhsT=wf_w[:, P * c : P * (c + 1)].bitcast(FP4X4), lhsT_scale=wf_sc[:, P * c : P * (c + 1)],
+                rhs=v0[:, j0 : j0 + n].bitcast(FP8X4), rhs_scale=v_sc[:, j0 : j0 + n], start=start, stop=False,
             )
 
         wb_q = {}
 
-        def wb_pass(acc, b, t, jh, cols, stop):
+        def wb_pass(acc, b, t, j0, n, stop):
             codes, scales = stationary(wb_q[b], t)
             nc.tensor.matmul_mx(
                 acc, lhsT=codes, lhsT_scale=scales,
-                rhs=v_w[1, jh][:, cols].bitcast(FP8X4), rhs_scale=v_sc[jh][4:P, cols], start=False, stop=stop,
+                rhs=v1[j0 // HALF][:, j0 % HALF : j0 % HALF + n].bitcast(FP8X4), rhs_scale=v_sc[4:P, j0 : j0 + n], start=False, stop=stop,
             )
 
-        e_w = {(b, jh): sbuf("e_w%d%d" % (b, jh), [P, HALF], U32) for b in range(2) for jh in range(2)}
+        at_planes = [room(4 * KIB) for b in range(2)]
+        at_h = [room(2 * KIB) for k in range(7)] + [at_planes[1]]
+        h_first = {}
+        e_w = {(b, 0): sbuf("e_w%d" % b, [P, HALF], U32)[:] for b in range(2)}
         e_sc = {(b, jh): sbuf("e_sc%d%d" % (b, jh), [P, HALF], U8) for b in range(2) for jh in range(2)}
 
-        y_first = {}
+        def y_first(b, jq):
+            return banks[4 * b + jq][:].rearrange("p (t j) -> p t j", t=4)
+
         for b in range(2):
             for jq in range(4):
-                y_first[b, jq] = bank("y%d%d" % (b, jq), [P, 4, P], 4 * b + jq)
                 for t in range(4):
-                    wf_pass(y_first[b, jq][:, t, :], b, t, 0, slice(P * jq, P * (jq + 1)), t == 0)
+                    wf_pass(y_first(b, jq)[:, t, :], b, t, P * jq, P, t == 0)
 
-        wb_q[0] = [quantise_weight("wb00", wb_raw[0], 0, nc.vector.tensor_copy), quantise_weight("wb01", wb_raw[0], 1, nc.scalar.copy)]
-        wb_q[1] = [quantise_weight("wb1%d" % tp, wb_raw[1], tp, nc.vector.tensor_copy) for tp in range(2)]
+        gather_second_pass(0, None)
+        for b in range(2):
+            nc.vector.tensor_copy(
+                wb_grouped[:].rearrange("p t m i -> p m i t"), wb_raw[b][:].rearrange("p i (m t) -> p m i t", t=4)
+            )
+            codes = sbuf("wb%d_w" % b, [P, HALF], U32)
+            scales = sbuf("wb%d_sc" % b, [P, HALF], U8)
+            nc.vector.quantize_mx(codes[:].bitcast(FP8X4), scales[:], wb_grouped[:].rearrange("p t m i -> p (t m i)"))
+            wb_q[b] = [(codes[:, 256 * tp : 256 * (tp + 1)], scales[:, 256 * tp : 256 * (tp + 1)]) for tp in range(2)]
 
-        def e_first(b, jp):
-            e_bf = sbuf("e_bf", [P, 256, 4], BF16, bufs=3)
-            for u in range(2):
-                jq = 2 * jp + u
+        e_bf = [sbuf("e_bf%d" % b, [P, HALF, 4], BF16) for b in range(2)]
+
+        def e_first(b):
+            for jq in range(4):
                 for t in range(4):
-                    wb_pass(y_first[b, jq][:, t, :], b, t, 0, slice(P * jq, P * (jq + 1)), t == 3)
-                act = sbuf("act", [P, P, 4], F32, tag="act", bufs=3)
-                nc.scalar.activation(act[:], y_first[b, jq][:].rearrange("p t j -> p j t"), ACT.Silu)
+                    wb_pass(y_first(b, jq)[:, t, :], b, t, P * jq, P, t == 3)
+                act = acts[b, jq][:].rearrange("p (j t) -> p j t", t=4)
+                nc.scalar.activation(act, y_first(b, jq).rearrange("p t j -> p j t"), ACT.Silu)
                 nc.vector.tensor_tensor(
-                    e_bf[:, P * u : P * (u + 1), :], act[:], gain_sb[:, b : b + 1, :].to_broadcast([P, P, 4]), MULT
+                    e_bf[b][:, P * jq : P * (jq + 1), :], act, gain_sb[:, b : b + 1, :].to_broadcast([P, P, 4]), MULT
                 )
-            cols = slice(256 * jp, 256 * (jp + 1))
-            nc.vector.quantize_mx(e_w[b, 0][:, cols].bitcast(FP8X4), e_sc[b, 0][:, cols], e_bf[:].rearrange("p j t -> p (j t)"))
+            nc.vector.quantize_mx(e_w[b, 0].bitcast(FP8X4), e_sc[b, 0][:], e_bf[b][:].rearrange("p j t -> p (j t)"))
 
         w2_q = {(a, b): {} for a in range(2) for b in range(2)}
 
         def quantise_w2(a, b, tp):
-            w2_q[a, b][tp] = quantise_weight("w2%d%d%d" % (a, b, tp), w2_raw[a, b], tp, nc.scalar.copy)
+            name = "w2%d%d%d" % (a, b, tp)
+            staging = acts[0, (b + tp) % 2]
+            if tp == 0:
+                codes = sbuf(name + "_w", [P, QUARTER], U32)[:]
+            else:
+                codes = sbuf(name + "_w", [P, QUARTER], U32, at_h[3 * a] + KIB * b)[:]
+            w2_q[a, b][tp] = quantise_weight(name, cast_weight(w2_raw[a, b], tp, staging), codes)
 
-        e_first(0, 0)
-        e_first(0, 1)
-        e_first(1, 0)
-        quantise_w2(0, 0, 0)
-        e_first(1, 1)
-        quantise_w2(0, 1, 0)
-
-        def encode(k, jh):
+        def encode(k, jh, cols, bank, h):
             a, t = divmod(k, 4)
-            acc = bank("h_acc%d%d" % (k, jh), [P, HALF], 4 + k % 4)
             for b in range(2):
                 codes, scales = stationary(w2_q[a, b], t)
                 nc.tensor.matmul_mx(
-                    acc[:], lhsT=codes, lhsT_scale=scales, rhs=e_w[b, jh][:].bitcast(FP8X4), rhs_scale=e_sc[b, jh][:],
+                    bank[:, cols], lhsT=codes, lhsT_scale=scales, rhs=e_w[b, jh][:, cols].bitcast(FP8X4), rhs_scale=e_sc[b, jh][:, cols],
                     start=(b == 0), stop=(b == 1),
                 )
-            h = sbuf("h%d%d" % (k, jh), [P, HALF], F32, "h%d" % k)
-            nc.scalar.copy(h[:], acc[:])
-            return h
+            nc.scalar.copy(h[:, cols], bank[:, cols])
 
-        def write_slots(k, jh, weight, h=None):
-            h = h if h is not None else encode(k, jh)
-            nc.vector.tensor_tensor(pages[k][:].indirect(idx2[:, 32 * jh : 32 * jh + 32]), h[:], weight, MULT)
+        def write_slots(k, jh, cols, h, weight):
+            first, last = (HALF * jh + cols.start) // 16, (HALF * jh + cols.stop) // 16
+            nc.vector.tensor_tensor(pages[k][:].indirect(idx2[:, first:last]), h[:, cols], weight[:, cols], MULT)
 
-        w2_raw[1, 0] = load_weight("w2_raw10", w2[0:HALF, HALF:], "tab0")
-        load_page(3, "tab1")
-        w2_raw[1, 1] = load_weight("w2_raw11", w2[HALF:, HALF:], "raw0")
-        load_page(4, "raw1")
+        whole = slice(0, HALF)
+        quarters = [slice(0, QUARTER), slice(QUARTER, HALF)]
+        planes = [sbuf("planes%d" % b, [P, 1024], F32, at_planes[b]) for b in range(2)]
+        woven = [sbuf("woven%d" % b, [P, HALF, 4], BF16) for b in range(2)]
 
-        write_slots(0, 0, wgs0[0][:])
-        write_slots(1, 0, wgs0[1][:])
+        def first_round(k):
+            h_first[k] = sbuf("h_first%d" % k, [P, HALF], F32, at_h[k])[:]
+            encode(k, 0, whole, banks[k], h_first[k])
+            write_slots(k, 0, whole, h_first[k], wgs0[k % 4])
+
+        e_first(0)
+        e_first(1)
+        quantise_w2(0, 0, 0)
+        quantise_w2(0, 1, 0)
+        gather_second_pass(1, at_last_act)
+        first_round(0)
+
+        def second_plane(b, t, bank):
+            acc = banks[bank]
+            wf_pass(acc[:], b, t, HALF, HALF, True)
+            wb_pass(acc[:], b, t, HALF, HALF, True)
+            act = acts[1, t % 2]
+            nc.scalar.activation(act[:], acc[:], ACT.Silu)
+            plane = planes[b][:].bitcast(BF16)[:, HALF * t : HALF * (t + 1)]
+            nc.scalar.activation(plane, act[:], ACT.Copy, scale=gain_sb[:, b, t : t + 1])
+
+        def second_weave(b):
+            source = planes[b][:].bitcast(BF16).rearrange("p (t c i) -> p c t i", t=4, i=4)
+            target = woven[b][:].rearrange("p (c i) t -> p c t i", i=4)
+            for u in range(2):
+                nc.scalar.copy(target[:, 64 * u : 64 * (u + 1)], source[:, 64 * u : 64 * (u + 1)])
+            e_w[b, 1] = sbuf("e_w%d1" % b, [P, HALF], U32, at_h[4 + 2 * b])[:]
+            nc.vector.quantize_mx(e_w[b, 1].bitcast(FP8X4), e_sc[b, 1][:], woven[b][:].rearrange("p j t -> p (j t)"))
+
+        load_page(4, at_tab0)
+        load_page(5, at_tab0 + 8 * KIB)
+        load_page(6, at_wb[0])
+        load_page(7, at_wb[1])
+
+        first_round(1)
         quantise_w2(0, 0, 1)
         quantise_w2(0, 1, 1)
-        load_page(5, "raw2")
-        load_page(6, "raw3")
-        write_slots(2, 0, wgs0[2][:])
+        second_plane(0, 0, 0)
+        second_plane(0, 1, 1)
+        first_round(2)
+        second_plane(0, 2, 2)
         quantise_w2(1, 0, 0)
-        write_slots(3, 0, wgs0[3][:])
         quantise_w2(1, 1, 0)
-        write_slots(4, 0, wgs0[0][:])
-        write_slots(5, 0, wgs0[1][:])
+        first_round(3)
+        first_round(4)
         quantise_w2(1, 0, 1)
         quantise_w2(1, 1, 1)
-        load_page(7, "tab0")
-        wgs1 = sbuf("wgs1", [P, 4, HALF], F32, "raw0")
-        for q in (0, 2, 1, 3):
-            nc.sync.dma_start(wgs1[32 * q : 32 * q + 32, :, :], wgs_rows[:, :, HALF:])
-        write_slots(6, 0, wgs0[2][:])
-        write_slots(7, 0, wgs0[3][:])
-
-        for b in range(2):
-            planes = sbuf("planes%d" % b, [P, 4, HALF], BF16)
-            for t in range(4):
-                acc = bank("y_second%d%d" % (b, t), [P, HALF], t)
-                wf_pass(acc[:], b, t, 1, slice(0, HALF), True)
-                wb_pass(acc[:], b, t, 1, slice(0, HALF), True)
-                act = sbuf("act", [P, HALF], F32, tag="act", bufs=3)
-                nc.scalar.activation(act[:], acc[:], ACT.Silu)
-                nc.scalar.activation(planes[:, t, :], act[:], ACT.Copy, scale=gain_sb[:, b, t : t + 1])
-            woven = sbuf("woven%d" % b, [P, HALF, 4], BF16)
-            nc.scalar.copy(
-                woven[:].rearrange("p (c i) t -> p c t i", i=4), planes[:].rearrange("p t (c i) -> p c t i", i=4)
-            )
-            nc.vector.quantize_mx(e_w[b, 1][:].bitcast(FP8X4), e_sc[b, 1][:], woven[:].rearrange("p j t -> p (j t)"))
+        wgs1 = load_wgs("wgs1", slice(0, 4), slice(HALF, S), at_w2[3])
+        first_round(5)
+        second_plane(0, 3, 4)
+        second_weave(0)
+        second_plane(1, 0, 5)
+        second_plane(1, 1, 4)
+        first_round(6)
+        second_plane(1, 2, 6)
+        second_plane(1, 3, 5)
+        second_weave(1)
+        first_round(7)
 
         w3_w = []
         for a in range(2):
-            w3_w.append(sbuf("w3_w%d" % a, [P, 512], I32, "v_w%d1" % a))
+            w3_w.append(sbuf("w3_w%d" % a, [P, 512], I32, at_w2[0] + 2 * KIB * a))
             nc.sync.dma_start(w3_w[a][:], w3_words[a].rearrange("p c i -> p (c i)").bitcast(I32))
-        shift_sb = sbuf("shift_sb", [P, 4, M], F32, "planes0")
+        w3_sc = wf_sc_raw[:, 0:512]
+        for q in range(4):
+            nc.sync.dma_start(w3_sc[32 * q : 32 * q + 8, :].bitcast(I32), w3_scales[:, 4 * q : 4 * q + 4, :].bitcast(I32))
+        shift_sb = sbuf("shift_sb", [P, 4, M], F32, at_w2[1])
         nc.sync.dma_start(shift_sb[:], shift.rearrange("(n p) m -> p n m", p=P))
 
-        h_second = [encode(k, 1) for k in range(8)]
+        h_second = [acts[0, jq][:] for jq in range(4)]
+        h_second = h_second + [e_bf[b][:].rearrange("p j t -> p (j t)").bitcast(F32)[:, HALF * u : HALF * (u + 1)] for b in range(2) for u in range(2)]
+        for k in range(8):
+            encode(k, 1, whole, banks[k % 4], h_second[k])
 
-        z_bf = {}
-        for mh in range(2):
-            z_bf[0, mh] = sbuf("z_bf0%d" % mh, [P, 256, 4], BF16, "e_w%d1" % mh)
-            z_bf[1, mh] = sbuf("z_bf1%d" % mh, [P, 256, 4], BF16)
+        z_bf = {(a, mh): woven[a][:, quarters[mh], :] for a in range(2) for mh in range(2)}
 
         def add_bias(k, mh, x):
             a, t = divmod(k, 4)
             nc.scalar.activation(z_bf[a, mh][:, :, t], x, ACT.Identity, bias=bias_sb[:, a, t : t + 1])
 
         def read_slots(k):
-            x = sbuf("x%d" % k, [P, M], F32, "h%d" % ((k + 1) % 7))
-            nc.vector.tensor_copy(x[:], pages[k][:].indirect(idx3[:]))
+            x = h_second[k]
+            nc.vector.tensor_copy(x, pages[k][:].indirect(idx3[:]))
             for mh in range(2):
-                add_bias(k, mh, x[:, 256 * mh : 256 * (mh + 1)])
-
-        accs = {}
+                add_bias(k, mh, x[:, quarters[mh]])
 
         def project(a, mh):
-            codes = sbuf("z_w%d%d" % (a, mh), [P, 256], U32)
-            scales = sbuf("z_sc%d%d" % (a, mh), [P, 256], U8)
-            nc.vector.quantize_mx(codes[:].bitcast(FP8X4), scales[:], z_bf[a, mh][:].rearrange("p m t -> p (m t)"))
+            codes = sbuf("z_w%d%d" % (a, mh), [P, QUARTER], U32)
+            scales = sbuf("z_sc%d%d" % (a, mh), [P, QUARTER], U8)
+            nc.vector.quantize_mx(codes[:].bitcast(FP8X4), scales[:], z_bf[a, mh].rearrange("p m t -> p (m t)"))
             for n in range(4):
-                if a == 0:
-                    accs[n, mh] = bank("o_acc%d%d" % (n, mh), [P, 256], 4 * mh + n)
                 cols = slice(P * n, P * (n + 1))
                 nc.tensor.matmul_mx(
-                    accs[n, mh][:], lhsT=w3_w[a][:, cols].bitcast(FP8X4), lhsT_scale=w3_sc[4 * a : P, cols],
+                    banks[4 * (1 - mh) + n][:, 0:QUARTER], lhsT=w3_w[a][:, cols].bitcast(FP8X4), lhsT_scale=w3_sc[4 * a : P, cols],
                     rhs=codes[:].bitcast(FP8X4), rhs_scale=scales[:], start=(a == 0), stop=(a == 1),
                 )
 
-        write_slots(0, 1, wgs1[:, 0, :], h_second[0])
+        write_slots(0, 1, whole, h_second[0], wgs1[:, 0, :])
         for k in range(1, 7):
-            write_slots(k, 1, wgs1[:, k % 4, :], h_second[k])
+            write_slots(k, 1, whole, h_second[k], wgs1[:, k % 4, :])
             read_slots(k - 1)
             if k == 5:
                 project(0, 0)
                 project(0, 1)
         read_slots(6)
-        write_slots(7, 1, wgs1[:, 3, :], h_second[7])
+        write_slots(7, 1, whole, h_second[7], wgs1[:, 3, :])
         for mh in range(2):
-            x = sbuf("x7%d" % mh, [P, 256], F32, "h%d" % (1 + mh))
-            nc.vector.tensor_copy(x[:], pages[7][:].indirect(idx3[:, 16 * mh : 16 * mh + 16]))
-            add_bias(7, mh, x[:])
+            x = h_second[7][:, quarters[mh]]
+            nc.vector.tensor_copy(x, pages[7][:].indirect(idx3[:, 16 * mh : 16 * mh + 16]))
+            add_bias(7, mh, x)
         for mh in range(2):
             project(1, mh)
         for mh in range(2):
-            cols = slice(256 * mh, 256 * (mh + 1))
             for n in range(4):
-                res = sbuf("res%d%d" % (n, mh), [P, 256], F32)
-                nc.vector.tensor_tensor(res[:], accs[n, mh][:], shift_sb[:, n, cols], ADD)
-                nc.sync.dma_start(out[P * n : P * (n + 1), cols], res[:])
+                res = shift_sb[:, n, quarters[mh]]
+                nc.vector.tensor_tensor(res, banks[4 * (1 - mh) + n][:, 0:QUARTER], res, ADD)
+                nc.sync.dma_start(out[P * n : P * (n + 1), quarters[mh]], res)

@@ -51,13 +51,14 @@ def tile_list_query_slot_cache_kernel(
         idx3 = lists.tile([P, M // 16], U16, name="idx3")
 
         at_tab0 = room(16 * KIB)
+        at_scales = free[0]
         tab_sc = sbuf("tab_sc", [P, T], U8)
         wf_sc_raw = sbuf("wf_sc_raw", [P, 1024], U8)
         wf_w = sbuf("wf_w", [P, 1024], U16)
         wf_sc = sbuf("wf_sc", [P, 1024], U8)
-        wf_raw = sbuf("wf_raw", [P, 56 * KIB], U16, at=free[0])
+        wf_raw = sbuf("wf_raw", [P, 1024], U16)
         at_tab1 = room(16 * KIB)
-        at_wb = [room(8 * KIB) for b in range(2)]
+        at_wb = room(16 * KIB)
         at_w2 = [room(8 * KIB) for b in range(4)]
 
         def load_tab(a, at):
@@ -85,25 +86,25 @@ def tile_list_query_slot_cache_kernel(
             return tile
 
         nc.sync.dma_start(idx[:], offs)
-        nc.sync.dma_start(wf_raw[:, 0:1024].bitcast(I32), wf_words[0].bitcast(I32))
-        nc.gpsimd.memset(wf_sc_raw[:].bitcast(I32), 0)
-        for q in range(4):
-            nc.sync.dma_start(wf_sc_raw[32 * q : 32 * q + 4, :].bitcast(I32), wf_scales[0, 4 * q : 4 * q + 4, :].bitcast(I32))
         tab = [load_tab(0, at_tab0)]
-        nc.sync.dma_start(idx2[:], offs2)
-        nc.sync.dma_start(idx3[:], offs3)
-        nc.vector.memset(tab_sc[:].bitcast(I32), 0)
-        for q in range(4):
-            nc.sync.dma_start(tab_sc[32 * q : 32 * q + 8, :].bitcast(I32), tab_scales[:, 4 * q : 4 * q + 4, :].bitcast(I32))
-        nc.vector.tensor_copy(
-            wf_w[:].rearrange("p (b t m) -> p b t m", b=2, t=4),
-            wf_raw[:, 0:1024].rearrange("p (b m t) -> p b t m", b=2, t=4),
-        )
-        tab.append(load_tab(1, at_tab1))
-        wb_raw = [load_weight("wb_raw0", wb[:, 0:HALF], at_wb[0])]
+        nc.sync.dma_start(wf_raw[:].bitcast(I32), wf_words[0].bitcast(I32))
+        wb_raw = sbuf("wb_raw", [P, 4, S], F32, at_wb)
+        nc.sync.dma_start(wb_raw[:], wb.rearrange("(p i) c -> p i c", i=4))
         gain_sb = sbuf("gain_sb", [P, 2, 4], F32)
         nc.sync.dma_start(gain_sb[:], gain.rearrange("(b p t) -> p b t", b=2, t=4))
-        wb_raw.append(load_weight("wb_raw1", wb[:, HALF:], at_wb[1]))
+        tab.append(load_tab(1, at_tab1))
+        nc.sync.dma_start(idx2[:], offs2)
+        nc.sync.dma_start(idx3[:], offs3)
+        for plane in (tab_sc, wf_sc_raw):
+            nc.vector.memset(plane[:].bitcast(I32), 0)
+        for q in range(4):
+            nc.gpsimd.dma_start(tab_sc[32 * q : 32 * q + 8, :].bitcast(I32), tab_scales[:, 4 * q : 4 * q + 4, :].bitcast(I32))
+        for q in range(4):
+            nc.gpsimd.dma_start(wf_sc_raw[32 * q : 32 * q + 4, :].bitcast(I32), wf_scales[0, 4 * q : 4 * q + 4, :].bitcast(I32))
+        nc.vector.tensor_copy(
+            wf_w[:].rearrange("p (b t m) -> p b t m", b=2, t=4),
+            wf_raw[:].rearrange("p (b m t) -> p b t m", b=2, t=4),
+        )
         w2_raw = {}
         for b in range(2):
             w2_raw[0, b] = load_weight("w2_raw0%d" % b, w2[HALF * b : HALF * (b + 1), 0:HALF], at_w2[b])
@@ -129,13 +130,12 @@ def tile_list_query_slot_cache_kernel(
         )
         v1 = {}
 
-        def gather_second_pass(jh, at):
-            v1[jh] = sbuf("v1%d" % jh, [P, HALF], U32, at)
+        def gather_second_pass(jh):
+            v1[jh] = sbuf("v1%d" % jh, [P, HALF], U32, at_scales + (3 - 2 * jh) * KIB)
             nc.vector.tensor_copy(v1[jh][:], tab[1][:].bitcast(U32).indirect(idx[:, 32 * jh : 32 * jh + 32]))
 
-        at_last_act = room(2 * KIB)
-        acts = {(b, jq): sbuf("act%d%d" % (b, jq), [P, HALF], F32, at_last_act if (b, jq) == (1, 3) else None) for b in range(2) for jq in range(4)}
-        wb_grouped = sbuf("wb_grouped", [P, 4, P, 4], BF16)
+        acts = {(b, jq): sbuf("act%d%d" % (b, jq), [P, HALF], F32) for b in range(2) for jq in range(4)}
+        wb_grouped = [sbuf("wb_grouped%d" % b, [P, 4, P, 4], BF16) for b in range(2)]
 
         def cast_weight(raw, tp, staging):
             tile = staging[:].bitcast(BF16).rearrange("p (t m i) -> p t m i", t=2, i=4)
@@ -172,7 +172,7 @@ def tile_list_query_slot_cache_kernel(
             )
 
         at_planes = [room(4 * KIB) for b in range(2)]
-        at_h = [room(2 * KIB) for k in range(7)] + [at_planes[1]]
+        at_h = [room(2 * KIB) for k in range(7)]
         h_first = {}
         e_w = {(b, 0): sbuf("e_w%d" % b, [P, HALF], U32)[:] for b in range(2)}
         e_sc = {(b, jh): sbuf("e_sc%d%d" % (b, jh), [P, HALF], U8) for b in range(2) for jh in range(2)}
@@ -185,20 +185,22 @@ def tile_list_query_slot_cache_kernel(
                 for t in range(4):
                     wf_pass(y_first(b, jq)[:, t, :], b, t, P * jq, P, t == 0)
 
-        gather_second_pass(0, None)
         for b in range(2):
-            nc.vector.tensor_copy(
-                wb_grouped[:].rearrange("p t m i -> p m i t"), wb_raw[b][:].rearrange("p i (m t) -> p m i t", t=4)
+            nc.scalar.copy(
+                wb_grouped[b][:].rearrange("p t m i -> p m i t"), wb_raw[:, :, HALF * b : HALF * (b + 1)].rearrange("p i (m t) -> p m i t", t=4)
             )
             codes = sbuf("wb%d_w" % b, [P, HALF], U32)
             scales = sbuf("wb%d_sc" % b, [P, HALF], U8)
-            nc.vector.quantize_mx(codes[:].bitcast(FP8X4), scales[:], wb_grouped[:].rearrange("p t m i -> p (t m i)"))
+            nc.vector.quantize_mx(codes[:].bitcast(FP8X4), scales[:], wb_grouped[b][:].rearrange("p t m i -> p (t m i)"))
             wb_q[b] = [(codes[:, 256 * tp : 256 * (tp + 1)], scales[:, 256 * tp : 256 * (tp + 1)]) for tp in range(2)]
+
+        for jh in range(2):
+            gather_second_pass(jh)
 
         e_bf = [sbuf("e_bf%d" % b, [P, HALF, 4], BF16) for b in range(2)]
 
-        def e_first(b):
-            for jq in range(4):
+        def e_first(b, jp):
+            for jq in (2 * jp, 2 * jp + 1):
                 for t in range(4):
                     wb_pass(y_first(b, jq)[:, t, :], b, t, P * jq, P, t == 3)
                 act = acts[b, jq][:].rearrange("p (j t) -> p j t", t=4)
@@ -206,13 +208,14 @@ def tile_list_query_slot_cache_kernel(
                 nc.vector.tensor_tensor(
                     e_bf[b][:, P * jq : P * (jq + 1), :], act, gain_sb[:, b : b + 1, :].to_broadcast([P, P, 4]), MULT
                 )
-            nc.vector.quantize_mx(e_w[b, 0].bitcast(FP8X4), e_sc[b, 0][:], e_bf[b][:].rearrange("p j t -> p (j t)"))
+            cols = slice(QUARTER * jp, QUARTER * (jp + 1))
+            nc.vector.quantize_mx(e_w[b, 0][:, cols].bitcast(FP8X4), e_sc[b, 0][:, cols], e_bf[b][:, cols, :].rearrange("p j t -> p (j t)"))
 
         w2_q = {(a, b): {} for a in range(2) for b in range(2)}
 
         def quantise_w2(a, b, tp):
             name = "w2%d%d%d" % (a, b, tp)
-            staging = acts[0, (b + tp) % 2]
+            staging = acts[0, 2 + (b + tp) % 2 if a == 0 else 2 * tp + b]
             if tp == 0:
                 codes = sbuf(name + "_w", [P, QUARTER], U32)[:]
             else:
@@ -239,22 +242,26 @@ def tile_list_query_slot_cache_kernel(
         woven = [sbuf("woven%d" % b, [P, HALF, 4], BF16) for b in range(2)]
 
         def first_round(k):
-            h_first[k] = sbuf("h_first%d" % k, [P, HALF], F32, at_h[k])[:]
+            h_first[k] = sbuf("h_first%d" % k, [P, HALF], F32, at_h[k])[:] if k < 7 else planes[1][:, 0:HALF]
             encode(k, 0, whole, banks[k], h_first[k])
             write_slots(k, 0, whole, h_first[k], wgs0[k % 4])
 
-        e_first(0)
-        e_first(1)
+        e_first(0, 0)
+        e_first(1, 0)
         quantise_w2(0, 0, 0)
         quantise_w2(0, 1, 0)
-        gather_second_pass(1, at_last_act)
-        first_round(0)
+        h_first[0] = sbuf("h_first0", [P, HALF], F32, at_h[0])[:]
+        encode(0, 0, quarters[0], banks[0], h_first[0])
+        e_first(1, 1)
+        e_first(0, 1)
+        write_slots(0, 0, quarters[0], h_first[0], wgs0[0])
+        encode(0, 0, quarters[1], banks[4], h_first[0])
+        write_slots(0, 0, quarters[1], h_first[0], wgs0[0])
 
-        def second_plane(b, t, bank):
+        def second_plane(b, t, bank, act):
             acc = banks[bank]
             wf_pass(acc[:], b, t, HALF, HALF, True)
             wb_pass(acc[:], b, t, HALF, HALF, True)
-            act = acts[1, t % 2]
             nc.scalar.activation(act[:], acc[:], ACT.Silu)
             plane = planes[b][:].bitcast(BF16)[:, HALF * t : HALF * (t + 1)]
             nc.scalar.activation(plane, act[:], ACT.Copy, scale=gain_sb[:, b, t : t + 1])
@@ -264,47 +271,53 @@ def tile_list_query_slot_cache_kernel(
             target = woven[b][:].rearrange("p (c i) t -> p c t i", i=4)
             for u in range(2):
                 nc.scalar.copy(target[:, 64 * u : 64 * (u + 1)], source[:, 64 * u : 64 * (u + 1)])
+
+        def second_quantise(b):
             e_w[b, 1] = sbuf("e_w%d1" % b, [P, HALF], U32, at_h[4 + 2 * b])[:]
             nc.vector.quantize_mx(e_w[b, 1].bitcast(FP8X4), e_sc[b, 1][:], woven[b][:].rearrange("p j t -> p (j t)"))
 
         load_page(4, at_tab0)
         load_page(5, at_tab0 + 8 * KIB)
-        load_page(6, at_wb[0])
-        load_page(7, at_wb[1])
+        load_page(6, at_wb)
+        load_page(7, at_wb + 8 * KIB)
 
         first_round(1)
         quantise_w2(0, 0, 1)
         quantise_w2(0, 1, 1)
-        second_plane(0, 0, 0)
-        second_plane(0, 1, 1)
+        wgs1 = load_wgs("wgs1", slice(0, 4), slice(HALF, S), at_w2[0])
+        second_plane(0, 0, 4, acts[1, 0])
+        second_plane(0, 1, 1, acts[1, 1])
+        second_plane(0, 2, 4, acts[1, 0])
         first_round(2)
-        second_plane(0, 2, 2)
         quantise_w2(1, 0, 0)
         quantise_w2(1, 1, 0)
         first_round(3)
-        first_round(4)
         quantise_w2(1, 0, 1)
         quantise_w2(1, 1, 1)
-        wgs1 = load_wgs("wgs1", slice(0, 4), slice(HALF, S), at_w2[3])
-        first_round(5)
-        second_plane(0, 3, 4)
+        late_acts = [sbuf("late_act%d" % n, [P, HALF], F32, at_w2[3] + 2 * KIB * n) for n in range(2)]
+        second_plane(0, 3, 1, late_acts[0])
         second_weave(0)
-        second_plane(1, 0, 5)
-        second_plane(1, 1, 4)
+        first_round(4)
+        second_quantise(0)
+        first_round(5)
+        second_plane(1, 0, 2, late_acts[1])
         first_round(6)
-        second_plane(1, 2, 6)
-        second_plane(1, 3, 5)
+        second_plane(1, 1, 3, late_acts[0])
+        second_plane(1, 2, 0, late_acts[1])
+        second_plane(1, 3, 1, late_acts[0])
         second_weave(1)
+        second_quantise(1)
         first_round(7)
 
         w3_w = []
         for a in range(2):
-            w3_w.append(sbuf("w3_w%d" % a, [P, 512], I32, at_w2[0] + 2 * KIB * a))
+            w3_w.append(sbuf("w3_w%d" % a, [P, 512], I32, at_w2[3] + (4 + 2 * a) * KIB))
             nc.sync.dma_start(w3_w[a][:], w3_words[a].rearrange("p c i -> p (c i)").bitcast(I32))
-        w3_sc = wf_sc_raw[:, 0:512]
+        w3_sc = sbuf("w3_sc", [P, 512], U8, at_w2[1])
+        nc.gpsimd.memset(w3_sc[:].bitcast(I32), 0)
         for q in range(4):
             nc.sync.dma_start(w3_sc[32 * q : 32 * q + 8, :].bitcast(I32), w3_scales[:, 4 * q : 4 * q + 4, :].bitcast(I32))
-        shift_sb = sbuf("shift_sb", [P, 4, M], F32, at_w2[1])
+        shift_sb = sbuf("shift_sb", [P, 4, M], F32, at_w2[2])
         nc.sync.dma_start(shift_sb[:], shift.rearrange("(n p) m -> p n m", p=P))
 
         h_second = [acts[0, jq][:] for jq in range(4)]

@@ -134,25 +134,12 @@ def tile_list_query_slot_cache_kernel(
             v1[jh] = sbuf("v1%d" % jh, [P, HALF], U32, at_scales + (3 - 2 * jh) * KIB)
             nc.vector.tensor_copy(v1[jh][:], tab[1][:].bitcast(U32).indirect(idx[:, 32 * jh : 32 * jh + 32]))
 
-        acts = {(b, jq): sbuf("act%d%d" % (b, jq), [P, HALF], F32) for b in range(2) for jq in range(4)}
+        acts = {(b, jp): sbuf("act%d%d" % (b, jp), [P, 2 * HALF], F32) for b in range(2) for jp in range(2)}
         wb_grouped = [sbuf("wb_grouped%d" % b, [P, 4, P, 4], BF16) for b in range(2)]
 
-        def cast_weight(raw, tp, staging):
-            tile = staging[:].bitcast(BF16).rearrange("p (t m i) -> p t m i", t=2, i=4)
-            nc.scalar.copy(
-                tile.rearrange("p t m i -> p m i t"),
-                raw[:].rearrange("p i (m t) -> p m i t", t=4)[:, :, :, 2 * tp : 2 * tp + 2],
-            )
-            return tile
-
-        def quantise_weight(name, tile, codes):
-            scales = sbuf(name + "_sc", [P, 256], U8)
-            nc.vector.quantize_mx(codes.bitcast(FP8X4), scales[:], tile.rearrange("p t m i -> p (t m i)"))
-            return codes, scales
-
-        def stationary(pairs, t):
-            codes, scales = pairs[t // 2]
-            cols = slice(P * (t % 2), P * (t % 2 + 1))
+        def stationary(quantised, c):
+            codes, scales = quantised
+            cols = slice(P * c, P * (c + 1))
             return codes[:, cols].bitcast(FP8X4), scales[:, cols]
 
         def wf_pass(acc, b, t, j0, n, start):
@@ -175,7 +162,7 @@ def tile_list_query_slot_cache_kernel(
         at_h = [room(2 * KIB) for k in range(7)]
         h_first = {}
         e_w = {(b, 0): sbuf("e_w%d" % b, [P, HALF], U32)[:] for b in range(2)}
-        e_sc = {(b, jh): sbuf("e_sc%d%d" % (b, jh), [P, HALF], U8) for b in range(2) for jh in range(2)}
+        e_sc = {(b, 0): sbuf("e_sc%d" % b, [P, HALF], U8)[:] for b in range(2)}
 
         def y_first(b, jq):
             return banks[4 * b + jq][:].rearrange("p (t j) -> p t j", t=4)
@@ -192,40 +179,48 @@ def tile_list_query_slot_cache_kernel(
             codes = sbuf("wb%d_w" % b, [P, HALF], U32)
             scales = sbuf("wb%d_sc" % b, [P, HALF], U8)
             nc.vector.quantize_mx(codes[:].bitcast(FP8X4), scales[:], wb_grouped[b][:].rearrange("p t m i -> p (t m i)"))
-            wb_q[b] = [(codes[:, 256 * tp : 256 * (tp + 1)], scales[:, 256 * tp : 256 * (tp + 1)]) for tp in range(2)]
+            wb_q[b] = (codes, scales)
 
         for jh in range(2):
             gather_second_pass(jh)
 
         e_bf = [sbuf("e_bf%d" % b, [P, HALF, 4], BF16) for b in range(2)]
 
-        def e_first(b, jp):
-            for jq in (2 * jp, 2 * jp + 1):
-                for t in range(4):
-                    wb_pass(y_first(b, jq)[:, t, :], b, t, P * jq, P, t == 3)
-                act = acts[b, jq][:].rearrange("p (j t) -> p j t", t=4)
-                nc.scalar.activation(act, y_first(b, jq).rearrange("p t j -> p j t"), ACT.Silu)
+        def e_first(b):
+            for jp in range(2):
+                for u in range(2):
+                    jq = 2 * jp + u
+                    for t in range(4):
+                        wb_pass(y_first(b, jq)[:, t, :], b, t, P * jq, P, t == 3)
+                    act = acts[b, jp][:, HALF * u : HALF * (u + 1)].rearrange("p (j t) -> p j t", t=4)
+                    nc.scalar.activation(act, y_first(b, jq).rearrange("p t j -> p j t"), ACT.Silu)
                 nc.vector.tensor_tensor(
-                    e_bf[b][:, P * jq : P * (jq + 1), :], act, gain_sb[:, b : b + 1, :].to_broadcast([P, P, 4]), MULT
+                    e_bf[b][:, QUARTER * jp : QUARTER * (jp + 1), :], acts[b, jp][:].rearrange("p (j t) -> p j t", t=4),
+                    gain_sb[:, b : b + 1, :].to_broadcast([P, QUARTER, 4]), MULT,
                 )
-            cols = slice(QUARTER * jp, QUARTER * (jp + 1))
-            nc.vector.quantize_mx(e_w[b, 0][:, cols].bitcast(FP8X4), e_sc[b, 0][:, cols], e_bf[b][:, cols, :].rearrange("p j t -> p (j t)"))
+            nc.vector.quantize_mx(e_w[b, 0].bitcast(FP8X4), e_sc[b, 0], e_bf[b][:].rearrange("p j t -> p (j t)"))
 
-        w2_q = {(a, b): {} for a in range(2) for b in range(2)}
+        w2_q = {}
 
-        def quantise_w2(a, b, tp):
-            name = "w2%d%d%d" % (a, b, tp)
-            staging = acts[0, 2 + (b + tp) % 2 if a == 0 else 2 * tp + b]
-            if tp == 0:
-                codes = sbuf(name + "_w", [P, QUARTER], U32)[:]
-            else:
-                codes = sbuf(name + "_w", [P, QUARTER], U32, at_h[3 * a] + KIB * b)[:]
-            w2_q[a, b][tp] = quantise_weight(name, cast_weight(w2_raw[a, b], tp, staging), codes)
+        def quantise_w2(a, tp, staging, at, pieces):
+            grouped = staging[:].bitcast(BF16)
+            codes = sbuf("w2%d%d_w" % (a, tp), [P, HALF], U32, at)
+            scales = sbuf("w2%d%d_sc" % (a, tp), [P, HALF], U8)
+            for b in range(2):
+                nc.scalar.copy(
+                    grouped[:, S * b : S * (b + 1)].rearrange("p (t m i) -> p m i t", t=2, i=4),
+                    w2_raw[a, b][:].rearrange("p i (m t) -> p m i t", t=4)[:, :, :, 2 * tp : 2 * tp + 2],
+                )
+            width = HALF // pieces
+            for n in range(pieces):
+                cols = slice(width * n, width * (n + 1))
+                nc.vector.quantize_mx(codes[:, cols].bitcast(FP8X4), scales[:, cols], grouped[:, 4 * cols.start : 4 * cols.stop])
+            w2_q[a, tp] = (codes, scales)
 
         def encode(k, jh, cols, bank, h):
             a, t = divmod(k, 4)
             for b in range(2):
-                codes, scales = stationary(w2_q[a, b], t)
+                codes, scales = stationary(w2_q[a, t // 2], 2 * b + t % 2)
                 nc.tensor.matmul_mx(
                     bank[:, cols], lhsT=codes, lhsT_scale=scales, rhs=e_w[b, jh][:, cols].bitcast(FP8X4), rhs_scale=e_sc[b, jh][:, cols],
                     start=(b == 0), stop=(b == 1),
@@ -239,42 +234,40 @@ def tile_list_query_slot_cache_kernel(
         whole = slice(0, HALF)
         quarters = [slice(0, QUARTER), slice(QUARTER, HALF)]
         planes = [sbuf("planes%d" % b, [P, 1024], F32, at_planes[b]) for b in range(2)]
-        woven = [sbuf("woven%d" % b, [P, HALF, 4], BF16) for b in range(2)]
+        woven_both = sbuf("woven", [P, S, 4], BF16)
+        woven = [woven_both[:, HALF * b : HALF * (b + 1), :] for b in range(2)]
 
         def first_round(k):
             h_first[k] = sbuf("h_first%d" % k, [P, HALF], F32, at_h[k])[:] if k < 7 else planes[1][:, 0:HALF]
             encode(k, 0, whole, banks[k], h_first[k])
             write_slots(k, 0, whole, h_first[k], wgs0[k % 4])
 
-        e_first(0, 0)
-        e_first(1, 0)
-        quantise_w2(0, 0, 0)
-        quantise_w2(0, 1, 0)
-        h_first[0] = sbuf("h_first0", [P, HALF], F32, at_h[0])[:]
-        encode(0, 0, quarters[0], banks[0], h_first[0])
-        e_first(1, 1)
-        e_first(0, 1)
-        write_slots(0, 0, quarters[0], h_first[0], wgs0[0])
-        encode(0, 0, quarters[1], banks[4], h_first[0])
-        write_slots(0, 0, quarters[1], h_first[0], wgs0[0])
+        e_first(0)
+        e_first(1)
+        quantise_w2(0, 0, acts[0, 0], None, 2)
+        first_round(0)
 
         def second_plane(b, t, bank, act):
             acc = banks[bank]
             wf_pass(acc[:], b, t, HALF, HALF, True)
             wb_pass(acc[:], b, t, HALF, HALF, True)
-            nc.scalar.activation(act[:], acc[:], ACT.Silu)
+            nc.scalar.activation(act, acc[:], ACT.Silu)
             plane = planes[b][:].bitcast(BF16)[:, HALF * t : HALF * (t + 1)]
-            nc.scalar.activation(plane, act[:], ACT.Copy, scale=gain_sb[:, b, t : t + 1])
+            nc.scalar.activation(plane, act, ACT.Copy, scale=gain_sb[:, b, t : t + 1])
 
         def second_weave(b):
             source = planes[b][:].bitcast(BF16).rearrange("p (t c i) -> p c t i", t=4, i=4)
-            target = woven[b][:].rearrange("p (c i) t -> p c t i", i=4)
+            target = woven[b].rearrange("p (c i) t -> p c t i", i=4)
             for u in range(2):
                 nc.scalar.copy(target[:, 64 * u : 64 * (u + 1)], source[:, 64 * u : 64 * (u + 1)])
 
-        def second_quantise(b):
-            e_w[b, 1] = sbuf("e_w%d1" % b, [P, HALF], U32, at_h[4 + 2 * b])[:]
-            nc.vector.quantize_mx(e_w[b, 1].bitcast(FP8X4), e_sc[b, 1][:], woven[b][:].rearrange("p j t -> p (j t)"))
+        def second_quantise():
+            codes = sbuf("e_w_second", [P, S], U32, at_h[5])
+            scales = sbuf("e_sc_second", [P, S], U8)
+            nc.vector.quantize_mx(codes[:].bitcast(FP8X4), scales[:], woven_both[:].rearrange("p j t -> p (j t)"))
+            for b in range(2):
+                e_w[b, 1] = codes[:, HALF * b : HALF * (b + 1)]
+                e_sc[b, 1] = scales[:, HALF * b : HALF * (b + 1)]
 
         load_page(4, at_tab0)
         load_page(5, at_tab0 + 8 * KIB)
@@ -282,23 +275,20 @@ def tile_list_query_slot_cache_kernel(
         load_page(7, at_wb + 8 * KIB)
 
         first_round(1)
-        quantise_w2(0, 0, 1)
-        quantise_w2(0, 1, 1)
+        quantise_w2(0, 1, acts[1, 1], at_h[0], 1)
         wgs1 = load_wgs("wgs1", slice(0, 4), slice(HALF, S), at_w2[0])
-        second_plane(0, 0, 4, acts[1, 0])
-        second_plane(0, 1, 1, acts[1, 1])
-        second_plane(0, 2, 4, acts[1, 0])
+        early_acts = [acts[1, 0][:, HALF * u : HALF * (u + 1)] for u in range(2)]
+        second_plane(0, 0, 0, early_acts[0])
+        second_plane(0, 1, 1, early_acts[1])
+        second_plane(0, 2, 0, early_acts[0])
         first_round(2)
-        quantise_w2(1, 0, 0)
-        quantise_w2(1, 1, 0)
+        quantise_w2(1, 0, acts[0, 0], None, 1)
         first_round(3)
-        quantise_w2(1, 0, 1)
-        quantise_w2(1, 1, 1)
-        late_acts = [sbuf("late_act%d" % n, [P, HALF], F32, at_w2[3] + 2 * KIB * n) for n in range(2)]
+        quantise_w2(1, 1, acts[0, 1], at_h[3], 1)
+        late_acts = [sbuf("late_act%d" % n, [P, HALF], F32, at_w2[3] + 2 * KIB * n)[:] for n in range(2)]
         second_plane(0, 3, 1, late_acts[0])
         second_weave(0)
         first_round(4)
-        second_quantise(0)
         first_round(5)
         second_plane(1, 0, 2, late_acts[1])
         first_round(6)
@@ -306,7 +296,7 @@ def tile_list_query_slot_cache_kernel(
         second_plane(1, 2, 0, late_acts[1])
         second_plane(1, 3, 1, late_acts[0])
         second_weave(1)
-        second_quantise(1)
+        second_quantise()
         first_round(7)
 
         w3_w = []
@@ -320,7 +310,7 @@ def tile_list_query_slot_cache_kernel(
         shift_sb = sbuf("shift_sb", [P, 4, M], F32, at_w2[2])
         nc.sync.dma_start(shift_sb[:], shift.rearrange("(n p) m -> p n m", p=P))
 
-        h_second = [acts[0, jq][:] for jq in range(4)]
+        h_second = [acts[0, jp][:, HALF * u : HALF * (u + 1)] for jp in range(2) for u in range(2)]
         h_second = h_second + [e_bf[b][:].rearrange("p j t -> p (j t)").bitcast(F32)[:, HALF * u : HALF * (u + 1)] for b in range(2) for u in range(2)]
         for k in range(8):
             encode(k, 1, whole, banks[k % 4], h_second[k])
@@ -337,15 +327,19 @@ def tile_list_query_slot_cache_kernel(
             for mh in range(2):
                 add_bias(k, mh, x[:, quarters[mh]])
 
+        z_w = [sbuf("z_w%d" % a, [P, M], U32) for a in range(2)]
+        z_sc = [sbuf("z_sc%d" % a, [P, M], U8) for a in range(2)]
+
+        def quantise_z(a, cols):
+            nc.vector.quantize_mx(z_w[a][:, cols].bitcast(FP8X4), z_sc[a][:, cols], woven[a][:, cols, :].rearrange("p m t -> p (m t)"))
+
         def project(a, mh):
-            codes = sbuf("z_w%d%d" % (a, mh), [P, QUARTER], U32)
-            scales = sbuf("z_sc%d%d" % (a, mh), [P, QUARTER], U8)
-            nc.vector.quantize_mx(codes[:].bitcast(FP8X4), scales[:], z_bf[a, mh].rearrange("p m t -> p (m t)"))
             for n in range(4):
                 cols = slice(P * n, P * (n + 1))
                 nc.tensor.matmul_mx(
-                    banks[4 * (1 - mh) + n][:, 0:QUARTER], lhsT=w3_w[a][:, cols].bitcast(FP8X4), lhsT_scale=w3_sc[4 * a : P, cols],
-                    rhs=codes[:].bitcast(FP8X4), rhs_scale=scales[:], start=(a == 0), stop=(a == 1),
+                    banks[4 + 2 * mh + n // 2][:, quarters[n % 2]], lhsT=w3_w[a][:, cols].bitcast(FP8X4), lhsT_scale=w3_sc[4 * a : P, cols],
+                    rhs=z_w[a][:, quarters[mh]].bitcast(FP8X4), rhs_scale=z_sc[a][:, quarters[mh]],
+                    start=(a == 0 and n % 2 == 0), stop=(a == 1 and n % 2 == 1),
                 )
 
         write_slots(0, 1, whole, h_second[0], wgs1[:, 0, :])
@@ -353,6 +347,7 @@ def tile_list_query_slot_cache_kernel(
             write_slots(k, 1, whole, h_second[k], wgs1[:, k % 4, :])
             read_slots(k - 1)
             if k == 5:
+                quantise_z(0, whole)
                 project(0, 0)
                 project(0, 1)
         read_slots(6)
@@ -362,9 +357,11 @@ def tile_list_query_slot_cache_kernel(
             nc.vector.tensor_copy(x, pages[7][:].indirect(idx3[:, 16 * mh : 16 * mh + 16]))
             add_bias(7, mh, x)
         for mh in range(2):
+            quantise_z(1, quarters[mh])
             project(1, mh)
+        out_rows = out.rearrange("(n p) m -> p n m", p=P)
         for mh in range(2):
-            for n in range(4):
-                res = shift_sb[:, n, quarters[mh]]
-                nc.vector.tensor_tensor(res, banks[4 * (1 - mh) + n][:, 0:QUARTER], res, ADD)
-                nc.sync.dma_start(out[P * n : P * (n + 1), quarters[mh]], res)
+            for u in range(2):
+                res = shift_sb[:, 2 * u : 2 * u + 2, quarters[mh]]
+                nc.vector.tensor_tensor(res, banks[4 + 2 * mh + u][:].rearrange("p (n m) -> p n m", n=2), res, ADD)
+                nc.sync.dma_start(out_rows[:, 2 * u : 2 * u + 2, quarters[mh]], res)

@@ -58,7 +58,7 @@ def tile_list_query_slot_cache_kernel(
         wf_sc = sbuf("wf_sc", [P, 1024], U8)
         wf_raw = sbuf("wf_raw", [P, 1024], U16)
         at_tab1 = room(16 * KIB)
-        at_wb = room(16 * KIB)
+        at_wb = [room(8 * KIB) for b in range(2)]
         at_w2 = [room(8 * KIB) for b in range(4)]
 
         def load_tab(a, at):
@@ -88,11 +88,11 @@ def tile_list_query_slot_cache_kernel(
         nc.sync.dma_start(idx[:], offs)
         tab = [load_tab(0, at_tab0)]
         nc.sync.dma_start(wf_raw[:].bitcast(I32), wf_words[0].bitcast(I32))
-        wb_raw = sbuf("wb_raw", [P, 4, S], F32, at_wb)
-        nc.sync.dma_start(wb_raw[:], wb.rearrange("(p i) c -> p i c", i=4))
+        wb_raw = [load_weight("wb_raw0", wb[:, 0:HALF], at_wb[0])]
+        tab.append(load_tab(1, at_tab1))
+        wb_raw.append(load_weight("wb_raw1", wb[:, HALF:], at_wb[1]))
         gain_sb = sbuf("gain_sb", [P, 2, 4], F32)
         nc.sync.dma_start(gain_sb[:], gain.rearrange("(b p t) -> p b t", b=2, t=4))
-        tab.append(load_tab(1, at_tab1))
         nc.sync.dma_start(idx2[:], offs2)
         nc.sync.dma_start(idx3[:], offs3)
         for plane in (tab_sc, wf_sc_raw):
@@ -172,33 +172,38 @@ def tile_list_query_slot_cache_kernel(
                 for t in range(4):
                     wf_pass(y_first(b, jq)[:, t, :], b, t, P * jq, P, t == 0)
 
-        for b in range(2):
-            nc.scalar.copy(
-                wb_grouped[b][:].rearrange("p t m i -> p m i t"), wb_raw[:, :, HALF * b : HALF * (b + 1)].rearrange("p i (m t) -> p m i t", t=4)
-            )
+        def quantise_wb(b):
             codes = sbuf("wb%d_w" % b, [P, HALF], U32)
             scales = sbuf("wb%d_sc" % b, [P, HALF], U8)
             nc.vector.quantize_mx(codes[:].bitcast(FP8X4), scales[:], wb_grouped[b][:].rearrange("p t m i -> p (t m i)"))
             wb_q[b] = (codes, scales)
 
+        for tp in range(2):
+            nc.scalar.copy(
+                wb_grouped[0][:, 2 * tp : 2 * tp + 2].rearrange("p t m i -> p m i t"),
+                wb_raw[0][:].rearrange("p i (m t) -> p m i t", t=4)[:, :, :, 2 * tp : 2 * tp + 2],
+            )
+        quantise_wb(0)
         for jh in range(2):
             gather_second_pass(jh)
+        nc.vector.tensor_copy(wb_grouped[1][:].rearrange("p t m i -> p m i t"), wb_raw[1][:].rearrange("p i (m t) -> p m i t", t=4))
+        quantise_wb(1)
 
         e_bf = [sbuf("e_bf%d" % b, [P, HALF, 4], BF16) for b in range(2)]
 
-        def e_first(b):
-            for jp in range(2):
-                for u in range(2):
-                    jq = 2 * jp + u
-                    for t in range(4):
-                        wb_pass(y_first(b, jq)[:, t, :], b, t, P * jq, P, t == 3)
-                    act = acts[b, jp][:, HALF * u : HALF * (u + 1)].rearrange("p (j t) -> p j t", t=4)
-                    nc.scalar.activation(act, y_first(b, jq).rearrange("p t j -> p j t"), ACT.Silu)
-                nc.vector.tensor_tensor(
-                    e_bf[b][:, QUARTER * jp : QUARTER * (jp + 1), :], acts[b, jp][:].rearrange("p (j t) -> p j t", t=4),
-                    gain_sb[:, b : b + 1, :].to_broadcast([P, QUARTER, 4]), MULT,
-                )
-            nc.vector.quantize_mx(e_w[b, 0].bitcast(FP8X4), e_sc[b, 0], e_bf[b][:].rearrange("p j t -> p (j t)"))
+        def e_first(b, jp):
+            for u in range(2):
+                jq = 2 * jp + u
+                for t in range(4):
+                    wb_pass(y_first(b, jq)[:, t, :], b, t, P * jq, P, t == 3)
+                act = acts[b, jp][:, HALF * u : HALF * (u + 1)].rearrange("p (j t) -> p j t", t=4)
+                nc.scalar.activation(act, y_first(b, jq).rearrange("p t j -> p j t"), ACT.Silu)
+            cols = slice(QUARTER * jp, QUARTER * (jp + 1))
+            nc.vector.tensor_tensor(
+                e_bf[b][:, cols, :], acts[b, jp][:].rearrange("p (j t) -> p j t", t=4),
+                gain_sb[:, b : b + 1, :].to_broadcast([P, QUARTER, 4]), MULT,
+            )
+            nc.vector.quantize_mx(e_w[b, 0][:, cols].bitcast(FP8X4), e_sc[b, 0][:, cols], e_bf[b][:, cols, :].rearrange("p j t -> p (j t)"))
 
         w2_q = {}
 
@@ -242,10 +247,16 @@ def tile_list_query_slot_cache_kernel(
             encode(k, 0, whole, banks[k], h_first[k])
             write_slots(k, 0, whole, h_first[k], wgs0[k % 4])
 
-        e_first(0)
-        e_first(1)
-        quantise_w2(0, 0, acts[0, 0], None, 2)
-        first_round(0)
+        e_first(0, 0)
+        e_first(1, 0)
+        quantise_w2(0, 0, wb_grouped[0][:].rearrange("p t m i -> p (t m i)").bitcast(F32), None, 2)
+        h_first[0] = sbuf("h_first0", [P, HALF], F32, at_h[0])[:]
+        encode(0, 0, quarters[0], banks[0], h_first[0])
+        e_first(0, 1)
+        e_first(1, 1)
+        write_slots(0, 0, quarters[0], h_first[0], wgs0[0])
+        encode(0, 0, quarters[1], banks[4], h_first[0])
+        write_slots(0, 0, quarters[1], h_first[0], wgs0[0])
 
         def second_plane(b, t, bank, act):
             acc = banks[bank]
@@ -271,16 +282,16 @@ def tile_list_query_slot_cache_kernel(
 
         load_page(4, at_tab0)
         load_page(5, at_tab0 + 8 * KIB)
-        load_page(6, at_wb)
-        load_page(7, at_wb + 8 * KIB)
+        load_page(6, at_wb[0])
+        load_page(7, at_wb[1])
 
         first_round(1)
         quantise_w2(0, 1, acts[1, 1], at_h[0], 1)
         wgs1 = load_wgs("wgs1", slice(0, 4), slice(HALF, S), at_w2[0])
         early_acts = [acts[1, 0][:, HALF * u : HALF * (u + 1)] for u in range(2)]
-        second_plane(0, 0, 0, early_acts[0])
+        second_plane(0, 0, 4, early_acts[0])
         second_plane(0, 1, 1, early_acts[1])
-        second_plane(0, 2, 0, early_acts[0])
+        second_plane(0, 2, 4, early_acts[0])
         first_round(2)
         quantise_w2(1, 0, acts[0, 0], None, 1)
         first_round(3)
@@ -360,8 +371,9 @@ def tile_list_query_slot_cache_kernel(
             quantise_z(1, quarters[mh])
             project(1, mh)
         out_rows = out.rearrange("(n p) m -> p n m", p=P)
-        for mh in range(2):
-            for u in range(2):
-                res = shift_sb[:, 2 * u : 2 * u + 2, quarters[mh]]
-                nc.vector.tensor_tensor(res, banks[4 + 2 * mh + u][:].rearrange("p (n m) -> p n m", n=2), res, ADD)
-                nc.sync.dma_start(out_rows[:, 2 * u : 2 * u + 2, quarters[mh]], res)
+        for mh, first, count in ((0, 0, 2), (0, 2, 2), (1, 0, 2), (1, 2, 1), (1, 3, 1)):
+            res = shift_sb[:, first : first + count, quarters[mh]]
+            acc = banks[4 + 2 * mh + first // 2][:].rearrange("p (n m) -> p n m", n=2)[:, first % 2 : first % 2 + count]
+            nc.vector.tensor_tensor(res, acc, res, ADD)
+            queue = nc.scalar if first == 2 else nc.sync
+            queue.dma_start(out_rows[:, first : first + count, quarters[mh]], res)

@@ -95,8 +95,8 @@ def tile_list_query_slot_cache_kernel(
         nc.sync.dma_start(gain_sb[:], gain.rearrange("(b p t) -> p b t", b=2, t=4))
         nc.sync.dma_start(idx2[:], offs2)
         nc.sync.dma_start(idx3[:], offs3)
-        for plane in (tab_sc, wf_sc_raw):
-            nc.vector.memset(plane[:].bitcast(I32), 0)
+        for scale_tile in (tab_sc, wf_sc_raw):
+            nc.vector.memset(scale_tile[:].bitcast(I32), 0)
         for q in range(4):
             nc.gpsimd.dma_start(tab_sc[32 * q : 32 * q + 8, :].bitcast(I32), tab_scales[:, 4 * q : 4 * q + 4, :].bitcast(I32))
         for q in range(4):
@@ -159,8 +159,8 @@ def tile_list_query_slot_cache_kernel(
             )
 
         at_planes = [room(4 * KIB) for b in range(2)]
+        at_before_h = room(KIB)
         at_h = [room(2 * KIB) for k in range(7)]
-        h_first = {}
         e_w = {(b, 0): sbuf("e_w%d" % b, [P, HALF], U32)[:] for b in range(2)}
         e_sc = {(b, 0): sbuf("e_sc%d" % b, [P, HALF], U8)[:] for b in range(2)}
 
@@ -230,11 +230,11 @@ def tile_list_query_slot_cache_kernel(
                     bank[:, cols], lhsT=codes, lhsT_scale=scales, rhs=e_w[b, jh][:, cols].bitcast(FP8X4), rhs_scale=e_sc[b, jh][:, cols],
                     start=(b == 0), stop=(b == 1),
                 )
-            nc.scalar.copy(h[:, cols], bank[:, cols])
+            nc.scalar.copy(h, bank[:, cols])
 
         def write_slots(k, jh, cols, h, weight):
             first, last = (HALF * jh + cols.start) // 16, (HALF * jh + cols.stop) // 16
-            nc.vector.tensor_tensor(pages[k][:].indirect(idx2[:, first:last]), h[:, cols], weight[:, cols], MULT)
+            nc.vector.tensor_tensor(pages[k][:].indirect(idx2[:, first:last]), h, weight[:, cols], MULT)
 
         whole = slice(0, HALF)
         quarters = [slice(0, QUARTER), slice(QUARTER, HALF)]
@@ -243,20 +243,20 @@ def tile_list_query_slot_cache_kernel(
         woven = [woven_both[:, HALF * b : HALF * (b + 1), :] for b in range(2)]
 
         def first_round(k):
-            h_first[k] = sbuf("h_first%d" % k, [P, HALF], F32, at_h[k])[:] if k < 7 else planes[1][:, 0:HALF]
-            encode(k, 0, whole, banks[k], h_first[k])
-            write_slots(k, 0, whole, h_first[k], wgs0[k % 4])
+            h = sbuf("h_first%d" % k, [P, HALF], F32, at_h[k])[:] if k < 7 else planes[1][:, 0:HALF]
+            encode(k, 0, whole, banks[k], h)
+            write_slots(k, 0, whole, h, wgs0[k % 4])
 
         e_first(0, 0)
         e_first(1, 0)
         quantise_w2(0, 0, wb_grouped[0][:].rearrange("p t m i -> p (t m i)").bitcast(F32), None, 2)
-        h_first[0] = sbuf("h_first0", [P, HALF], F32, at_h[0])[:]
-        encode(0, 0, quarters[0], banks[0], h_first[0])
+        h_quarter = [sbuf("h_quarter%d" % u, [P, QUARTER], F32, at_h[0] + KIB * u)[:] for u in range(2)]
+        encode(0, 0, quarters[0], banks[0], h_quarter[0])
         e_first(0, 1)
         e_first(1, 1)
-        write_slots(0, 0, quarters[0], h_first[0], wgs0[0])
-        encode(0, 0, quarters[1], banks[4], h_first[0])
-        write_slots(0, 0, quarters[1], h_first[0], wgs0[0])
+        write_slots(0, 0, quarters[0], h_quarter[0], wgs0[0])
+        encode(0, 0, quarters[1], banks[4], h_quarter[1])
+        write_slots(0, 0, quarters[1], h_quarter[1], wgs0[0])
 
         def second_plane(b, t, bank, act):
             acc = banks[bank]
@@ -286,7 +286,7 @@ def tile_list_query_slot_cache_kernel(
         load_page(7, at_wb[1])
 
         first_round(1)
-        quantise_w2(0, 1, acts[1, 1], at_h[0], 1)
+        quantise_w2(0, 1, acts[1, 1], at_before_h, 1)
         wgs1 = load_wgs("wgs1", slice(0, 4), slice(HALF, S), at_w2[0])
         early_acts = [acts[1, 0][:, HALF * u : HALF * (u + 1)] for u in range(2)]
         second_plane(0, 0, 4, early_acts[0])
@@ -295,7 +295,7 @@ def tile_list_query_slot_cache_kernel(
         first_round(2)
         quantise_w2(1, 0, acts[0, 0], None, 1)
         first_round(3)
-        quantise_w2(1, 1, acts[0, 1], at_h[3], 1)
+        quantise_w2(1, 1, acts[0, 1], at_h[2], 1)
         late_acts = [sbuf("late_act%d" % n, [P, HALF], F32, at_w2[3] + 2 * KIB * n)[:] for n in range(2)]
         second_plane(0, 3, 1, late_acts[0])
         second_weave(0)
@@ -338,18 +338,15 @@ def tile_list_query_slot_cache_kernel(
             for mh in range(2):
                 add_bias(k, mh, x[:, quarters[mh]])
 
-        z_w = [sbuf("z_w%d" % a, [P, M], U32) for a in range(2)]
-        z_sc = [sbuf("z_sc%d" % a, [P, M], U8) for a in range(2)]
-
-        def quantise_z(a, cols):
-            nc.vector.quantize_mx(z_w[a][:, cols].bitcast(FP8X4), z_sc[a][:, cols], woven[a][:, cols, :].rearrange("p m t -> p (m t)"))
-
-        def project(a, mh):
+        def project(a, mh, at):
+            codes = sbuf("z_w%d%d" % (a, mh), [P, QUARTER], U32, at)
+            scales = sbuf("z_sc%d%d" % (a, mh), [P, QUARTER], U8)
+            nc.vector.quantize_mx(codes[:].bitcast(FP8X4), scales[:], z_bf[a, mh].rearrange("p m t -> p (m t)"))
             for n in range(4):
                 cols = slice(P * n, P * (n + 1))
                 nc.tensor.matmul_mx(
                     banks[4 + 2 * mh + n // 2][:, quarters[n % 2]], lhsT=w3_w[a][:, cols].bitcast(FP8X4), lhsT_scale=w3_sc[4 * a : P, cols],
-                    rhs=z_w[a][:, quarters[mh]].bitcast(FP8X4), rhs_scale=z_sc[a][:, quarters[mh]],
+                    rhs=codes[:].bitcast(FP8X4), rhs_scale=scales[:],
                     start=(a == 0 and n % 2 == 0), stop=(a == 1 and n % 2 == 1),
                 )
 
@@ -358,18 +355,16 @@ def tile_list_query_slot_cache_kernel(
             write_slots(k, 1, whole, h_second[k], wgs1[:, k % 4, :])
             read_slots(k - 1)
             if k == 5:
-                quantise_z(0, whole)
-                project(0, 0)
-                project(0, 1)
+                project(0, 0, None)
         read_slots(6)
         write_slots(7, 1, whole, h_second[7], wgs1[:, 3, :])
+        project(0, 1, at_w2[0])
         for mh in range(2):
             x = h_second[7][:, quarters[mh]]
             nc.vector.tensor_copy(x, pages[7][:].indirect(idx3[:, 16 * mh : 16 * mh + 16]))
             add_bias(7, mh, x)
         for mh in range(2):
-            quantise_z(1, quarters[mh])
-            project(1, mh)
+            project(1, mh, None)
         out_rows = out.rearrange("(n p) m -> p n m", p=P)
         for mh, first, count in ((0, 0, 2), (0, 2, 2), (1, 0, 2), (1, 2, 1), (1, 3, 1)):
             res = shift_sb[:, first : first + count, quarters[mh]]

@@ -1,6 +1,7 @@
 from contextlib import ExitStack
 
 import concourse.mybir as mybir
+from concourse.masks import make_identity
 
 F32 = mybir.dt.float32
 BF16 = mybir.dt.bfloat16
@@ -50,16 +51,19 @@ def tile_list_query_slot_cache_kernel(
         idx2 = lists.tile([P, S // 16], U16, name="idx2")
         idx3 = lists.tile([P, M // 16], U16, name="idx3")
 
-        at_tab0 = room(16 * KIB)
+        at_before_tab0 = room(2 * KIB)
+        at_tab0 = room(16 * KIB + 64)
         at_scales = free[0]
         tab_sc = sbuf("tab_sc", [P, T], U8)
         wf_sc_raw = sbuf("wf_sc_raw", [P, 1024], U8)
         wf_w = sbuf("wf_w", [P, 1024], U16)
         wf_sc = sbuf("wf_sc", [P, 1024], U8)
+        at_wf_raw = free[0]
         wf_raw = sbuf("wf_raw", [P, 1024], U16)
         at_tab1 = room(16 * KIB)
-        at_wb = [room(8 * KIB) for b in range(2)]
-        at_w2 = [room(8 * KIB) for b in range(4)]
+        at_before_wb = room(2 * KIB)
+        at_wb = [room(8 * KIB + 64) for b in range(2)]
+        at_w2 = [room(8 * KIB + 64) for b in range(4)]
 
         def load_tab(a, at):
             tile = sbuf("tab%d" % a, [P, T], I32, at)
@@ -67,22 +71,34 @@ def tile_list_query_slot_cache_kernel(
             return tile
 
         def load_weight(name, rows, at):
-            tile = sbuf(name, [P, 4, HALF], F32, at)
+            tile = sbuf(name, [P, 4, rows.shape[1]], F32, at)
             nc.sync.dma_start(tile[:], rows.rearrange("(p i) c -> p i c", i=4))
             return tile
 
-        page_rows = page0.rearrange("(a p t) c -> a t p c", a=2, t=4)
-        wgs_rows = wgs.rearrange("(q t) j -> q t j", t=4)
         pages = {}
 
         def load_page(k, at=None):
             pages[k] = sbuf("page%d" % k, [P, T2], F32, at)
-            nc.sync.dma_start(pages[k][:], page_rows[k // 4, k % 4])
+            rows = page0[P * k : P * (k + 1), :] if k < 4 else page0[HALF:, :].rearrange("(p t) c -> t p c", t=4)[k - 4]
+            nc.sync.dma_start(pages[k][:], rows)
 
-        def load_wgs(name, ts, cols, at=None):
+        w2_raw = {}
+
+        def load_w2(c):
+            for b in range(2):
+                rows = w2[HALF * b : HALF * (b + 1), QUARTER * c : QUARTER * (c + 1)]
+                w2_raw[c, b] = load_weight("w2_raw%d%d" % (c, b), rows, at_w2[c] + 4 * KIB * b)
+
+        def load_dealt(name, ts, jh, at=None):
             tile = sbuf(name, [P, ts.stop - ts.start, HALF], F32, at)
+            rows = wgs.rearrange("(q t) j -> q t j", t=4)[:, ts, HALF * jh : HALF * (jh + 1)]
             for q in (0, 2, 1, 3):
-                nc.sync.dma_start(tile[32 * q : 32 * q + 32, :, :], wgs_rows[:, ts, cols])
+                nc.sync.dma_start(tile[32 * q : 32 * q + 32, :, :], rows)
+            return tile
+
+        def load_wgs(jh, at=None):
+            tile = sbuf("wgs%d" % jh, [P, HALF], F32, at)
+            nc.sync.dma_start(tile[:], wgs[:, HALF * jh : HALF * (jh + 1)])
             return tile
 
         nc.sync.dma_start(idx[:], offs)
@@ -105,20 +121,19 @@ def tile_list_query_slot_cache_kernel(
             wf_w[:].rearrange("p (b t m) -> p b t m", b=2, t=4),
             wf_raw[:].rearrange("p (b m t) -> p b t m", b=2, t=4),
         )
-        w2_raw = {}
-        for b in range(2):
-            w2_raw[0, b] = load_weight("w2_raw0%d" % b, w2[HALF * b : HALF * (b + 1), 0:HALF], at_w2[b])
-        wgs_00 = load_wgs("wgs_00", slice(0, 1), slice(0, HALF))
+        load_w2(0)
+        wgs0 = load_wgs(0)
         load_page(0)
-        wgs_0r = load_wgs("wgs_0r", slice(1, 4), slice(0, HALF))
-        wgs0 = [wgs_00[:, 0, :]] + [wgs_0r[:, t, :] for t in range(3)]
-        for k in range(1, 3):
-            load_page(k)
-        for b in range(2):
-            w2_raw[1, b] = load_weight("w2_raw1%d" % b, w2[HALF * b : HALF * (b + 1), HALF:], at_w2[2 + b])
+        load_w2(1)
+        load_page(1)
+        load_page(2)
+        w2_late = [load_weight("w2_late%d" % b, w2[HALF * b : HALF * (b + 1), HALF:], at_w2[2 + b]) for b in range(2)]
         load_page(3)
-        bias_sb = sbuf("bias_sb", [P, 2, 4], F32)
-        nc.sync.dma_start(bias_sb[:], bias.rearrange("(a p t) -> p a t", a=2, t=4))
+        dealt0 = [load_dealt("dealt00", slice(0, 1), 0)]
+        load_page(4)
+        dealt0.append(load_dealt("dealt01", slice(1, 2), 0))
+        ident = sbuf("ident", [P, P], F32, at_wf_raw)
+        make_identity(nc, ident[:])
 
         v0 = sbuf("v0", [P, S], U32)
         nc.vector.tensor_copy(v0[:], tab[0][:].bitcast(U32).indirect(idx[:]))
@@ -160,9 +175,9 @@ def tile_list_query_slot_cache_kernel(
 
         at_planes = [room(4 * KIB) for b in range(2)]
         at_before_h = room(KIB)
-        at_h = [room(2 * KIB) for k in range(7)]
-        e_w = {(b, 0): sbuf("e_w%d" % b, [P, HALF], U32)[:] for b in range(2)}
-        e_sc = {(b, 0): sbuf("e_sc%d" % b, [P, HALF], U8)[:] for b in range(2)}
+        at_h = [room(2 * KIB) for k in range(5)]
+        e_w = [sbuf("e_w%d" % b, [P, HALF], U32) for b in range(2)]
+        e_sc = [sbuf("e_sc%d" % b, [P, HALF], U8) for b in range(2)]
 
         def y_first(b, jq):
             return banks[4 * b + jq][:].rearrange("p (t j) -> p t j", t=4)
@@ -189,6 +204,7 @@ def tile_list_query_slot_cache_kernel(
         nc.vector.tensor_copy(wb_grouped[1][:].rearrange("p t m i -> p m i t"), wb_raw[1][:].rearrange("p i (m t) -> p m i t", t=4))
         quantise_wb(1)
 
+        at_e_bf = free[0]
         e_bf = [sbuf("e_bf%d" % b, [P, HALF, 4], BF16) for b in range(2)]
 
         def e_first(b, jp):
@@ -203,33 +219,41 @@ def tile_list_query_slot_cache_kernel(
                 e_bf[b][:, cols, :], acts[b, jp][:].rearrange("p (j t) -> p j t", t=4),
                 gain_sb[:, b : b + 1, :].to_broadcast([P, QUARTER, 4]), MULT,
             )
-            nc.vector.quantize_mx(e_w[b, 0][:, cols].bitcast(FP8X4), e_sc[b, 0][:, cols], e_bf[b][:, cols, :].rearrange("p j t -> p (j t)"))
+            nc.vector.quantize_mx(e_w[b][:, cols].bitcast(FP8X4), e_sc[b][:, cols], e_bf[b][:, cols, :].rearrange("p j t -> p (j t)"))
 
         w2_q = {}
 
-        def quantise_w2(a, tp, staging, at, pieces):
+        def quantise_w2(c, staging, at, pieces):
             grouped = staging[:].bitcast(BF16)
-            codes = sbuf("w2%d%d_w" % (a, tp), [P, HALF], U32, at)
-            scales = sbuf("w2%d%d_sc" % (a, tp), [P, HALF], U8)
+            codes = sbuf("w2%d_w" % c, [P, HALF], U32, at)
+            scales = sbuf("w2%d_sc" % c, [P, HALF], U8)
             for b in range(2):
-                nc.scalar.copy(
-                    grouped[:, S * b : S * (b + 1)].rearrange("p (t m i) -> p m i t", t=2, i=4),
-                    w2_raw[a, b][:].rearrange("p i (m t) -> p m i t", t=4)[:, :, :, 2 * tp : 2 * tp + 2],
-                )
+                if c < 2:
+                    nc.scalar.copy(
+                        grouped[:, S * b : S * (b + 1)].rearrange("p (c x i) -> p c i x", x=4, i=4),
+                        w2_raw[c, b][:].rearrange("p i (c x) -> p c i x", x=4),
+                    )
+                else:
+                    nc.scalar.copy(
+                        grouped[:, S * b : S * (b + 1)].rearrange("p (t m i) -> p m i t", t=2, i=4),
+                        w2_late[b][:].rearrange("p i (m t) -> p m i t", t=4)[:, :, :, 2 * c - 4 : 2 * c - 2],
+                    )
             width = HALF // pieces
             for n in range(pieces):
                 cols = slice(width * n, width * (n + 1))
                 nc.vector.quantize_mx(codes[:, cols].bitcast(FP8X4), scales[:, cols], grouped[:, 4 * cols.start : 4 * cols.stop])
-            w2_q[a, tp] = (codes, scales)
+            w2_q[c] = (codes, scales)
 
-        def encode(k, jh, cols, bank, h):
-            a, t = divmod(k, 4)
+        def product(k, part, acc):
             for b in range(2):
-                codes, scales = stationary(w2_q[a, t // 2], 2 * b + t % 2)
+                codes, scales = stationary(w2_q[k // 2], 2 * b + k % 2)
                 nc.tensor.matmul_mx(
-                    bank[:, cols], lhsT=codes, lhsT_scale=scales, rhs=e_w[b, jh][:, cols].bitcast(FP8X4), rhs_scale=e_sc[b, jh][:, cols],
+                    acc, lhsT=codes, lhsT_scale=scales, rhs=part[b][0].bitcast(FP8X4), rhs_scale=part[b][1],
                     start=(b == 0), stop=(b == 1),
                 )
+
+        def encode(k, cols, bank, h):
+            product(k, [(e_w[b][:, cols], e_sc[b][:, cols]) for b in range(2)], bank[:, cols])
             nc.scalar.copy(h, bank[:, cols])
 
         def write_slots(k, jh, cols, h, weight):
@@ -242,106 +266,191 @@ def tile_list_query_slot_cache_kernel(
         woven_both = sbuf("woven", [P, S, 4], BF16)
         woven = [woven_both[:, HALF * b : HALF * (b + 1), :] for b in range(2)]
 
-        def first_round(k):
-            h = sbuf("h_first%d" % k, [P, HALF], F32, at_h[k])[:] if k < 7 else planes[1][:, 0:HALF]
-            encode(k, 0, whole, banks[k], h)
-            write_slots(k, 0, whole, h, wgs0[k % 4])
+        def first_round(k, at):
+            h = sbuf("h_first%d" % k, [P, HALF], F32, at)[:]
+            encode(k, whole, banks[k], h)
+            write_slots(k, 0, whole, h, wgs0 if k < 4 else dealt0[k - 4][:, 0, :])
 
         e_first(0, 0)
         e_first(1, 0)
-        quantise_w2(0, 0, wb_grouped[0][:].rearrange("p t m i -> p (t m i)").bitcast(F32), None, 2)
+        quantise_w2(0, wb_grouped[0][:].rearrange("p t m i -> p (t m i)").bitcast(F32), None, 2)
         h_quarter = [sbuf("h_quarter%d" % u, [P, QUARTER], F32, at_h[0] + KIB * u)[:] for u in range(2)]
-        encode(0, 0, quarters[0], banks[0], h_quarter[0])
+        encode(0, quarters[0], banks[0], h_quarter[0])
         e_first(0, 1)
         e_first(1, 1)
-        write_slots(0, 0, quarters[0], h_quarter[0], wgs0[0])
-        encode(0, 0, quarters[1], banks[4], h_quarter[1])
-        write_slots(0, 0, quarters[1], h_quarter[1], wgs0[0])
+        write_slots(0, 0, quarters[0], h_quarter[0], wgs0)
+        encode(0, quarters[1], banks[4], h_quarter[1])
+        write_slots(0, 0, quarters[1], h_quarter[1], wgs0)
 
-        def second_plane(b, t, bank, act):
-            acc = banks[bank]
-            wf_pass(acc[:], b, t, HALF, HALF, True)
-            wb_pass(acc[:], b, t, HALF, HALF, True)
-            nc.scalar.activation(act, acc[:], ACT.Silu)
-            plane = planes[b][:].bitcast(BF16)[:, HALF * t : HALF * (t + 1)]
-            nc.scalar.activation(plane, act, ACT.Copy, scale=gain_sb[:, b, t : t + 1])
+        def second_planes(u, b, tp, bank, act):
+            j0 = HALF + QUARTER * u
+            for n in range(2):
+                for jq in range(2):
+                    wf_pass(bank[:, QUARTER * n + P * jq : QUARTER * n + P * (jq + 1)], b, 2 * tp + n, j0 + P * jq, P, n + jq == 0)
+            for n in range(2):
+                wb_pass(bank[:, quarters[n]], b, 2 * tp + n, j0, QUARTER, n == 1)
+            nc.scalar.activation(act, bank[:], ACT.Silu)
+            for n in range(2):
+                t = 2 * tp + n
+                plane = planes[b][:].bitcast(BF16)[:, S * u + QUARTER * t : S * u + QUARTER * (t + 1)]
+                nc.scalar.activation(plane, act[:, quarters[n]], ACT.Copy, scale=gain_sb[:, b, t : t + 1])
 
-        def second_weave(b):
-            source = planes[b][:].bitcast(BF16).rearrange("p (t c i) -> p c t i", t=4, i=4)
-            target = woven[b].rearrange("p (c i) t -> p c t i", i=4)
-            for u in range(2):
-                nc.scalar.copy(target[:, 64 * u : 64 * (u + 1)], source[:, 64 * u : 64 * (u + 1)])
+        def second_e(u, b, first_bank, act_tiles):
+            for tp in range(2):
+                second_planes(u, b, tp, banks[first_bank + tp], act_tiles[tp])
+            nc.scalar.copy(
+                woven[u][:, quarters[b], :].rearrange("p (c i) t -> p c t i", i=4),
+                planes[b][:].bitcast(BF16)[:, S * u : S * (u + 1)].rearrange("p (t c i) -> p c t i", t=4, i=4),
+            )
 
-        def second_quantise():
-            codes = sbuf("e_w_second", [P, S], U32, at_h[5])
-            scales = sbuf("e_sc_second", [P, S], U8)
-            nc.vector.quantize_mx(codes[:].bitcast(FP8X4), scales[:], woven_both[:].rearrange("p j t -> p (j t)"))
-            for b in range(2):
-                e_w[b, 1] = codes[:, HALF * b : HALF * (b + 1)]
-                e_sc[b, 1] = scales[:, HALF * b : HALF * (b + 1)]
+        def second_quantise(u, at):
+            codes = sbuf("e_w_second%d" % u, [P, HALF], U32, at)
+            scales = sbuf("e_sc_second%d" % u, [P, HALF], U8)
+            nc.vector.quantize_mx(codes[:].bitcast(FP8X4), scales[:], woven[u].rearrange("p j t -> p (j t)"))
+            return [(codes[:, quarters[b]], scales[:, quarters[b]]) for b in range(2)]
 
-        load_page(4, at_tab0)
-        load_page(5, at_tab0 + 8 * KIB)
-        load_page(6, at_wb[0])
-        load_page(7, at_wb[1])
+        load_page(5, at_tab0 + 64)
+        dealt0.append(load_dealt("dealt02", slice(2, 3), 0, at_before_tab0 + 64))
+        load_page(6, at_tab0 + 8 * KIB + 64)
+        dealt0.append(load_dealt("dealt03", slice(3, 4), 0, at_before_wb + 64))
+        load_page(7, at_wb[0] + 64)
+        wgs1 = load_wgs(1, at_wb[1])
+        bias_sb = sbuf("bias_sb", [P, 4], F32, at_wb[1] + 2 * KIB)
+        with nc.allow_non_contiguous_dma(reason="one value a partition for each page tile"):
+            nc.sync.dma_start(bias_sb[:], bias[0:HALF].rearrange("(k p) -> p k", p=P))
+        bias_dealt = sbuf("bias_dealt", [P, 4], F32, at_wb[1] + 3 * KIB)
+        nc.sync.dma_start(bias_dealt[:], bias[HALF:].rearrange("(p t) -> p t", t=4))
 
-        first_round(1)
-        quantise_w2(0, 1, acts[1, 1], at_before_h, 1)
-        wgs1 = load_wgs("wgs1", slice(0, 4), slice(HALF, S), at_w2[0])
-        early_acts = [acts[1, 0][:, HALF * u : HALF * (u + 1)] for u in range(2)]
-        second_plane(0, 0, 4, early_acts[0])
-        second_plane(0, 1, 1, early_acts[1])
-        second_plane(0, 2, 4, early_acts[0])
-        first_round(2)
-        quantise_w2(1, 0, acts[0, 0], None, 1)
-        first_round(3)
-        quantise_w2(1, 1, acts[0, 1], at_h[2], 1)
-        late_acts = [sbuf("late_act%d" % n, [P, HALF], F32, at_w2[3] + 2 * KIB * n)[:] for n in range(2)]
-        second_plane(0, 3, 1, late_acts[0])
-        second_weave(0)
-        first_round(4)
-        first_round(5)
-        second_plane(1, 0, 2, late_acts[1])
-        first_round(6)
-        second_plane(1, 1, 3, late_acts[0])
-        second_plane(1, 2, 0, late_acts[1])
-        second_plane(1, 3, 1, late_acts[0])
-        second_weave(1)
-        second_quantise()
-        first_round(7)
+        def behind_cast(c, n):
+            return at_w2[c] + (2 + 2 * n) * KIB + 64
 
-        w3_w = []
-        for a in range(2):
-            w3_w.append(sbuf("w3_w%d" % a, [P, 512], I32, at_w2[3] + (4 + 2 * a) * KIB))
+        def acts_behind_cast(c):
+            return [sbuf("act_c%d%d" % (c, n), [P, HALF], F32, behind_cast(c, 2 * n))[:] for n in range(2)]
+
+        quantise_w2(1, acts[1, 1], at_before_h, 1)
+        first_round(1, behind_cast(1, 1))
+        first_round(2, at_h[1])
+        second_e(0, 0, 6, acts_behind_cast(1))
+        first_round(3, at_h[2])
+        quantise_w2(2, acts[0, 0], None, 1)
+        first_round(4, at_h[1])
+        quantise_w2(3, acts[0, 0], None, 1)
+        first_round(5, behind_cast(3, 1))
+        late = acts_behind_cast(3)
+        second_e(0, 1, 0, late)
+        e_third = second_quantise(0, behind_cast(3, 1))
+        first_round(6, at_h[3])
+        first_round(7, at_h[4])
+        second_e(1, 0, 2, late)
+
+        h_third = []
+        for first, count, at in ((0, 1, at_h[2]), (1, 1, at_h[0] + KIB), (2, 2, at_h[1])):
+            h = sbuf("h_third%d" % first, [P, count, QUARTER], F32, at)
+            for u in range(count):
+                product(first + u, e_third, banks[first % 2][:, quarters[u]])
+            nc.scalar.copy(h[:].rearrange("p u j -> p (u j)"), banks[first % 2][:, 0 : QUARTER * count])
+            h_third = h_third + [h[:, u, :] for u in range(count)]
+        second_e(1, 1, 4, late)
+        for k in range(2):
+            write_slots(k, 1, quarters[0], h_third[k], wgs1)
+        e_fourth = second_quantise(1, at_h[2])
+        for k in range(2, 4):
+            write_slots(k, 1, quarters[0], h_third[k], wgs1)
+
+        w3_w = {}
+
+        def load_w3(a, at):
+            w3_w[a] = sbuf("w3_w%d" % a, [P, 512], I32, at)
             nc.sync.dma_start(w3_w[a][:], w3_words[a].rearrange("p c i -> p (c i)").bitcast(I32))
-        w3_sc = sbuf("w3_sc", [P, 512], U8, at_w2[1])
+
+        load_w3(1, at_wb[1] + 4 * KIB)
+        w3_sc = sbuf("w3_sc", [P, 512], U8, at_wf_raw + KIB)
         nc.gpsimd.memset(w3_sc[:].bitcast(I32), 0)
         for q in range(4):
             nc.sync.dma_start(w3_sc[32 * q : 32 * q + 8, :].bitcast(I32), w3_scales[:, 4 * q : 4 * q + 4, :].bitcast(I32))
+        dealt1 = load_dealt("dealt1", slice(0, 4), 1, at_w2[0])
         shift_sb = sbuf("shift_sb", [P, 4, M], F32, at_w2[2])
         nc.sync.dma_start(shift_sb[:], shift.rearrange("(n p) m -> p n m", p=P))
 
         h_second = [acts[0, jp][:, HALF * u : HALF * (u + 1)] for jp in range(2) for u in range(2)]
         h_second = h_second + [e_bf[b][:].rearrange("p j t -> p (j t)").bitcast(F32)[:, HALF * u : HALF * (u + 1)] for b in range(2) for u in range(2)]
-        for k in range(8):
-            encode(k, 1, whole, banks[k % 4], h_second[k])
+
+        for n in range(2):
+            for u in range(2):
+                product(2 * n + u, e_fourth, banks[n][:, quarters[u]])
+            nc.scalar.copy(
+                acts[0, n][:].rearrange("p (u j) -> p u j", u=2)[:, :, quarters[1]],
+                banks[n][:].rearrange("p (u j) -> p u j", u=2),
+            )
+
+        def encode_rest(k, bank):
+            product(k, e_third, bank[:, quarters[0]])
+            product(k, e_fourth, bank[:, quarters[1]])
+            nc.scalar.copy(h_second[k], bank[:])
+
+        for k in range(4, 6):
+            encode_rest(k, banks[k + 2])
 
         z_bf = {(a, mh): woven[a][:, quarters[mh], :] for a in range(2) for mh in range(2)}
 
-        def add_bias(k, mh, x):
-            a, t = divmod(k, 4)
-            nc.scalar.activation(z_bf[a, mh][:, :, t], x, ACT.Identity, bias=bias_sb[:, a, t : t + 1])
+        z_turned = [sbuf("z_turned%d" % a, [P, 4, 2, P, 2], BF16, at_tab1 + 4 * KIB * a) for a in range(1)]
+
+        def add_bias(k, x, blocks, bank):
+            a, kk = divmod(k, 4)
+            count = blocks.stop - blocks.start
+            for n in range(count):
+                nc.tensor.matmul(
+                    bank[:, P * n : P * (n + 1)], lhsT=bias_sb[:, k : k + 1].to_broadcast([P, P]), rhs=ident[:],
+                    is_transpose=True, start=(n == 0), stop=False,
+                )
+            for n in range(count):
+                mb = blocks.start + n
+                nc.tensor.matmul(
+                    bank[:, P * n : P * (n + 1)], lhsT=x[:, P * mb : P * (mb + 1)], rhs=ident[:],
+                    is_transpose=True, start=False, stop=(n == count - 1),
+                )
+            nc.scalar.copy(
+                z_turned[a][:, blocks, :, 32 * kk : 32 * (kk + 1), :],
+                bank[:, 0 : P * count].rearrange("p (n q u e) -> p n u q e", q=32, u=2, e=2),
+            )
+
+        def turn_back(a, mh):
+            bank = banks[2 + mh]
+            words = z_turned[a][:].rearrange("p n u q e -> p (n u q e)").bitcast(F32)
+            for n in range(4):
+                cols = slice(P * (4 * mh + n), P * (4 * mh + n + 1))
+                nc.tensor.transpose(bank[:, P * n : P * (n + 1)], words[:, cols], ident[:])
+            nc.scalar.copy(
+                z_bf[a, mh].rearrange("p m t -> p (m t)").bitcast(F32).rearrange("p (n m u) -> p n m u", n=2, u=2),
+                bank[:].rearrange("p (n u m) -> p n m u", n=2, u=2),
+            )
+
+        def add_dealt(k, mh, x):
+            nc.scalar.activation(z_bf[1, mh][:, :, k - 4], x, ACT.Identity, bias=bias_dealt[:, k - 4 : k - 3])
 
         def read_slots(k):
-            x = h_second[k]
+            x = sbuf("x%d" % k, [P, M], F32, at_tab1 + 2 * KIB * (k - 4))[:] if k in (4, 5) else h_second[k]
             nc.vector.tensor_copy(x, pages[k][:].indirect(idx3[:]))
-            for mh in range(2):
-                add_bias(k, mh, x[:, quarters[mh]])
+            if k < 4:
+                add_bias(k, x, slice(0, 4), banks[k % 2])
+            else:
+                for mh in range(2):
+                    add_dealt(k, mh, x[:, quarters[mh]])
+            if k == 3:
+                for mh in range(2):
+                    turn_back(0, mh)
+                    encode_rest(6 + mh, banks[2 + mh])
 
-        def project(a, mh, at):
+        z_q = {}
+
+        def quantise_z(a, mh, at):
             codes = sbuf("z_w%d%d" % (a, mh), [P, QUARTER], U32, at)
             scales = sbuf("z_sc%d%d" % (a, mh), [P, QUARTER], U8)
             nc.vector.quantize_mx(codes[:].bitcast(FP8X4), scales[:], z_bf[a, mh].rearrange("p m t -> p (m t)"))
+            z_q[a, mh] = (codes, scales)
+
+        def project(a, mh):
+            codes, scales = z_q[a, mh]
             for n in range(4):
                 cols = slice(P * n, P * (n + 1))
                 nc.tensor.matmul_mx(
@@ -350,21 +459,29 @@ def tile_list_query_slot_cache_kernel(
                     start=(a == 0 and n % 2 == 0), stop=(a == 1 and n % 2 == 1),
                 )
 
-        write_slots(0, 1, whole, h_second[0], wgs1[:, 0, :])
+        write_slots(0, 1, quarters[1], h_second[0][:, quarters[1]], wgs1)
         for k in range(1, 7):
-            write_slots(k, 1, whole, h_second[k], wgs1[:, k % 4, :])
+            if k < 4:
+                write_slots(k, 1, quarters[1], h_second[k][:, quarters[1]], wgs1)
+            else:
+                write_slots(k, 1, whole, h_second[k], dealt1[:, k - 4, :])
             read_slots(k - 1)
             if k == 5:
-                project(0, 0, None)
+                quantise_z(0, 0, at_e_bf)
+            if k == 6:
+                quantise_z(0, 1, at_e_bf + KIB)
         read_slots(6)
-        write_slots(7, 1, whole, h_second[7], wgs1[:, 3, :])
-        project(0, 1, at_w2[0])
+        load_w3(0, at_tab0 + 8 * KIB + 64)
+        for mh in range(2):
+            project(0, mh)
+        write_slots(7, 1, whole, h_second[7], dealt1[:, 3, :])
         for mh in range(2):
             x = h_second[7][:, quarters[mh]]
             nc.vector.tensor_copy(x, pages[7][:].indirect(idx3[:, 16 * mh : 16 * mh + 16]))
-            add_bias(7, mh, x)
+            add_dealt(7, mh, x)
         for mh in range(2):
-            project(1, mh, None)
+            quantise_z(1, mh, None)
+            project(1, mh)
         out_rows = out.rearrange("(n p) m -> p n m", p=P)
         for mh, first, count in ((0, 0, 2), (0, 2, 2), (1, 0, 2), (1, 2, 1), (1, 3, 1)):
             res = shift_sb[:, first : first + count, quarters[mh]]

@@ -58,6 +58,7 @@ def tile_list_query_slot_cache_kernel(
         wf_sc_raw = sbuf("wf_sc_raw", [P, 1024], U8)
         wf_w = sbuf("wf_w", [P, 1024], U16)
         wf_sc = sbuf("wf_sc", [P, 1024], U8)
+        wf_sc_rows = sbuf("wf_sc_rows", [P, 256], I32)
         at_wf_raw = free[0]
         wf_raw = sbuf("wf_raw", [P, 1024], U16)
         at_tab1 = room(16 * KIB)
@@ -116,7 +117,9 @@ def tile_list_query_slot_cache_kernel(
         for q in range(4):
             nc.gpsimd.dma_start(tab_sc[32 * q : 32 * q + 8, :].bitcast(I32), tab_scales[:, 4 * q : 4 * q + 4, :].bitcast(I32))
         for q in range(4):
-            nc.gpsimd.dma_start(wf_sc_raw[32 * q : 32 * q + 4, :].bitcast(I32), wf_scales[0, 4 * q : 4 * q + 4, :].bitcast(I32))
+            rows = slice(32 * q, 32 * q + 4)
+            nc.scalar.dma_start(wf_sc_rows[rows, :], wf_scales[0, 4 * q : 4 * q + 4, :].bitcast(I32))
+            nc.vector.tensor_copy(wf_sc_raw[rows, :].bitcast(I32), wf_sc_rows[rows, :])
         nc.vector.tensor_copy(
             wf_w[:].rearrange("p (b t m) -> p b t m", b=2, t=4),
             wf_raw[:].rearrange("p (b m t) -> p b t m", b=2, t=4),

@@ -20,6 +20,7 @@ T, S, T2, M = 4096, 1024, 2048, 512
 HALF = 512
 QUARTER = 256
 KIB = 1024
+LAP = 64
 FLOPS = 4831838208
 
 
@@ -52,7 +53,7 @@ def tile_list_query_slot_cache_kernel(
         idx3 = lists.tile([P, M // 16], U16, name="idx3")
 
         at_before_tab0 = room(2 * KIB)
-        at_tab0 = room(16 * KIB + 64)
+        at_tab0 = room(16 * KIB + LAP)
         at_scales = free[0]
         tab_sc = sbuf("tab_sc", [P, T], U8)
         wf_sc_raw = sbuf("wf_sc_raw", [P, 1024], U8)
@@ -63,8 +64,8 @@ def tile_list_query_slot_cache_kernel(
         wf_raw = sbuf("wf_raw", [P, 1024], U16)
         at_tab1 = room(16 * KIB)
         at_before_wb = room(2 * KIB)
-        at_wb = [room(8 * KIB + 64) for b in range(2)]
-        at_w2 = [room(8 * KIB + 64) for b in range(4)]
+        at_wb = [room(8 * KIB + LAP) for b in range(2)]
+        at_w2 = [room(8 * KIB + LAP) for n in range(4)]
 
         def load_tab(a, at):
             tile = sbuf("tab%d" % a, [P, T], I32, at)
@@ -97,9 +98,9 @@ def tile_list_query_slot_cache_kernel(
                 nc.sync.dma_start(tile[32 * q : 32 * q + 32, :, :], rows)
             return tile
 
-        def load_wgs(jh, at=None):
-            tile = sbuf("wgs%d" % jh, [P, HALF], F32, at)
-            nc.sync.dma_start(tile[:], wgs[:, HALF * jh : HALF * (jh + 1)])
+        def load_wgs(first, count, at=None):
+            tile = sbuf("wgs%d" % first, [P, count], F32, at)
+            nc.sync.dma_start(tile[:], wgs[:, first : first + count])
             return tile
 
         nc.sync.dma_start(idx[:], offs)
@@ -125,13 +126,14 @@ def tile_list_query_slot_cache_kernel(
             wf_raw[:].rearrange("p (b m t) -> p b t m", b=2, t=4),
         )
         load_w2(0)
-        wgs0 = load_wgs(0)
+        wgs0 = load_wgs(0, HALF)
         load_page(0)
         load_w2(1)
         load_page(1)
         load_page(2)
-        w2_late = [load_weight("w2_late%d" % b, w2[HALF * b : HALF * (b + 1), HALF:], at_w2[2 + b]) for b in range(2)]
         load_page(3)
+        wgs_third = load_wgs(HALF, QUARTER)
+        w2_dealt = [load_weight("w2_dealt%d" % b, w2[HALF * b : HALF * (b + 1), HALF:], at_w2[2 + b]) for b in range(2)]
         dealt0 = [load_dealt("dealt00", slice(0, 1), 0)]
         load_page(4)
         dealt0.append(load_dealt("dealt01", slice(1, 2), 0))
@@ -141,7 +143,8 @@ def tile_list_query_slot_cache_kernel(
         v0 = sbuf("v0", [P, S], U32)
         nc.vector.tensor_copy(v0[:], tab[0][:].bitcast(U32).indirect(idx[:]))
         v_sc = sbuf("v_sc", [P, S], U8)
-        nc.vector.tensor_copy(v_sc[:], tab_sc[:].indirect(idx[:]))
+        for jh in range(2):
+            nc.vector.tensor_copy(v_sc[:, HALF * jh : HALF * (jh + 1)], tab_sc[:].indirect(idx[:, 32 * jh : 32 * jh + 32]))
         nc.vector.tensor_copy(
             wf_sc[:].rearrange("p (b t m) -> p b t m", b=2, t=4),
             wf_sc_raw[:].rearrange("p (b m t) -> p b t m", b=2, t=4),
@@ -160,25 +163,24 @@ def tile_list_query_slot_cache_kernel(
             cols = slice(P * c, P * (c + 1))
             return codes[:, cols].bitcast(FP8X4), scales[:, cols]
 
-        def wf_pass(acc, b, t, j0, n, start):
+        def wf_pass(acc, b, t, j0, n, start, stop):
             c = 4 * b + t
             nc.tensor.matmul_mx(
                 acc, lhsT=wf_w[:, P * c : P * (c + 1)].bitcast(FP4X4), lhsT_scale=wf_sc[:, P * c : P * (c + 1)],
-                rhs=v0[:, j0 : j0 + n].bitcast(FP8X4), rhs_scale=v_sc[:, j0 : j0 + n], start=start, stop=False,
+                rhs=v0[:, j0 : j0 + n].bitcast(FP8X4), rhs_scale=v_sc[:, j0 : j0 + n], start=start, stop=stop,
             )
 
         wb_q = {}
 
-        def wb_pass(acc, b, t, j0, n, stop):
+        def wb_pass(acc, b, t, j0, n, start, stop):
             codes, scales = stationary(wb_q[b], t)
             nc.tensor.matmul_mx(
                 acc, lhsT=codes, lhsT_scale=scales,
-                rhs=v1[j0 // HALF][:, j0 % HALF : j0 % HALF + n].bitcast(FP8X4), rhs_scale=v_sc[4:P, j0 : j0 + n], start=False, stop=stop,
+                rhs=v1[j0 // HALF][:, j0 % HALF : j0 % HALF + n].bitcast(FP8X4), rhs_scale=v_sc[4:P, j0 : j0 + n], start=start, stop=stop,
             )
 
-        at_planes = [room(4 * KIB) for b in range(2)]
         at_before_h = room(KIB)
-        at_h = [room(2 * KIB) for k in range(5)]
+        at_h = [room(2 * KIB) for n in range(5)]
         e_w = [sbuf("e_w%d" % b, [P, HALF], U32) for b in range(2)]
         e_sc = [sbuf("e_sc%d" % b, [P, HALF], U8) for b in range(2)]
 
@@ -186,9 +188,9 @@ def tile_list_query_slot_cache_kernel(
             return banks[4 * b + jq][:].rearrange("p (t j) -> p t j", t=4)
 
         for b in range(2):
-            for jq in range(4):
+            for jq in range(2):
                 for t in range(4):
-                    wf_pass(y_first(b, jq)[:, t, :], b, t, P * jq, P, t == 0)
+                    wf_pass(y_first(b, jq)[:, t, :], b, t, P * jq, P, t == 0, False)
 
         def quantise_wb(b):
             codes = sbuf("wb%d_w" % b, [P, HALF], U32)
@@ -211,10 +213,14 @@ def tile_list_query_slot_cache_kernel(
         e_bf = [sbuf("e_bf%d" % b, [P, HALF, 4], BF16) for b in range(2)]
 
         def e_first(b, jp):
+            opened = jp == 0
             for u in range(2):
                 jq = 2 * jp + u
                 for t in range(4):
-                    wb_pass(y_first(b, jq)[:, t, :], b, t, P * jq, P, t == 3)
+                    wb_pass(y_first(b, jq)[:, t, :], b, t, P * jq, P, t == 0 and not opened, t == 3 and opened)
+                if not opened:
+                    for t in range(4):
+                        wf_pass(y_first(b, jq)[:, t, :], b, t, P * jq, P, False, t == 3)
                 act = acts[b, jp][:, HALF * u : HALF * (u + 1)].rearrange("p (j t) -> p j t", t=4)
                 nc.scalar.activation(act, y_first(b, jq).rearrange("p t j -> p j t"), ACT.Silu)
             cols = slice(QUARTER * jp, QUARTER * (jp + 1))
@@ -226,30 +232,20 @@ def tile_list_query_slot_cache_kernel(
 
         w2_q = {}
 
-        def quantise_w2(c, staging, at, pieces):
-            grouped = staging[:].bitcast(BF16)
+        def quantise_w2(c, grouped, at):
             codes = sbuf("w2%d_w" % c, [P, HALF], U32, at)
             scales = sbuf("w2%d_sc" % c, [P, HALF], U8)
             for b in range(2):
-                if c < 2:
-                    nc.scalar.copy(
-                        grouped[:, S * b : S * (b + 1)].rearrange("p (c x i) -> p c i x", x=4, i=4),
-                        w2_raw[c, b][:].rearrange("p i (c x) -> p c i x", x=4),
-                    )
-                else:
-                    nc.scalar.copy(
-                        grouped[:, S * b : S * (b + 1)].rearrange("p (t m i) -> p m i t", t=2, i=4),
-                        w2_late[b][:].rearrange("p i (m t) -> p m i t", t=4)[:, :, :, 2 * c - 4 : 2 * c - 2],
-                    )
-            width = HALF // pieces
-            for n in range(pieces):
-                cols = slice(width * n, width * (n + 1))
-                nc.vector.quantize_mx(codes[:, cols].bitcast(FP8X4), scales[:, cols], grouped[:, 4 * cols.start : 4 * cols.stop])
+                nc.scalar.copy(
+                    grouped[:, S * b : S * (b + 1)].rearrange("p (c x i) -> p c i x", x=4, i=4),
+                    w2_raw[c, b][:].rearrange("p i (c x) -> p c i x", x=4),
+                )
+            nc.vector.quantize_mx(codes[:].bitcast(FP8X4), scales[:], grouped)
             w2_q[c] = (codes, scales)
 
         def product(k, part, acc):
             for b in range(2):
-                codes, scales = stationary(w2_q[k // 2], 2 * b + k % 2)
+                codes, scales = stationary(w2_q[k // 2], 2 * b + k % 2) if k < 4 else stationary(w2_dealt_q, 4 * b + k - 4)
                 nc.tensor.matmul_mx(
                     acc, lhsT=codes, lhsT_scale=scales, rhs=part[b][0].bitcast(FP8X4), rhs_scale=part[b][1],
                     start=(b == 0), stop=(b == 1),
@@ -261,37 +257,36 @@ def tile_list_query_slot_cache_kernel(
 
         def write_slots(k, jh, cols, h, weight):
             first, last = (HALF * jh + cols.start) // 16, (HALF * jh + cols.stop) // 16
-            nc.vector.tensor_tensor(pages[k][:].indirect(idx2[:, first:last]), h, weight[:, cols], MULT)
+            nc.vector.tensor_tensor(pages[k][:].indirect(idx2[:, first:last]), h, weight, MULT)
 
         whole = slice(0, HALF)
         quarters = [slice(0, QUARTER), slice(QUARTER, HALF)]
-        planes = [sbuf("planes%d" % b, [P, 1024], F32, at_planes[b]) for b in range(2)]
+        planes = [sbuf("planes%d" % b, [P, 1024], F32) for b in range(2)]
         woven_both = sbuf("woven", [P, S, 4], BF16)
-        woven = [woven_both[:, HALF * b : HALF * (b + 1), :] for b in range(2)]
+        woven = [woven_both[:, HALF * u : HALF * (u + 1), :] for u in range(2)]
 
-        def first_round(k, at):
-            h = sbuf("h_first%d" % k, [P, HALF], F32, at)[:]
+        def first_half(k, h):
             encode(k, whole, banks[k], h)
-            write_slots(k, 0, whole, h, wgs0 if k < 4 else dealt0[k - 4][:, 0, :])
+            write_slots(k, 0, whole, h, wgs0[:] if k < 4 else dealt0[k - 4][:, 0, :])
 
         e_first(0, 0)
         e_first(1, 0)
-        quantise_w2(0, wb_grouped[0][:].rearrange("p t m i -> p (t m i)").bitcast(F32), None, 2)
+        quantise_w2(0, wb_grouped[0][:].rearrange("p t m i -> p (t m i)"), None)
         h_quarter = [sbuf("h_quarter%d" % u, [P, QUARTER], F32, at_h[0] + KIB * u)[:] for u in range(2)]
         encode(0, quarters[0], banks[0], h_quarter[0])
         e_first(0, 1)
         e_first(1, 1)
-        write_slots(0, 0, quarters[0], h_quarter[0], wgs0)
+        write_slots(0, 0, quarters[0], h_quarter[0], wgs0[:, quarters[0]])
         encode(0, quarters[1], banks[4], h_quarter[1])
-        write_slots(0, 0, quarters[1], h_quarter[1], wgs0)
+        write_slots(0, 0, quarters[1], h_quarter[1], wgs0[:, quarters[1]])
 
         def second_planes(u, b, tp, bank, act):
             j0 = HALF + QUARTER * u
             for n in range(2):
                 for jq in range(2):
-                    wf_pass(bank[:, QUARTER * n + P * jq : QUARTER * n + P * (jq + 1)], b, 2 * tp + n, j0 + P * jq, P, n + jq == 0)
+                    wf_pass(bank[:, QUARTER * n + P * jq : QUARTER * n + P * (jq + 1)], b, 2 * tp + n, j0 + P * jq, P, n + jq == 0, False)
             for n in range(2):
-                wb_pass(bank[:, quarters[n]], b, 2 * tp + n, j0, QUARTER, n == 1)
+                wb_pass(bank[:, quarters[n]], b, 2 * tp + n, j0, QUARTER, False, n == 1)
             nc.scalar.activation(act, bank[:], ACT.Silu)
             for n in range(2):
                 t = 2 * tp + n
@@ -312,53 +307,65 @@ def tile_list_query_slot_cache_kernel(
             nc.vector.quantize_mx(codes[:].bitcast(FP8X4), scales[:], woven[u].rearrange("p j t -> p (j t)"))
             return [(codes[:, quarters[b]], scales[:, quarters[b]]) for b in range(2)]
 
-        load_page(5, at_tab0 + 64)
-        dealt0.append(load_dealt("dealt02", slice(2, 3), 0, at_before_tab0 + 64))
-        load_page(6, at_tab0 + 8 * KIB + 64)
-        dealt0.append(load_dealt("dealt03", slice(3, 4), 0, at_before_wb + 64))
-        load_page(7, at_wb[0] + 64)
-        wgs1 = load_wgs(1, at_wb[1])
+        load_page(5, at_tab0 + LAP)
+        dealt0.append(load_dealt("dealt02", slice(2, 3), 0, at_before_tab0 + LAP))
+        load_page(6, at_tab0 + 8 * KIB + LAP)
+        dealt0.append(load_dealt("dealt03", slice(3, 4), 0, at_before_wb + LAP))
+        load_page(7, at_wb[0] + LAP)
+        wgs_fourth = load_wgs(HALF + QUARTER, QUARTER, at_wb[1])
         bias_sb = sbuf("bias_sb", [P, 4], F32, at_wb[1] + 2 * KIB)
         with nc.allow_non_contiguous_dma(reason="one value a partition for each page tile"):
             nc.sync.dma_start(bias_sb[:], bias[0:HALF].rearrange("(k p) -> p k", p=P))
         bias_dealt = sbuf("bias_dealt", [P, 4], F32, at_wb[1] + 3 * KIB)
         nc.sync.dma_start(bias_dealt[:], bias[HALF:].rearrange("(p t) -> p t", t=4))
 
-        def behind_cast(c, n):
-            return at_w2[c] + (2 + 2 * n) * KIB + 64
+        def behind_cast(place, n):
+            return at_w2[place] + (2 + 2 * n) * KIB + LAP
 
-        def acts_behind_cast(c):
-            return [sbuf("act_c%d%d" % (c, n), [P, HALF], F32, behind_cast(c, 2 * n))[:] for n in range(2)]
+        def acts_behind_cast(place):
+            return [sbuf("act_c%d%d" % (place, n), [P, HALF], F32, behind_cast(place, 2 * n))[:] for n in range(2)]
 
-        quantise_w2(1, acts[1, 1], at_before_h, 1)
-        first_round(1, behind_cast(1, 1))
-        first_round(2, at_h[1])
-        second_e(0, 0, 6, acts_behind_cast(1))
-        first_round(3, at_h[2])
-        quantise_w2(2, acts[0, 0], None, 1)
-        first_round(4, at_h[1])
-        quantise_w2(3, acts[0, 0], None, 1)
-        first_round(5, behind_cast(3, 1))
-        late = acts_behind_cast(3)
-        second_e(0, 1, 0, late)
-        e_third = second_quantise(0, behind_cast(3, 1))
-        first_round(6, at_h[3])
-        first_round(7, at_h[4])
-        second_e(1, 0, 2, late)
+        def h_tile(name, at):
+            return sbuf(name, [P, HALF], F32, at)[:]
 
-        h_third = []
-        for first, count, at in ((0, 1, at_h[2]), (1, 1, at_h[0] + KIB), (2, 2, at_h[1])):
+        def third_h(first, count, at):
             h = sbuf("h_third%d" % first, [P, count, QUARTER], F32, at)
             for u in range(count):
-                product(first + u, e_third, banks[first % 2][:, quarters[u]])
-            nc.scalar.copy(h[:].rearrange("p u j -> p (u j)"), banks[first % 2][:, 0 : QUARTER * count])
-            h_third = h_third + [h[:, u, :] for u in range(count)]
-        second_e(1, 1, 4, late)
+                product(first + u, e_third, banks[2 + first % 2][:, quarters[u]])
+            nc.scalar.copy(h[:].rearrange("p u j -> p (u j)"), banks[2 + first % 2][:, 0 : QUARTER * count])
+            return [h[:, u, :] for u in range(count)]
+
+        quantise_w2(1, acts[1, 1][:].bitcast(BF16), at_before_h)
+        first_half(1, h_tile("h1", behind_cast(1, 1)))
+        first_half(2, h_tile("h2", at_h[1]))
+        early = acts_behind_cast(1)
+        second_e(0, 0, 6, [acts[1, 0][:, 0:HALF], early[1]])
+        second_e(0, 1, 4, early)
+        e_third = second_quantise(0, None)
+        first_half(3, planes[1][:, 0:HALF])
+        h_third = third_h(0, 1, None) + third_h(1, 1, at_h[0] + KIB)
         for k in range(2):
-            write_slots(k, 1, quarters[0], h_third[k], wgs1)
-        e_fourth = second_quantise(1, at_h[2])
+            write_slots(k, 1, quarters[0], h_third[k], wgs_third[:])
+        grouped = sbuf("w2_dealt_grouped", [P, 2, 4, P, 4], BF16, at_tab1 + 8 * KIB)
+        for b in range(2):
+            for tp in range(2):
+                nc.scalar.copy(
+                    grouped[:, b, 2 * tp : 2 * tp + 2].rearrange("p t m i -> p m i t"),
+                    w2_dealt[b][:].rearrange("p i (m t) -> p m i t", t=4)[:, :, :, 2 * tp : 2 * tp + 2],
+                )
+        w2_dealt_q = (sbuf("w2_dealt_w", [P, S], U32), sbuf("w2_dealt_sc", [P, S], U8))
+        nc.vector.quantize_mx(w2_dealt_q[0][:].bitcast(FP8X4), w2_dealt_q[1][:], grouped[:].rearrange("p b t m i -> p (b t m i)"))
+        h_third = h_third + third_h(2, 2, behind_cast(3, 1))
         for k in range(2, 4):
-            write_slots(k, 1, quarters[0], h_third[k], wgs1)
+            write_slots(k, 1, quarters[0], h_third[k], wgs_third[:])
+        for k in range(4, 6):
+            first_half(k, h_tile("h%d" % k, at_h[k - 3]))
+        late = acts_behind_cast(3)
+        second_e(1, 0, 0, late)
+        second_e(1, 1, 2, late)
+        e_fourth = second_quantise(1, at_h[2])
+        for k in range(6, 8):
+            first_half(k, h_tile("h%d" % k, at_h[k - 3]))
 
         w3_w = {}
 
@@ -375,8 +382,8 @@ def tile_list_query_slot_cache_kernel(
         shift_sb = sbuf("shift_sb", [P, 4, M], F32, at_w2[2])
         nc.sync.dma_start(shift_sb[:], shift.rearrange("(n p) m -> p n m", p=P))
 
-        h_second = [acts[0, jp][:, HALF * u : HALF * (u + 1)] for jp in range(2) for u in range(2)]
-        h_second = h_second + [e_bf[b][:].rearrange("p j t -> p (j t)").bitcast(F32)[:, HALF * u : HALF * (u + 1)] for b in range(2) for u in range(2)]
+        h_last = [acts[0, jp][:, HALF * u : HALF * (u + 1)] for jp in range(2) for u in range(2)]
+        h_last = h_last + [e_bf[b][:].rearrange("p j t -> p (j t)").bitcast(F32)[:, HALF * u : HALF * (u + 1)] for b in range(2) for u in range(2)]
 
         for n in range(2):
             for u in range(2):
@@ -389,102 +396,93 @@ def tile_list_query_slot_cache_kernel(
         def encode_rest(k, bank):
             product(k, e_third, bank[:, quarters[0]])
             product(k, e_fourth, bank[:, quarters[1]])
-            nc.scalar.copy(h_second[k], bank[:])
+            nc.scalar.copy(h_last[k], bank[:])
 
         for k in range(4, 6):
             encode_rest(k, banks[k + 2])
 
         z_bf = {(a, mh): woven[a][:, quarters[mh], :] for a in range(2) for mh in range(2)}
+        z_turned = sbuf("z_turned", [P, 4, 2, P, 2], BF16, at_tab1)
 
-        z_turned = [sbuf("z_turned%d" % a, [P, 4, 2, P, 2], BF16, at_tab1 + 4 * KIB * a) for a in range(1)]
-
-        def add_bias(k, x, blocks, bank):
-            a, kk = divmod(k, 4)
-            count = blocks.stop - blocks.start
-            for n in range(count):
+        def add_bias_plain(k, x, bank):
+            for n in range(4):
                 nc.tensor.matmul(
                     bank[:, P * n : P * (n + 1)], lhsT=bias_sb[:, k : k + 1].to_broadcast([P, P]), rhs=ident[:],
                     is_transpose=True, start=(n == 0), stop=False,
                 )
-            for n in range(count):
-                mb = blocks.start + n
+            for n in range(4):
                 nc.tensor.matmul(
-                    bank[:, P * n : P * (n + 1)], lhsT=x[:, P * mb : P * (mb + 1)], rhs=ident[:],
-                    is_transpose=True, start=False, stop=(n == count - 1),
+                    bank[:, P * n : P * (n + 1)], lhsT=x[:, P * n : P * (n + 1)], rhs=ident[:],
+                    is_transpose=True, start=False, stop=(n == 3),
                 )
             nc.scalar.copy(
-                z_turned[a][:, blocks, :, 32 * kk : 32 * (kk + 1), :],
-                bank[:, 0 : P * count].rearrange("p (n q u e) -> p n u q e", q=32, u=2, e=2),
+                z_turned[:, :, :, 32 * k : 32 * (k + 1), :],
+                bank[:].rearrange("p (n q u e) -> p n u q e", q=32, u=2, e=2),
             )
 
-        def turn_back(a, mh):
+        def turn_back(mh):
             bank = banks[2 + mh]
-            words = z_turned[a][:].rearrange("p n u q e -> p (n u q e)").bitcast(F32)
+            words = z_turned[:].rearrange("p n u q e -> p (n u q e)").bitcast(F32)
             for n in range(4):
                 cols = slice(P * (4 * mh + n), P * (4 * mh + n + 1))
                 nc.tensor.transpose(bank[:, P * n : P * (n + 1)], words[:, cols], ident[:])
             nc.scalar.copy(
-                z_bf[a, mh].rearrange("p m t -> p (m t)").bitcast(F32).rearrange("p (n m u) -> p n m u", n=2, u=2),
+                z_bf[0, mh].rearrange("p m t -> p (m t)").bitcast(F32).rearrange("p (n m u) -> p n m u", n=2, u=2),
                 bank[:].rearrange("p (n u m) -> p n m u", n=2, u=2),
             )
 
-        def add_dealt(k, mh, x):
+        def add_bias_dealt(k, mh, x):
             nc.scalar.activation(z_bf[1, mh][:, :, k - 4], x, ACT.Identity, bias=bias_dealt[:, k - 4 : k - 3])
 
         def read_slots(k):
-            x = sbuf("x%d" % k, [P, M], F32, at_tab1 + 2 * KIB * (k - 4))[:] if k in (4, 5) else h_second[k]
+            x = sbuf("x%d" % k, [P, M], F32, at_tab1 + 2 * KIB * (k - 4))[:] if k in (4, 5) else h_last[k]
             nc.vector.tensor_copy(x, pages[k][:].indirect(idx3[:]))
             if k < 4:
-                add_bias(k, x, slice(0, 4), banks[k % 2])
+                add_bias_plain(k, x, banks[k % 2])
             else:
                 for mh in range(2):
-                    add_dealt(k, mh, x[:, quarters[mh]])
+                    add_bias_dealt(k, mh, x[:, quarters[mh]])
             if k == 3:
                 for mh in range(2):
-                    turn_back(0, mh)
+                    turn_back(mh)
                     encode_rest(6 + mh, banks[2 + mh])
 
-        z_q = {}
+        def quantise_z(name, z, width, at):
+            codes = sbuf(name + "_w", [P, width], U32, at)
+            scales = sbuf(name + "_sc", [P, width], U8)
+            nc.vector.quantize_mx(codes[:].bitcast(FP8X4), scales[:], z.rearrange("p m t -> p (m t)"))
+            return codes, scales
 
-        def quantise_z(a, mh, at):
-            codes = sbuf("z_w%d%d" % (a, mh), [P, QUARTER], U32, at)
-            scales = sbuf("z_sc%d%d" % (a, mh), [P, QUARTER], U8)
-            nc.vector.quantize_mx(codes[:].bitcast(FP8X4), scales[:], z_bf[a, mh].rearrange("p m t -> p (m t)"))
-            z_q[a, mh] = (codes, scales)
-
-        def project(a, mh):
-            codes, scales = z_q[a, mh]
+        def project(a, mh, codes, scales):
             for n in range(4):
                 cols = slice(P * n, P * (n + 1))
                 nc.tensor.matmul_mx(
                     banks[4 + 2 * mh + n // 2][:, quarters[n % 2]], lhsT=w3_w[a][:, cols].bitcast(FP8X4), lhsT_scale=w3_sc[4 * a : P, cols],
-                    rhs=codes[:].bitcast(FP8X4), rhs_scale=scales[:],
+                    rhs=codes.bitcast(FP8X4), rhs_scale=scales,
                     start=(a == 0 and n % 2 == 0), stop=(a == 1 and n % 2 == 1),
                 )
 
-        write_slots(0, 1, quarters[1], h_second[0][:, quarters[1]], wgs1)
+        write_slots(0, 1, quarters[1], h_last[0][:, quarters[1]], wgs_fourth[:])
         for k in range(1, 7):
             if k < 4:
-                write_slots(k, 1, quarters[1], h_second[k][:, quarters[1]], wgs1)
+                write_slots(k, 1, quarters[1], h_last[k][:, quarters[1]], wgs_fourth[:])
             else:
-                write_slots(k, 1, whole, h_second[k], dealt1[:, k - 4, :])
+                write_slots(k, 1, whole, h_last[k], dealt1[:, k - 4, :])
             read_slots(k - 1)
             if k == 5:
-                quantise_z(0, 0, at_e_bf)
-            if k == 6:
-                quantise_z(0, 1, at_e_bf + KIB)
+                z0_codes, z0_scales = quantise_z("z0", woven[0], M, at_e_bf)
         read_slots(6)
-        load_w3(0, at_tab0 + 8 * KIB + 64)
+        load_w3(0, at_tab0 + 8 * KIB + LAP)
         for mh in range(2):
-            project(0, mh)
-        write_slots(7, 1, whole, h_second[7], dealt1[:, 3, :])
+            project(0, mh, z0_codes[:, quarters[mh]], z0_scales[:, quarters[mh]])
+        write_slots(7, 1, whole, h_last[7], dealt1[:, 3, :])
         for mh in range(2):
-            x = h_second[7][:, quarters[mh]]
+            x = h_last[7][:, quarters[mh]]
             nc.vector.tensor_copy(x, pages[7][:].indirect(idx3[:, 16 * mh : 16 * mh + 16]))
-            add_dealt(7, mh, x)
+            add_bias_dealt(7, mh, x)
         for mh in range(2):
-            quantise_z(1, mh, None)
-            project(1, mh)
+            codes, scales = quantise_z("z1%d" % mh, z_bf[1, mh], QUARTER, None)
+            project(1, mh, codes[:], scales[:])
         out_rows = out.rearrange("(n p) m -> p n m", p=P)
         for mh, first, count in ((0, 0, 2), (0, 2, 2), (1, 0, 2), (1, 2, 1), (1, 3, 1)):
             res = shift_sb[:, first : first + count, quarters[mh]]

@@ -63,7 +63,6 @@ def tile_list_query_slot_cache_kernel(
         at_wf_raw = free[0]
         wf_raw = sbuf("wf_raw", [P, 1024], U16)
         at_tab1 = room(16 * KIB)
-        at_before_wb = room(2 * KIB)
         at_wb = [room(8 * KIB + LAP) for b in range(2)]
         at_w2 = [room(8 * KIB + LAP) for n in range(4)]
 
@@ -155,7 +154,9 @@ def tile_list_query_slot_cache_kernel(
             v1[jh] = sbuf("v1%d" % jh, [P, HALF], U32, at_scales + (3 - 2 * jh) * KIB)
             nc.vector.tensor_copy(v1[jh][:], tab[1][:].bitcast(U32).indirect(idx[:, 32 * jh : 32 * jh + 32]))
 
-        acts = {(b, jp): sbuf("act%d%d" % (b, jp), [P, 2 * HALF], F32) for b in range(2) for jp in range(2)}
+        act_wide = sbuf("act_wide", [P, 3 * HALF], F32)
+        acts = {(b, jp): sbuf("act%d%d" % (b, jp), [P, 2 * HALF], F32) for b in range(2) for jp in range(2) if (b, jp) != (0, 1)}
+        acts[0, 1] = act_wide[:, HALF:]
         wb_grouped = [sbuf("wb_grouped%d" % b, [P, 4, P, 4], BF16) for b in range(2)]
 
         def stationary(quantised, c):
@@ -179,8 +180,7 @@ def tile_list_query_slot_cache_kernel(
                 rhs=v1[j0 // HALF][:, j0 % HALF : j0 % HALF + n].bitcast(FP8X4), rhs_scale=v_sc[4:P, j0 : j0 + n], start=start, stop=stop,
             )
 
-        at_before_h = room(KIB)
-        at_h = [room(2 * KIB) for n in range(5)]
+        at_h = [room(2 * KIB) for n in range(3)]
         e_w = [sbuf("e_w%d" % b, [P, HALF], U32) for b in range(2)]
         e_sc = [sbuf("e_sc%d" % b, [P, HALF], U8) for b in range(2)]
 
@@ -209,7 +209,6 @@ def tile_list_query_slot_cache_kernel(
         nc.vector.tensor_copy(wb_grouped[1][:].rearrange("p t m i -> p m i t"), wb_raw[1][:].rearrange("p i (m t) -> p m i t", t=4))
         quantise_wb(1)
 
-        at_e_bf = free[0]
         e_bf = [sbuf("e_bf%d" % b, [P, HALF, 4], BF16) for b in range(2)]
 
         def e_first(b, jp):
@@ -232,8 +231,8 @@ def tile_list_query_slot_cache_kernel(
 
         w2_q = {}
 
-        def quantise_w2(c, grouped, at):
-            codes = sbuf("w2%d_w" % c, [P, HALF], U32, at)
+        def quantise_w2(c, grouped):
+            codes = sbuf("w2%d_w" % c, [P, HALF], U32)
             scales = sbuf("w2%d_sc" % c, [P, HALF], U8)
             for b in range(2):
                 nc.scalar.copy(
@@ -265,17 +264,17 @@ def tile_list_query_slot_cache_kernel(
         woven_both = sbuf("woven", [P, S, 4], BF16)
         woven = [woven_both[:, HALF * u : HALF * (u + 1), :] for u in range(2)]
 
-        def first_half(k, h):
-            encode(k, whole, banks[k], h)
+        def first_half(k, h, bank):
+            encode(k, whole, bank, h)
             write_slots(k, 0, whole, h, wgs0[:] if k < 4 else dealt0[k - 4][:, 0, :])
 
         e_first(0, 0)
-        e_first(1, 0)
-        quantise_w2(0, wb_grouped[0][:].rearrange("p t m i -> p (t m i)"), None)
-        h_quarter = [sbuf("h_quarter%d" % u, [P, QUARTER], F32, at_h[0] + KIB * u)[:] for u in range(2)]
-        encode(0, quarters[0], banks[0], h_quarter[0])
         e_first(0, 1)
+        e_first(1, 0)
+        quantise_w2(0, act_wide[:, 0 : 2 * HALF].bitcast(BF16))
         e_first(1, 1)
+        h_quarter = [acts[1, 1][:, HALF : HALF + QUARTER], sbuf("h_quarter", [P, QUARTER], F32)[:]]
+        encode(0, quarters[0], banks[0], h_quarter[0])
         write_slots(0, 0, quarters[0], h_quarter[0], wgs0[:, quarters[0]])
         encode(0, quarters[1], banks[4], h_quarter[1])
         write_slots(0, 0, quarters[1], h_quarter[1], wgs0[:, quarters[1]])
@@ -310,14 +309,14 @@ def tile_list_query_slot_cache_kernel(
         load_page(5, at_tab0 + LAP)
         dealt0.append(load_dealt("dealt02", slice(2, 3), 0, at_before_tab0 + LAP))
         load_page(6, at_tab0 + 8 * KIB + LAP)
-        dealt0.append(load_dealt("dealt03", slice(3, 4), 0, at_before_wb + LAP))
-        load_page(7, at_wb[0] + LAP)
-        wgs_fourth = load_wgs(HALF + QUARTER, QUARTER, at_wb[1])
-        bias_sb = sbuf("bias_sb", [P, 4], F32, at_wb[1] + 2 * KIB)
+        wgs_fourth = load_wgs(HALF + QUARTER, QUARTER, at_wb[0])
+        bias_sb = sbuf("bias_sb", [P, 4], F32, at_wb[0] + KIB)
         with nc.allow_non_contiguous_dma(reason="one value a partition for each page tile"):
             nc.sync.dma_start(bias_sb[:], bias[0:HALF].rearrange("(k p) -> p k", p=P))
-        bias_dealt = sbuf("bias_dealt", [P, 4], F32, at_wb[1] + 3 * KIB)
+        bias_dealt = sbuf("bias_dealt", [P, 4], F32, at_wb[0] + KIB + LAP)
         nc.sync.dma_start(bias_dealt[:], bias[HALF:].rearrange("(p t) -> p t", t=4))
+        dealt0.append(load_dealt("dealt03", slice(3, 4), 0, at_wb[1] - 2 * KIB + LAP))
+        load_page(7, at_wb[1] + LAP)
 
         def behind_cast(place, n):
             return at_w2[place] + (2 + 2 * n) * KIB + LAP
@@ -335,37 +334,44 @@ def tile_list_query_slot_cache_kernel(
             nc.scalar.copy(h[:].rearrange("p u j -> p (u j)"), banks[2 + first % 2][:, 0 : QUARTER * count])
             return [h[:, u, :] for u in range(count)]
 
-        quantise_w2(1, acts[1, 1][:].bitcast(BF16), at_before_h)
-        first_half(1, h_tile("h1", behind_cast(1, 1)))
-        first_half(2, h_tile("h2", at_h[1]))
+        quantise_w2(1, e_bf[1][:].rearrange("p j t -> p (j t)"))
+        first_half(1, h_tile("h1", behind_cast(1, 1)), banks[1])
+        first_half(2, h_tile("h2", at_h[0]), banks[2])
+        h3 = sbuf("h3", [P, QUARTER], F32)[:]
+        encode(3, quarters[0], banks[3], h3)
+        write_slots(3, 0, quarters[0], h3, wgs0[:, quarters[0]])
         early = acts_behind_cast(1)
         second_e(0, 0, 6, [acts[1, 0][:, 0:HALF], early[1]])
         second_e(0, 1, 4, early)
         e_third = second_quantise(0, None)
-        first_half(3, planes[1][:, 0:HALF])
-        h_third = third_h(0, 1, None) + third_h(1, 1, at_h[0] + KIB)
-        for k in range(2):
-            write_slots(k, 1, quarters[0], h_third[k], wgs_third[:])
+        encode(3, quarters[1], banks[3], planes[1][:, 0:QUARTER])
+        write_slots(3, 0, quarters[1], planes[1][:, 0:QUARTER], wgs0[:, quarters[1]])
         grouped = sbuf("w2_dealt_grouped", [P, 2, 4, P, 4], BF16, at_tab1 + 8 * KIB)
-        for b in range(2):
+
+        def cast_dealt(b):
             for tp in range(2):
                 nc.scalar.copy(
                     grouped[:, b, 2 * tp : 2 * tp + 2].rearrange("p t m i -> p m i t"),
                     w2_dealt[b][:].rearrange("p i (m t) -> p m i t", t=4)[:, :, :, 2 * tp : 2 * tp + 2],
                 )
+
+        cast_dealt(0)
+        h_third = third_h(0, 1, at_w2[2]) + third_h(1, 1, at_w2[2] + KIB)
+        for k in range(2):
+            write_slots(k, 1, quarters[0], h_third[k], wgs_third[:])
+        cast_dealt(1)
         w2_dealt_q = (sbuf("w2_dealt_w", [P, S], U32), sbuf("w2_dealt_sc", [P, S], U8))
         nc.vector.quantize_mx(w2_dealt_q[0][:].bitcast(FP8X4), w2_dealt_q[1][:], grouped[:].rearrange("p b t m i -> p (b t m i)"))
         h_third = h_third + third_h(2, 2, behind_cast(3, 1))
         for k in range(2, 4):
             write_slots(k, 1, quarters[0], h_third[k], wgs_third[:])
         for k in range(4, 6):
-            first_half(k, h_tile("h%d" % k, at_h[k - 3]))
+            first_half(k, h_tile("h%d" % k, at_h[k - 4]), banks[k])
         late = acts_behind_cast(3)
         second_e(1, 0, 0, late)
         second_e(1, 1, 2, late)
-        e_fourth = second_quantise(1, at_h[2])
-        for k in range(6, 8):
-            first_half(k, h_tile("h%d" % k, at_h[k - 3]))
+        e_fourth = second_quantise(1, at_h[1])
+        first_half(6, h_tile("h6", at_h[2]), banks[6])
 
         w3_w = {}
 
@@ -373,7 +379,8 @@ def tile_list_query_slot_cache_kernel(
             w3_w[a] = sbuf("w3_w%d" % a, [P, 512], I32, at)
             nc.sync.dma_start(w3_w[a][:], w3_words[a].rearrange("p c i -> p (c i)").bitcast(I32))
 
-        load_w3(1, at_wb[1] + 4 * KIB)
+        for a in range(2):
+            load_w3(a, at_wb[0] + (2 + 2 * a) * KIB)
         w3_sc = sbuf("w3_sc", [P, 512], U8, at_wf_raw + KIB)
         nc.gpsimd.memset(w3_sc[:].bitcast(I32), 0)
         for q in range(4):
@@ -469,17 +476,19 @@ def tile_list_query_slot_cache_kernel(
             else:
                 write_slots(k, 1, whole, h_last[k], dealt1[:, k - 4, :])
             read_slots(k - 1)
-            if k == 5:
-                z0_codes, z0_scales = quantise_z("z0", woven[0], M, at_e_bf)
+            if k == 2:
+                first_half(7, h_last[0], banks[2])
         read_slots(6)
-        load_w3(0, at_tab0 + 8 * KIB + LAP)
-        for mh in range(2):
-            project(0, mh, z0_codes[:, quarters[mh]], z0_scales[:, quarters[mh]])
         write_slots(7, 1, whole, h_last[7], dealt1[:, 3, :])
+        codes, scales = quantise_z("z00", z_bf[0, 0], QUARTER, at_tab0 + 8 * KIB + LAP)
+        project(0, 0, codes[:], scales[:])
         for mh in range(2):
             x = h_last[7][:, quarters[mh]]
             nc.vector.tensor_copy(x, pages[7][:].indirect(idx3[:, 16 * mh : 16 * mh + 16]))
             add_bias_dealt(7, mh, x)
+            if mh == 0:
+                codes, scales = quantise_z("z01", z_bf[0, 1], QUARTER, at_w2[0])
+                project(0, 1, codes[:], scales[:])
         for mh in range(2):
             codes, scales = quantise_z("z1%d" % mh, z_bf[1, mh], QUARTER, None)
             project(1, mh, codes[:], scales[:])

@@ -110,8 +110,6 @@ def tile_list_query_slot_cache_kernel(
         wb_raw.append(load_weight("wb_raw1", wb[:, HALF:], at_wb[1]))
         gain_sb = sbuf("gain_sb", [P, 2, 4], F32)
         nc.sync.dma_start(gain_sb[:], gain.rearrange("(b p t) -> p b t", b=2, t=4))
-        nc.sync.dma_start(idx2[:], offs2)
-        nc.sync.dma_start(idx3[:], offs3)
         for scale_tile in (tab_sc, wf_sc_raw):
             nc.vector.memset(scale_tile[:].bitcast(I32), 0)
         for q in range(4):
@@ -127,10 +125,12 @@ def tile_list_query_slot_cache_kernel(
         load_w2(0)
         wgs0 = load_wgs(0, HALF)
         load_page(0)
+        nc.sync.dma_start(idx2[:], offs2)
         load_w2(1)
         load_page(1)
         load_page(2)
         load_page(3)
+        nc.sync.dma_start(idx3[:], offs3)
         wgs_third = load_wgs(HALF, QUARTER)
         w2_dealt = [load_weight("w2_dealt%d" % b, w2[HALF * b : HALF * (b + 1), HALF:], at_w2[2 + b]) for b in range(2)]
         dealt0 = [load_dealt("dealt00", slice(0, 1), 0)]
@@ -206,7 +206,11 @@ def tile_list_query_slot_cache_kernel(
         quantise_wb(0)
         for jh in range(2):
             gather_second_pass(jh)
-        nc.vector.tensor_copy(wb_grouped[1][:].rearrange("p t m i -> p m i t"), wb_raw[1][:].rearrange("p i (m t) -> p m i t", t=4))
+        for tp in range(2):
+            nc.vector.tensor_copy(
+                wb_grouped[1][:, 2 * tp : 2 * tp + 2].rearrange("p t m i -> p m i t"),
+                wb_raw[1][:].rearrange("p i (m t) -> p m i t", t=4)[:, :, :, 2 * tp : 2 * tp + 2],
+            )
         quantise_wb(1)
 
         e_bf = [sbuf("e_bf%d" % b, [P, HALF, 4], BF16) for b in range(2)]

@@ -231,6 +231,8 @@ def tile_list_query_slot_cache_kernel(
                 e_bf[b][:, cols, :], acts[b, jp][:].rearrange("p (j t) -> p j t", t=4),
                 gain_sb[:, b : b + 1, :].to_broadcast([P, QUARTER, 4]), MULT,
             )
+
+        def quantise_first(b, cols):
             nc.vector.quantize_mx(e_w[b][:, cols].bitcast(FP8X4), e_sc[b][:, cols], e_bf[b][:, cols, :].rearrange("p j t -> p (j t)"))
 
         w2_q = {}
@@ -275,8 +277,11 @@ def tile_list_query_slot_cache_kernel(
         e_first(0, 0)
         e_first(0, 1)
         e_first(1, 0)
+        quantise_first(0, whole)
+        quantise_first(1, quarters[0])
         quantise_w2(0, act_wide[:, 0 : 2 * HALF].bitcast(BF16))
         e_first(1, 1)
+        quantise_first(1, quarters[1])
         h_quarter = [acts[1, 1][:, HALF : HALF + QUARTER], sbuf("h_quarter", [P, QUARTER], F32)[:]]
         encode(0, quarters[0], banks[0], h_quarter[0])
         write_slots(0, 0, quarters[0], h_quarter[0], wgs0[:, quarters[0]])
@@ -338,7 +343,11 @@ def tile_list_query_slot_cache_kernel(
             nc.scalar.copy(h[:].rearrange("p u j -> p (u j)"), banks[2 + first % 2][:, 0 : QUARTER * count])
             return [h[:, u, :] for u in range(count)]
 
-        quantise_w2(1, e_bf[1][:].rearrange("p j t -> p (j t)"))
+        codes, scales = sbuf("w21_w", [P, HALF], U32), sbuf("w21_sc", [P, HALF], U8)
+        for b, staged in enumerate((e_bf[1][:, quarters[0], :].rearrange("p j t -> p (j t)"), acts[1, 1][:, 0:HALF].bitcast(BF16))):
+            nc.scalar.copy(staged.rearrange("p (c x i) -> p c i x", x=4, i=4), w2_raw[1, b][:].rearrange("p i (c x) -> p c i x", x=4))
+            nc.vector.quantize_mx(codes[:, quarters[b]].bitcast(FP8X4), scales[:, quarters[b]], staged)
+        w2_q[1] = (codes, scales)
         first_half(1, h_tile("h1", behind_cast(1, 1)), banks[1])
         first_half(2, h_tile("h2", at_h[0]), banks[2])
         h3 = sbuf("h3", [P, QUARTER], F32)[:]
@@ -464,14 +473,16 @@ def tile_list_query_slot_cache_kernel(
             nc.vector.quantize_mx(codes[:].bitcast(FP8X4), scales[:], z.rearrange("p m t -> p (m t)"))
             return codes, scales
 
-        def project(a, mh, codes, scales):
-            for n in range(4):
-                cols = slice(P * n, P * (n + 1))
-                nc.tensor.matmul_mx(
-                    banks[4 + 2 * mh + n // 2][:, quarters[n % 2]], lhsT=w3_w[a][:, cols].bitcast(FP8X4), lhsT_scale=w3_sc[4 * a : P, cols],
-                    rhs=codes.bitcast(FP8X4), rhs_scale=scales,
-                    start=(a == 0 and n % 2 == 0), stop=(a == 1 and n % 2 == 1),
-                )
+        def project(a, first, count, codes, scales):
+            for n in range(count):
+                entries = slice(P * n, P * (n + 1))
+                for c in range(4):
+                    cols = slice(P * c, P * (c + 1))
+                    nc.tensor.matmul_mx(
+                        banks[4 + first + n][:, cols], lhsT=w3_w[a][:, cols].bitcast(FP8X4), lhsT_scale=w3_sc[4 * a : P, cols],
+                        rhs=codes[:, entries].bitcast(FP8X4), rhs_scale=scales[:, entries],
+                        start=(a == 0 and c == 0), stop=(a == 1 and c == 3),
+                    )
 
         write_slots(0, 1, quarters[1], h_last[0][:, quarters[1]], wgs_fourth[:])
         for k in range(1, 7):
@@ -485,21 +496,21 @@ def tile_list_query_slot_cache_kernel(
         read_slots(6)
         write_slots(7, 1, whole, h_last[7], dealt1[:, 3, :])
         codes, scales = quantise_z("z00", z_bf[0, 0], QUARTER, at_tab0 + 8 * KIB + LAP)
-        project(0, 0, codes[:], scales[:])
-        for mh in range(2):
-            x = h_last[7][:, quarters[mh]]
-            nc.vector.tensor_copy(x, pages[7][:].indirect(idx3[:, 16 * mh : 16 * mh + 16]))
-            add_bias_dealt(7, mh, x)
-            if mh == 0:
+        project(0, 0, 2, codes, scales)
+        for n in range(4):
+            x = h_last[7][:, P * n : P * (n + 1)]
+            nc.vector.tensor_copy(x, pages[7][:].indirect(idx3[:, 8 * n : 8 * n + 8]))
+            nc.scalar.activation(woven[1][:, P * n : P * (n + 1), 3], x, ACT.Identity, bias=bias_dealt[:, 3:4])
+            if n == 1:
                 codes, scales = quantise_z("z01", z_bf[0, 1], QUARTER, at_w2[0])
-                project(0, 1, codes[:], scales[:])
-        for mh in range(2):
-            codes, scales = quantise_z("z1%d" % mh, z_bf[1, mh], QUARTER, None)
-            project(1, mh, codes[:], scales[:])
-        out_rows = out.rearrange("(n p) m -> p n m", p=P)
-        for mh, first, count in ((0, 0, 2), (0, 2, 2), (1, 0, 2), (1, 2, 1), (1, 3, 1)):
-            res = shift_sb[:, first : first + count, quarters[mh]]
-            acc = banks[4 + 2 * mh + first // 2][:].rearrange("p (n m) -> p n m", n=2)[:, first % 2 : first % 2 + count]
+                project(0, 2, 2, codes, scales)
+        for n in range(4):
+            codes, scales = quantise_z("z1%d" % n, woven[1][:, P * n : P * (n + 1), :], P, None)
+            project(1, n, 1, codes, scales)
+        out_rows = out.rearrange("(c p) m -> p c m", p=P)
+        for n, first, count in ((0, 0, 4), (1, 0, 4), (2, 0, 4), (3, 0, 2), (3, 2, 2)):
+            res = shift_sb[:, first : first + count, P * n : P * (n + 1)]
+            acc = banks[4 + n][:].rearrange("p (c m) -> p c m", c=4)[:, first : first + count]
             nc.vector.tensor_tensor(res, acc, res, ADD)
-            queue = nc.scalar if first == 2 else nc.sync
-            queue.dma_start(out_rows[:, first : first + count, quarters[mh]], res)
+            queue = nc.scalar if (n, first) in ((1, 0), (3, 0)) else nc.sync
+            queue.dma_start(out_rows[:, first : first + count, P * n : P * (n + 1)], res)

from contextlib import ExitStack

import concourse.mybir as mybir
from concourse.masks import make_identity

F32 = mybir.dt.float32
BF16 = mybir.dt.bfloat16
I32 = mybir.dt.int32
U32 = mybir.dt.uint32
U16 = mybir.dt.uint16
U8 = mybir.dt.uint8
FP8X4 = mybir.dt.float8_e4m3fn_x4
FP4X4 = mybir.dt.float4_e2m1fn_x4
MULT = mybir.AluOpType.mult
ADD = mybir.AluOpType.add
ACT = mybir.ActivationFunctionType

P = 128
T, S, T2, M = 4096, 1024, 2048, 512
HALF = 512
QUARTER = 256
KIB = 1024
LAP = 64
FLOPS = 4831838208


def tile_list_query_slot_cache_kernel(
    tc, tab_words, tab_scales, offs, wf_words, wf_scales, wb, gain, w2, page0, wgs,
    offs2, offs3, bias, w3_words, w3_scales, shift, out,
):
    nc = tc.nc
    with ExitStack() as ctx:
        lists = ctx.enter_context(tc.tile_pool(name="lists", bufs=1))
        sb = ctx.enter_context(tc.tile_pool(name="sb", bufs=1))
        psum = ctx.enter_context(tc.psum_pool(name="psum", bufs=1))
        banks = [psum.tile([P, HALF], F32, name="bank%d" % n) for n in range(8)]

        free = [0]

        def room(nbytes):
            start = free[0]
            free[0] = start + (nbytes + 63) // 64 * 64
            return start

        def sbuf(name, shape, dtype, at=None):
            nbytes = 1 if dtype == U8 else 2 if dtype in (BF16, U16) else 4
            for n in shape[1:]:
                nbytes = nbytes * n
            return sb.tile(shape, dtype, name=name, align_bytes=64, offset=room(nbytes) if at is None else at)

        idx = lists.tile([P, S // 16], U16, name="idx")
        idx2 = lists.tile([P, S // 16], U16, name="idx2")
        idx3 = lists.tile([P, M // 16], U16, name="idx3")

        at_before_tab0 = room(2 * KIB)
        at_tab0 = room(16 * KIB + LAP)
        at_scales = free[0]
        tab_sc = sbuf("tab_sc", [P, T], U8)
        wf_sc_raw = sbuf("wf_sc_raw", [P, 1024], U8)
        wf_w = sbuf("wf_w", [P, 1024], U16)
        wf_sc = sbuf("wf_sc", [P, 1024], U8)
        wf_sc_rows = sbuf("wf_sc_rows", [P, 256], I32)
        at_wf_raw = free[0]
        wf_raw = sbuf("wf_raw", [P, 1024], U16)
        at_tab1 = room(16 * KIB)
        at_wb = [room(8 * KIB + LAP) for b in range(2)]
        at_w2 = [room(8 * KIB + LAP) for n in range(4)]

        def load_tab(a, at):
            tile = sbuf("tab%d" % a, [P, T], I32, at)
            nc.sync.dma_start(tile[:], tab_words[a].rearrange("p t i -> p (t i)").bitcast(I32))
            return tile

        def load_weight(name, rows, at):
            tile = sbuf(name, [P, 4, rows.shape[1]], F32, at)
            nc.sync.dma_start(tile[:], rows.rearrange("(p i) c -> p i c", i=4))
            return tile

        pages = {}

        def load_page(k, at=None):
            pages[k] = sbuf("page%d" % k, [P, T2], F32, at)
            rows = page0[P * k : P * (k + 1), :] if k < 4 else page0[HALF:, :].rearrange("(p t) c -> t p c", t=4)[k - 4]
            nc.sync.dma_start(pages[k][:], rows)

        w2_raw = {}

        def load_w2(c):
            for b in range(2):
                rows = w2[HALF * b : HALF * (b + 1), QUARTER * c : QUARTER * (c + 1)]
                w2_raw[c, b] = load_weight("w2_raw%d%d" % (c, b), rows, at_w2[c] + 4 * KIB * b)

        def load_dealt(name, ts, jh, at=None):
            tile = sbuf(name, [P, ts.stop - ts.start, HALF], F32, at)
            rows = wgs.rearrange("(q t) j -> q t j", t=4)[:, ts, HALF * jh : HALF * (jh + 1)]
            for q in (0, 2, 1, 3):
                nc.sync.dma_start(tile[32 * q : 32 * q + 32, :, :], rows)
            return tile

        def load_wgs(first, count, at=None):
            tile = sbuf("wgs%d" % first, [P, count], F32, at)
            nc.sync.dma_start(tile[:], wgs[:, first : first + count])
            return tile

        nc.sync.dma_start(idx[:], offs)
        tab = [load_tab(0, at_tab0)]
        nc.sync.dma_start(wf_raw[:].bitcast(I32), wf_words[0].bitcast(I32))
        wb_raw = [load_weight("wb_raw0", wb[:, 0:HALF], at_wb[0])]
        tab.append(load_tab(1, at_tab1))
        wb_raw.append(load_weight("wb_raw1", wb[:, HALF:], at_wb[1]))
        gain_sb = sbuf("gain_sb", [P, 2, 4], F32)
        nc.sync.dma_start(gain_sb[:], gain.rearrange("(b p t) -> p b t", b=2, t=4))
        for scale_tile in (tab_sc, wf_sc_raw):
            nc.vector.memset(scale_tile[:].bitcast(I32), 0)
        for q in range(4):
            nc.gpsimd.dma_start(tab_sc[32 * q : 32 * q + 8, :].bitcast(I32), tab_scales[:, 4 * q : 4 * q + 4, :].bitcast(I32))
        for q in range(4):
            rows = slice(32 * q, 32 * q + 4)
            nc.scalar.dma_start(wf_sc_rows[rows, :], wf_scales[0, 4 * q : 4 * q + 4, :].bitcast(I32))
            nc.vector.tensor_copy(wf_sc_raw[rows, :].bitcast(I32), wf_sc_rows[rows, :])
        nc.vector.tensor_copy(
            wf_w[:].rearrange("p (b t m) -> p b t m", b=2, t=4),
            wf_raw[:].rearrange("p (b m t) -> p b t m", b=2, t=4),
        )
        load_w2(0)
        wgs0 = load_wgs(0, HALF)
        load_page(0)
        nc.sync.dma_start(idx2[:], offs2)
        load_w2(1)
        load_page(1)
        load_page(2)
        load_page(3)
        nc.sync.dma_start(idx3[:], offs3)
        wgs_third = load_wgs(HALF, QUARTER)
        w2_dealt = [load_weight("w2_dealt%d" % b, w2[HALF * b : HALF * (b + 1), HALF:], at_w2[2 + b]) for b in range(2)]
        dealt0 = [load_dealt("dealt00", slice(0, 1), 0)]
        load_page(4)
        dealt0.append(load_dealt("dealt01", slice(1, 2), 0))
        ident = sbuf("ident", [P, P], F32, at_wf_raw)
        make_identity(nc, ident[:])

        v0 = sbuf("v0", [P, S], U32)
        nc.vector.tensor_copy(v0[:], tab[0][:].bitcast(U32).indirect(idx[:]))
        v_sc = sbuf("v_sc", [P, S], U8)
        for jh in range(2):
            nc.vector.tensor_copy(v_sc[:, HALF * jh : HALF * (jh + 1)], tab_sc[:].indirect(idx[:, 32 * jh : 32 * jh + 32]))
        nc.vector.tensor_copy(
            wf_sc[:].rearrange("p (b t m) -> p b t m", b=2, t=4),
            wf_sc_raw[:].rearrange("p (b m t) -> p b t m", b=2, t=4),
        )
        v1 = {}

        def gather_second_pass(jh):
            v1[jh] = sbuf("v1%d" % jh, [P, HALF], U32, at_scales + (3 - 2 * jh) * KIB)
            nc.vector.tensor_copy(v1[jh][:], tab[1][:].bitcast(U32).indirect(idx[:, 32 * jh : 32 * jh + 32]))

        act_wide = sbuf("act_wide", [P, 3 * HALF], F32)
        acts = {(b, jp): sbuf("act%d%d" % (b, jp), [P, 2 * HALF], F32) for b in range(2) for jp in range(2) if (b, jp) != (0, 1)}
        acts[0, 1] = act_wide[:, HALF:]
        wb_grouped = [sbuf("wb_grouped%d" % b, [P, 4, P, 4], BF16) for b in range(2)]

        def stationary(quantised, c):
            codes, scales = quantised
            cols = slice(P * c, P * (c + 1))
            return codes[:, cols].bitcast(FP8X4), scales[:, cols]

        def wf_pass(acc, b, t, j0, n, start, stop):
            c = 4 * b + t
            nc.tensor.matmul_mx(
                acc, lhsT=wf_w[:, P * c : P * (c + 1)].bitcast(FP4X4), lhsT_scale=wf_sc[:, P * c : P * (c + 1)],
                rhs=v0[:, j0 : j0 + n].bitcast(FP8X4), rhs_scale=v_sc[:, j0 : j0 + n], start=start, stop=stop,
            )

        wb_q = {}

        def wb_pass(acc, b, t, j0, n, start, stop):
            codes, scales = stationary(wb_q[b], t)
            nc.tensor.matmul_mx(
                acc, lhsT=codes, lhsT_scale=scales,
                rhs=v1[j0 // HALF][:, j0 % HALF : j0 % HALF + n].bitcast(FP8X4), rhs_scale=v_sc[4:P, j0 : j0 + n], start=start, stop=stop,
            )

        at_h = [room(2 * KIB) for n in range(3)]
        e_w = [sbuf("e_w%d" % b, [P, HALF], U32) for b in range(2)]
        e_sc = [sbuf("e_sc%d" % b, [P, HALF], U8) for b in range(2)]

        def y_first(b, jq):
            return banks[4 * b + jq][:].rearrange("p (t j) -> p t j", t=4)

        for b in range(2):
            for jq in range(2):
                for t in range(4):
                    wf_pass(y_first(b, jq)[:, t, :], b, t, P * jq, P, t == 0, False)

        def quantise_wb(b):
            codes = sbuf("wb%d_w" % b, [P, HALF], U32)
            scales = sbuf("wb%d_sc" % b, [P, HALF], U8)
            nc.vector.quantize_mx(codes[:].bitcast(FP8X4), scales[:], wb_grouped[b][:].rearrange("p t m i -> p (t m i)"))
            wb_q[b] = (codes, scales)

        for tp in range(2):
            nc.scalar.copy(
                wb_grouped[0][:, 2 * tp : 2 * tp + 2].rearrange("p t m i -> p m i t"),
                wb_raw[0][:].rearrange("p i (m t) -> p m i t", t=4)[:, :, :, 2 * tp : 2 * tp + 2],
            )
        quantise_wb(0)
        for jh in range(2):
            gather_second_pass(jh)
        for tp in range(2):
            nc.vector.tensor_copy(
                wb_grouped[1][:, 2 * tp : 2 * tp + 2].rearrange("p t m i -> p m i t"),
                wb_raw[1][:].rearrange("p i (m t) -> p m i t", t=4)[:, :, :, 2 * tp : 2 * tp + 2],
            )
        quantise_wb(1)

        e_bf = [sbuf("e_bf%d" % b, [P, HALF, 4], BF16) for b in range(2)]

        def e_first(b, jp):
            opened = jp == 0
            for u in range(2):
                jq = 2 * jp + u
                for t in range(4):
                    wb_pass(y_first(b, jq)[:, t, :], b, t, P * jq, P, t == 0 and not opened, t == 3 and opened)
                if not opened:
                    for t in range(4):
                        wf_pass(y_first(b, jq)[:, t, :], b, t, P * jq, P, False, t == 3)
                act = acts[b, jp][:, HALF * u : HALF * (u + 1)].rearrange("p (j t) -> p j t", t=4)
                nc.scalar.activation(act, y_first(b, jq).rearrange("p t j -> p j t"), ACT.Silu)
            cols = slice(QUARTER * jp, QUARTER * (jp + 1))
            nc.vector.tensor_tensor(
                e_bf[b][:, cols, :], acts[b, jp][:].rearrange("p (j t) -> p j t", t=4),
                gain_sb[:, b : b + 1, :].to_broadcast([P, QUARTER, 4]), MULT,
            )

        def quantise_first(b, cols):
            nc.vector.quantize_mx(e_w[b][:, cols].bitcast(FP8X4), e_sc[b][:, cols], e_bf[b][:, cols, :].rearrange("p j t -> p (j t)"))

        w2_q = {}

        def quantise_w2(c, grouped):
            codes = sbuf("w2%d_w" % c, [P, HALF], U32)
            scales = sbuf("w2%d_sc" % c, [P, HALF], U8)
            for b in range(2):
                nc.scalar.copy(
                    grouped[:, S * b : S * (b + 1)].rearrange("p (c x i) -> p c i x", x=4, i=4),
                    w2_raw[c, b][:].rearrange("p i (c x) -> p c i x", x=4),
                )
            nc.vector.quantize_mx(codes[:].bitcast(FP8X4), scales[:], grouped)
            w2_q[c] = (codes, scales)

        def product(k, part, acc):
            for b in range(2):
                codes, scales = stationary(w2_q[k // 2], 2 * b + k % 2) if k < 4 else stationary(w2_dealt_q, 4 * b + k - 4)
                nc.tensor.matmul_mx(
                    acc, lhsT=codes, lhsT_scale=scales, rhs=part[b][0].bitcast(FP8X4), rhs_scale=part[b][1],
                    start=(b == 0), stop=(b == 1),
                )

        def encode(k, cols, bank, h):
            product(k, [(e_w[b][:, cols], e_sc[b][:, cols]) for b in range(2)], bank[:, cols])
            nc.scalar.copy(h, bank[:, cols])

        def write_slots(k, jh, cols, h, weight):
            first, last = (HALF * jh + cols.start) // 16, (HALF * jh + cols.stop) // 16
            nc.vector.tensor_tensor(pages[k][:].indirect(idx2[:, first:last]), h, weight, MULT)

        whole = slice(0, HALF)
        quarters = [slice(0, QUARTER), slice(QUARTER, HALF)]
        planes = [sbuf("planes%d" % b, [P, 1024], F32) for b in range(2)]
        woven_both = sbuf("woven", [P, S, 4], BF16)
        woven = [woven_both[:, HALF * u : HALF * (u + 1), :] for u in range(2)]

        def first_half(k, h, bank):
            encode(k, whole, bank, h)
            write_slots(k, 0, whole, h, wgs0[:] if k < 4 else dealt0[k - 4][:, 0, :])

        e_first(0, 0)
        e_first(0, 1)
        e_first(1, 0)
        quantise_first(0, whole)
        quantise_first(1, quarters[0])
        quantise_w2(0, act_wide[:, 0 : 2 * HALF].bitcast(BF16))
        e_first(1, 1)
        quantise_first(1, quarters[1])
        h_quarter = [acts[1, 1][:, HALF : HALF + QUARTER], sbuf("h_quarter", [P, QUARTER], F32)[:]]
        encode(0, quarters[0], banks[0], h_quarter[0])
        write_slots(0, 0, quarters[0], h_quarter[0], wgs0[:, quarters[0]])
        encode(0, quarters[1], banks[4], h_quarter[1])
        write_slots(0, 0, quarters[1], h_quarter[1], wgs0[:, quarters[1]])

        def second_planes(u, b, tp, bank, act):
            j0 = HALF + QUARTER * u
            for n in range(2):
                for jq in range(2):
                    wf_pass(bank[:, QUARTER * n + P * jq : QUARTER * n + P * (jq + 1)], b, 2 * tp + n, j0 + P * jq, P, n + jq == 0, False)
            for n in range(2):
                wb_pass(bank[:, quarters[n]], b, 2 * tp + n, j0, QUARTER, False, n == 1)
            nc.scalar.activation(act, bank[:], ACT.Silu)
            for n in range(2):
                t = 2 * tp + n
                plane = planes[b][:].bitcast(BF16)[:, S * u + QUARTER * t : S * u + QUARTER * (t + 1)]
                nc.scalar.activation(plane, act[:, quarters[n]], ACT.Copy, scale=gain_sb[:, b, t : t + 1])

        def second_e(u, b, first_bank, act_tiles):
            for tp in range(2):
                second_planes(u, b, tp, banks[first_bank + tp], act_tiles[tp])
            nc.scalar.copy(
                woven[u][:, quarters[b], :].rearrange("p (c i) t -> p c t i", i=4),
                planes[b][:].bitcast(BF16)[:, S * u : S * (u + 1)].rearrange("p (t c i) -> p c t i", t=4, i=4),
            )

        def second_quantise(u, at):
            codes = sbuf("e_w_second%d" % u, [P, HALF], U32, at)
            scales = sbuf("e_sc_second%d" % u, [P, HALF], U8)
            nc.vector.quantize_mx(codes[:].bitcast(FP8X4), scales[:], woven[u].rearrange("p j t -> p (j t)"))
            return [(codes[:, quarters[b]], scales[:, quarters[b]]) for b in range(2)]

        load_page(5, at_tab0 + LAP)
        dealt0.append(load_dealt("dealt02", slice(2, 3), 0, at_before_tab0 + LAP))
        load_page(6, at_tab0 + 8 * KIB + LAP)
        wgs_fourth = load_wgs(HALF + QUARTER, QUARTER, at_wb[0])
        bias_sb = sbuf("bias_sb", [P, 4], F32, at_wb[0] + KIB)
        with nc.allow_non_contiguous_dma(reason="one value a partition for each page tile"):
            nc.sync.dma_start(bias_sb[:], bias[0:HALF].rearrange("(k p) -> p k", p=P))
        bias_dealt = sbuf("bias_dealt", [P, 4], F32, at_wb[0] + KIB + LAP)
        nc.sync.dma_start(bias_dealt[:], bias[HALF:].rearrange("(p t) -> p t", t=4))
        dealt0.append(load_dealt("dealt03", slice(3, 4), 0, at_wb[1] - 2 * KIB + LAP))
        load_page(7, at_wb[1] + LAP)

        def behind_cast(place, n):
            return at_w2[place] + (2 + 2 * n) * KIB + LAP

        def acts_behind_cast(place):
            return [sbuf("act_c%d%d" % (place, n), [P, HALF], F32, behind_cast(place, 2 * n))[:] for n in range(2)]

        def h_tile(name, at):
            return sbuf(name, [P, HALF], F32, at)[:]

        def third_h(first, count, at):
            h = sbuf("h_third%d" % first, [P, count, QUARTER], F32, at)
            for u in range(count):
                product(first + u, e_third, banks[2 + first % 2][:, quarters[u]])
            nc.scalar.copy(h[:].rearrange("p u j -> p (u j)"), banks[2 + first % 2][:, 0 : QUARTER * count])
            return [h[:, u, :] for u in range(count)]

        codes, scales = sbuf("w21_w", [P, HALF], U32), sbuf("w21_sc", [P, HALF], U8)
        for b, staged in enumerate((e_bf[1][:, quarters[0], :].rearrange("p j t -> p (j t)"), acts[1, 1][:, 0:HALF].bitcast(BF16))):
            nc.scalar.copy(staged.rearrange("p (c x i) -> p c i x", x=4, i=4), w2_raw[1, b][:].rearrange("p i (c x) -> p c i x", x=4))
            nc.vector.quantize_mx(codes[:, quarters[b]].bitcast(FP8X4), scales[:, quarters[b]], staged)
        w2_q[1] = (codes, scales)
        first_half(1, h_tile("h1", behind_cast(1, 1)), banks[1])
        first_half(2, h_tile("h2", at_h[0]), banks[2])
        h3 = sbuf("h3", [P, QUARTER], F32)[:]
        encode(3, quarters[0], banks[3], h3)
        write_slots(3, 0, quarters[0], h3, wgs0[:, quarters[0]])
        early = acts_behind_cast(1)
        second_e(0, 0, 6, [acts[1, 0][:, 0:HALF], early[1]])
        second_e(0, 1, 4, early)
        e_third = second_quantise(0, None)
        encode(3, quarters[1], banks[3], planes[1][:, 0:QUARTER])
        write_slots(3, 0, quarters[1], planes[1][:, 0:QUARTER], wgs0[:, quarters[1]])
        grouped = sbuf("w2_dealt_grouped", [P, 2, 4, P, 4], BF16, at_tab1 + 8 * KIB)

        def cast_dealt(b):
            for tp in range(2):
                nc.scalar.copy(
                    grouped[:, b, 2 * tp : 2 * tp + 2].rearrange("p t m i -> p m i t"),
                    w2_dealt[b][:].rearrange("p i (m t) -> p m i t", t=4)[:, :, :, 2 * tp : 2 * tp + 2],
                )

        cast_dealt(0)
        h_third = third_h(0, 1, at_w2[2]) + third_h(1, 1, at_w2[2] + KIB)
        for k in range(2):
            write_slots(k, 1, quarters[0], h_third[k], wgs_third[:])
        cast_dealt(1)
        w2_dealt_q = (sbuf("w2_dealt_w", [P, S], U32), sbuf("w2_dealt_sc", [P, S], U8))
        nc.vector.quantize_mx(w2_dealt_q[0][:].bitcast(FP8X4), w2_dealt_q[1][:], grouped[:].rearrange("p b t m i -> p (b t m i)"))
        h_third = h_third + third_h(2, 2, behind_cast(3, 1))
        for k in range(2, 4):
            write_slots(k, 1, quarters[0], h_third[k], wgs_third[:])
        for k in range(4, 6):
            first_half(k, h_tile("h%d" % k, at_h[k - 4]), banks[k])
        late = acts_behind_cast(3)
        second_e(1, 0, 0, late)
        second_e(1, 1, 2, late)
        e_fourth = second_quantise(1, at_h[1])
        first_half(6, h_tile("h6", at_h[2]), banks[6])

        w3_w = {}

        def load_w3(a, at):
            w3_w[a] = sbuf("w3_w%d" % a, [P, 512], I32, at)
            nc.sync.dma_start(w3_w[a][:], w3_words[a].rearrange("p c i -> p (c i)").bitcast(I32))

        for a in range(2):
            load_w3(a, at_wb[0] + (2 + 2 * a) * KIB)
        w3_sc = sbuf("w3_sc", [P, 512], U8, at_wf_raw + KIB)
        nc.gpsimd.memset(w3_sc[:].bitcast(I32), 0)
        for q in range(4):
            nc.sync.dma_start(w3_sc[32 * q : 32 * q + 8, :].bitcast(I32), w3_scales[:, 4 * q : 4 * q + 4, :].bitcast(I32))
        dealt1 = load_dealt("dealt1", slice(0, 4), 1, at_w2[0])
        shift_sb = sbuf("shift_sb", [P, 4, M], F32, at_w2[2])
        nc.sync.dma_start(shift_sb[:], shift.rearrange("(n p) m -> p n m", p=P))

        h_last = [acts[0, jp][:, HALF * u : HALF * (u + 1)] for jp in range(2) for u in range(2)]
        h_last = h_last + [e_bf[b][:].rearrange("p j t -> p (j t)").bitcast(F32)[:, HALF * u : HALF * (u + 1)] for b in range(2) for u in range(2)]

        for n in range(2):
            for u in range(2):
                product(2 * n + u, e_fourth, banks[n][:, quarters[u]])
            nc.scalar.copy(
                acts[0, n][:].rearrange("p (u j) -> p u j", u=2)[:, :, quarters[1]],
                banks[n][:].rearrange("p (u j) -> p u j", u=2),
            )

        def encode_rest(k, bank):
            product(k, e_third, bank[:, quarters[0]])
            product(k, e_fourth, bank[:, quarters[1]])
            nc.scalar.copy(h_last[k], bank[:])

        for k in range(4, 6):
            encode_rest(k, banks[k + 2])

        z_bf = {(a, mh): woven[a][:, quarters[mh], :] for a in range(2) for mh in range(2)}
        z_turned = sbuf("z_turned", [P, 4, 2, P, 2], BF16, at_tab1)

        def add_bias_plain(k, x, bank):
            for n in range(4):
                nc.tensor.matmul(
                    bank[:, P * n : P * (n + 1)], lhsT=bias_sb[:, k : k + 1].to_broadcast([P, P]), rhs=ident[:],
                    is_transpose=True, start=(n == 0), stop=False,
                )
            for n in range(4):
                nc.tensor.matmul(
                    bank[:, P * n : P * (n + 1)], lhsT=x[:, P * n : P * (n + 1)], rhs=ident[:],
                    is_transpose=True, start=False, stop=(n == 3),
                )
            nc.scalar.copy(
                z_turned[:, :, :, 32 * k : 32 * (k + 1), :],
                bank[:].rearrange("p (n q u e) -> p n u q e", q=32, u=2, e=2),
            )

        def turn_back(mh):
            bank = banks[2 + mh]
            words = z_turned[:].rearrange("p n u q e -> p (n u q e)").bitcast(F32)
            for n in range(4):
                cols = slice(P * (4 * mh + n), P * (4 * mh + n + 1))
                nc.tensor.transpose(bank[:, P * n : P * (n + 1)], words[:, cols], ident[:])
            nc.scalar.copy(
                z_bf[0, mh].rearrange("p m t -> p (m t)").bitcast(F32).rearrange("p (n m u) -> p n m u", n=2, u=2),
                bank[:].rearrange("p (n u m) -> p n m u", n=2, u=2),
            )

        def add_bias_dealt(k, mh, x):
            nc.scalar.activation(z_bf[1, mh][:, :, k - 4], x, ACT.Identity, bias=bias_dealt[:, k - 4 : k - 3])

        def read_slots(k):
            x = sbuf("x%d" % k, [P, M], F32, at_tab1 + 2 * KIB * (k - 4))[:] if k in (4, 5) else h_last[k]
            nc.vector.tensor_copy(x, pages[k][:].indirect(idx3[:]))
            if k < 4:
                add_bias_plain(k, x, banks[k % 2])
            else:
                for mh in range(2):
                    add_bias_dealt(k, mh, x[:, quarters[mh]])
            if k == 3:
                for mh in range(2):
                    turn_back(mh)
                    encode_rest(6 + mh, banks[2 + mh])

        def quantise_z(name, z, width, at):
            codes = sbuf(name + "_w", [P, width], U32, at)
            scales = sbuf(name + "_sc", [P, width], U8)
            nc.vector.quantize_mx(codes[:].bitcast(FP8X4), scales[:], z.rearrange("p m t -> p (m t)"))
            return codes, scales

        def project(a, first, count, codes, scales):
            for n in range(count):
                entries = slice(P * n, P * (n + 1))
                for c in range(4):
                    cols = slice(P * c, P * (c + 1))
                    nc.tensor.matmul_mx(
                        banks[4 + first + n][:, cols], lhsT=w3_w[a][:, cols].bitcast(FP8X4), lhsT_scale=w3_sc[4 * a : P, cols],
                        rhs=codes[:, entries].bitcast(FP8X4), rhs_scale=scales[:, entries],
                        start=(a == 0 and c == 0), stop=(a == 1 and c == 3),
                    )

        write_slots(0, 1, quarters[1], h_last[0][:, quarters[1]], wgs_fourth[:])
        for k in range(1, 7):
            if k < 4:
                write_slots(k, 1, quarters[1], h_last[k][:, quarters[1]], wgs_fourth[:])
            else:
                write_slots(k, 1, whole, h_last[k], dealt1[:, k - 4, :])
            read_slots(k - 1)
            if k == 2:
                first_half(7, h_last[0], banks[2])
        read_slots(6)
        write_slots(7, 1, whole, h_last[7], dealt1[:, 3, :])
        codes, scales = quantise_z("z00", z_bf[0, 0], QUARTER, at_tab0 + 8 * KIB + LAP)
        project(0, 0, 2, codes, scales)
        for n in range(4):
            x = h_last[7][:, P * n : P * (n + 1)]
            nc.vector.tensor_copy(x, pages[7][:].indirect(idx3[:, 8 * n : 8 * n + 8]))
            nc.scalar.activation(woven[1][:, P * n : P * (n + 1), 3], x, ACT.Identity, bias=bias_dealt[:, 3:4])
            if n == 1:
                codes, scales = quantise_z("z01", z_bf[0, 1], QUARTER, at_w2[0])
                project(0, 2, 2, codes, scales)
        for n in range(4):
            codes, scales = quantise_z("z1%d" % n, woven[1][:, P * n : P * (n + 1), :], P, None)
            project(1, n, 1, codes, scales)
        out_rows = out.rearrange("(c p) m -> p c m", p=P)
        for n, first, count in ((0, 0, 4), (1, 0, 4), (2, 0, 4), (3, 0, 2), (3, 2, 2)):
            res = shift_sb[:, first : first + count, P * n : P * (n + 1)]
            acc = banks[4 + n][:].rearrange("p (c m) -> p c m", c=4)[:, first : first + count]
            nc.vector.tensor_tensor(res, acc, res, ADD)
            queue = nc.scalar if (n, first) in ((1, 0), (3, 0)) else nc.sync
            queue.dma_start(out_rows[:, first : first + count, P * n : P * (n + 1)], res)
